import numpy as np, ml_dtypes
CORES = [3,11,19,27,35,43]
N = 6
BF = ml_dtypes.bfloat16
def gentries(a):
    return np.ascontiguousarray(a.reshape(8, 16, -1).transpose(0, 2, 1)).reshape(8, -1)
def gtable(e):
    e = np.asarray(e); return np.ascontiguousarray(e.reshape(8, -1, 16).transpose(0, 2, 1)).reshape(128, -1).astype(np.int32)
W, T, K, C, J, RO = 4096, 128, 16, 32, 5, 3
Q = W // T
def lay(v):
    return np.ascontiguousarray(v.transpose(0, 1, 3, 2)).reshape(N, 128, -1).astype(np.float32).astype(BF)
def pack(x, s, m, z, w, kp):
    return {"rec": lay(x), "st": lay(s.reshape(N, 8, T * K, 16)), "nm": np.stack([gtable(a.reshape(8, -1)) for a in m]), "arr": lay(z),
            "wt": np.ascontiguousarray(w.reshape(N, 128, 1)).astype(np.int32), "kap": np.stack([gtable(a) for a in kp])}
def consts(rng):
    return rng.integers(0, 256, (N, 8, 16)), rng.integers(0, 1024, (N, 8, C))
def make(rng, base, sp, wild):
    share = rng.choice(np.array([0.5, 0.7, 0.9]), (N, 8, 1, 1))
    def mix(n):
        v = np.clip(base + ((rng.random((N, 8, T, n, 16)) - 0.5) * sp).astype(np.int64), 0, 255)
        return np.where((rng.random((N, 8, T, n)) < share)[..., None], v, wild((N, 8, T, n)))
    x = mix(Q).reshape(N, 8, W, 16); s = mix(K); z = mix(1)[:, :, :, 0]
    own = Q * np.arange(T)[:, None] + rng.integers(0, Q, (N, 8, T, K))
    m = np.where(rng.random((N, 8, T, K)) < share, own, rng.integers(0, W, (N, 8, T, K)))
    return x, s, m, z
def setup_inputs(rng):
    x, s, m, z = make(rng, rng.integers(0, 256, (N, 8, T, 1, 16)), 24.0, lambda sh: rng.integers(0, 256, sh + (16,)))
    return pack(x, s, m, z, *consts(rng))
def setup_inputs_spread(rng):
    def uneven(sh):
        return np.minimum((np.exp2(8 * rng.random(sh + (1,))) * rng.random(sh + (16,))).astype(np.int64), 255)
    base = uneven((N, 8, T, 1)); x, s, m, z = make(rng, base, 0.5 * base + 2, uneven)
    m = np.where(rng.random((N, 8, T, K)) < 0.3, np.minimum((W * rng.random((N, 8, T, K)) ** 3).astype(np.int64), W - 1), m)
    w = np.minimum(np.exp2(8 * rng.random((N, 8, 16))).astype(np.int64) - 1, 255); kp = np.minimum(np.exp2(10 * rng.random((N, 8, C))).astype(np.int64) - 1, 1023)
    return pack(x, s, m, z, w, kp)
def setup_inputs_ends(rng):
    def ext(sh):
        k = rng.integers(0, 3, sh + (1,)); return 255 * np.where(k == 2, rng.integers(0, 2, sh + (16,)), k)
    x = ext((N, 8, W)); s = ext((N, 8, T, K)); z = ext((N, 8, T)); h = T // 2
    m = (W - 1) * rng.integers(0, 2, (N, 8, T, K)); w = 255 * rng.integers(0, 2, (N, 8, 16)); kp = 1023 * rng.integers(0, 2, (N, 8, C))
    w[:, 0, 3] = 0; kp[:, 0, 3] = 0
    w[:, 7] = 255; kp[:, 7] = 1023; x[:, 7] = 0; s[:, 7, h:] = 255; m[:, 7, h:] = W - 1
    z[:, 7] = 255 * rng.integers(0, 2, (N, T, 1)); z[:, 7, h:] = 255
    u = (16 * 255 * 255) & (W - 1); c = ((u * u >> 5) + 1023 * u + 1023) & (W - 1); x[0::2, 7, c, 15] = 1
    x[:, 6] = 0; s[:, 6, h:] = 0; z[:, 6, h:] = 0
    s[:, 5, T - 1] = 0; s[:, 5, T - 1, K - 1] = 255; z[:, 5, T - 1] = 255
    s[:, 5, T - 2] = 255; z[:, 5, T - 2] = 0
    s[:, 5, T - 3] = 0; s[:, 5, T - 3, K - 1, 15] = 1; z[:, 5, T - 3] = 255
    s[:, 5, T - 4] = 255; s[:, 5, T - 4, K - 2, 15] = 254; z[:, 5, T - 4] = 0
    x[:, 4] = rng.integers(0, 4, (N, W, 16)); s[:, 4] = rng.integers(252, 256, (N, T, K, 16))
    z[:, 4, :h] = rng.integers(252, 256, (N, h, 16)); z[:, 4, h:] = rng.integers(0, 4, (N, T - h, 16))
    m[:, 4] = rng.integers(0, W, (N, T, K)); w[:, 4] = rng.integers(0, 256, (N, 16)); kp[:, 4] = rng.integers(0, 1024, (N, C))
    return pack(x, s, m, z, w, kp)
def setup_inputs_corners(rng):
    gi = np.arange(8)[None, :]; ri = np.arange(N)[:, None]; row = np.arange(K); lane = np.arange(T)
    kind = np.argsort(rng.random((N, 8, T)), axis=-1) % 8; code = np.argsort(rng.random((N, 8, T)), axis=-1) % 6
    kind[:, :, T - 1] = gi; code[:, :, T - 1] = (gi + ri) % 6
    goal = np.array([0, K - 1, K - 2, K - 1 - J, K - J, 0, 0, 0])[kind]; goal = np.where(kind == 7, rng.integers(0, K, kind.shape), goal)
    z = rng.integers(0, 101, (N, 8, T, 16)); z[kind == 6] = np.array([255, 1] + [0] * 14)
    s = rng.integers(150, 256, (N, 8, T, K, 16)); hit = (row == goal[..., None]) | (kind == 5)[..., None]
    s = np.where(hit[..., None], z[:, :, :, None, :], s)
    tot = np.sum(z, axis=-1); n = Q * lane + (tot & (Q - 1)); far = Q * lane + ((tot + 1) & (Q - 1))
    x = rng.integers(0, 101, (N, 8, W, 16)); x[:, :, 0] = 0; x[:, :, W - 1] = 255
    a, b, c = np.nonzero(code == 3); x[a, b, far[a, b, c]] = 255
    k = code[..., None]; n1 = n[..., None]; last = np.where(row == (goal + J)[..., None], far[..., None], n1)
    m = np.where(k == 4, rng.integers(0, W, (N, 8, T, K)), np.roll(n, -1, axis=2)[..., None])
    m = np.where(k == 0, n1, np.where(k == 1, 0, np.where(k == 2, W - 1, np.where(k == 3, last, m))))
    w, kp = consts(rng); w[:, 0::2, 0] = (W - 1) // 255; w[:, 0::2, 1] = (W - 1) % 255; w[:, 5] = 0
    kp[:, 0] = 1023; kp[:, 3] = 0
    return pack(x, s, m, z, w, kp)
def setup_inputs_crowd(rng):
    v = rng.integers(40, 80, (N, 8, 16)); v[..., 0] |= 1
    v[..., 1] += (np.sum(v, axis=-1) & (Q - 1)) == 1
    w, kp = consts(rng); w[..., 0] ^= 1 - (np.sum(w * v, axis=-1) & 1)
    kp[..., 1] = 2 * (kp[..., 1] >> 1); kp[..., 2] |= 1
    x = v[:, :, None, :] + rng.integers(0, 4, (N, 8, W, 16)); x[:, :, 0::Q] = v[:, :, None, :]
    x[:, :, 1::Q] = v[:, :, None, :] + 100 + rng.integers(0, 75, (N, 8, T, 16))
    s = rng.integers(0, 256, (N, 8, T, K, 16)); s[:, :, :, 0] = v[:, :, None, :]
    z = np.repeat(v[:, :, None, :], T, axis=2)
    go = np.ones((N, 8, T), bool)
    for q in range(1, N):
        for g in range(8):
            mode = int(rng.integers(0, 4)) if q > 2 else int(rng.integers(0, 2))
            if q == 1: mode = 1 if g == 7 else 0
            if q == 2 and g == 3: mode = 1
            if mode == 1: go[q, g, T - 1 if q == 1 else int(rng.integers(0, T))] = False
            if mode == 2: go[q, g] = False
            if mode == 3: go[q, g] = rng.permutation(T) < T // 2
    off = Q * rng.integers(0, T, (N, 8, T, K)) + 1; off[:, 0::2] = off[:, 0::2, :1, :1]
    m = np.where(go[..., None], off, Q * rng.integers(0, T, (N, 8, T, K)))
    y = np.where(go[1][..., None], x[1][np.arange(8)[:, None], m[1, :, :, 1]], np.abs(z[1] - s[1, :, :, K - 1]))
    s[2, :, :, K - 1] = np.maximum(y - rng.integers(0, 4, y.shape), 0)
    return pack(x, s, m, z, w, kp)
def setup_inputs_ties(rng):
    p = rng.integers(20, 236, (N, 8, 16)); e = 20 * (np.arange(16) & 1)
    pats = np.stack([p, p + 10, p - 10, p + e, p + 20 - e], axis=2); a = np.arange(N)[:, None, None]; b = np.arange(8)[None, :, None]
    x = pats[a, b, rng.integers(0, 5, (N, 8, W))]; z = pats[a, b, rng.integers(0, 5, (N, 8, T))]
    s = pats[a, b, rng.integers(0, 5, (N, 8, T * K))].reshape(N, 8, T, K, 16)
    return pack(x, s, rng.integers(0, W, (N, 8, T, K)), z, *consts(rng))
def check_inputs(d):
    bad = []
    for k, hi in (("rec", 255), ("st", 255), ("nm", W - 1), ("arr", 255), ("wt", 255), ("kap", 1023)):
        v = np.asarray(d[k]).astype(np.float64)
        if not (np.all(v >= 0) and np.all(v <= hi)): bad.append("range of " + k)
        elif np.any(v != np.floor(v)): bad.append("whole numbers in " + k)
    return bad
def unlay(a):
    return np.ascontiguousarray(a.astype(np.float32).astype(np.int32).reshape(N, 8, 16, -1).transpose(0, 1, 3, 2))
def reference(rec, st, nm, arr, wt, kap):
    x = unlay(rec); s = unlay(st).reshape(N, 8, T, K, 16); z = unlay(arr)
    m = np.stack([gentries(a) for a in nm]).astype(np.int32).reshape(N, 8, T, K)
    w = wt.astype(np.int32).reshape(N, 8, 1, 16); kp = np.stack([gentries(a) for a in kap]).astype(np.int32)[:, :, None, :]
    ri = np.arange(N)[:, None, None]; gi = np.arange(8)[None, :, None]; li = np.arange(T)[None, None, :]; row = np.arange(K)
    cnt = np.zeros((N, 1, 1, 1), np.int32)
    for t in range(RO):
        n = (Q * li + (np.sum(z, axis=-1) & (Q - 1))).astype(np.int32)
        x[ri, gi, n] = z
        g = np.argmin(np.sum(np.abs(s - z[:, :, :, None, :]), axis=-1, dtype=np.int32), axis=-1)
        mid = (s[ri, gi, li, g] + z) >> 1
        low = row < g[..., None]
        s = np.where(low[..., None], np.concatenate([s[:, :, :, 1:], s[:, :, :, -1:]], axis=3), s)
        m = np.where(low, np.concatenate([m[..., 1:], m[..., -1:]], axis=3), m)
        s[ri, gi, li, g] = mid; m[ri, gi, li, g] = n
        rel = np.zeros((N, 8, T), bool); gone = np.zeros((N, 8, T), np.int32)
        for j in range(1, J + 1):
            live = g + j < K; p = np.minimum(g + j, K - 1)
            b = s[ri, gi, li, p - 1]
            u = (np.sum(w * b, axis=-1, dtype=np.int32) & (W - 1))[..., None]
            c = ((u * u >> 5) + kp * u + kp[..., :1] * j + cnt) & (W - 1)
            old = m[ri, gi, li, p]; c[..., 0] = old
            v = x[ri[..., None], gi[..., None], c]
            f = np.argmin(np.sum(np.abs(v - b[:, :, :, None, :]), axis=-1, dtype=np.int32), axis=-1)
            e = c[ri, gi, li, f]; xe = v[ri, gi, li, f]
            s[ri, gi, li, p] = np.where(live[..., None], (b + xe) >> 1, s[ri, gi, li, p])
            m[ri, gi, li, p] = np.where(live, e, old)
            now = live & (e != old) & ~rel
            gone = np.where(now, old, gone); rel = rel | now
        nxt = np.where(rel[..., None], x[ri, gi, gone], np.abs(z - s[:, :, :, K - 1]))
        cnt = (np.sum(rel, axis=(1, 2)).astype(np.int32) & 63).reshape(N, 1, 1, 1)
        z = np.stack([nxt[(q - 1 - t % 3) % N] for q in range(N)])
    mo = np.stack([gtable(a.reshape(8, -1)) for a in m])
    return {"so": lay(s.reshape(N, 8, T * K, 16)), "mo": mo.astype(np.float32), "zo": lay(z)}

@@ -1,0 +1,669 @@
+from concourse.mybir import dt, AluOpType, AxisListType, ActivationFunctionType
+
+AL = AluOpType
+AF = ActivationFunctionType
+RO, NJ = 3, 5
+AMAJ = False
+
+POOL = {"PF": "float32", "PI": "int32", "PU": "uint16", "PH": "float16", "PB": "bfloat16"}
+USED = {k: 0 for k in POOL}
+LAY = {}
+SCRATCH = {}
+
+
+def own(name, where, shape, dtype):
+    SCRATCH[name] = (where, shape, dtype)
+    LAY[name] = (name, 0, shape[-1])
+
+
+def alloc(name, pool, n):
+    o = (USED[pool] + 15) // 16 * 16
+    LAY[name] = (pool, o, n)
+    USED[pool] = o + n
+
+
+own("X", "sbuf", [128, 4224], "bfloat16")
+own("IOTA", "sbuf", [128, 4096], "float32")
+own("NMI", "sbuf", [128, 128], "int32")
+own("WTI", "sbuf", [128, 1], "int32")
+own("KPI", "sbuf", [128, 2], "int32")
+for _h in range(2):
+    own("SB%d" % _h, "sbuf", [128, 3072], "bfloat16")
+    own("G%d" % _h, "sbuf", [128, 2048], "bfloat16")
+    own("MX%d" % _h, "sbuf", [128, 2048], "bfloat16")
+    own("NU%d" % _h, "sbuf", [128, NJ, 4, 32] if AMAJ else [128, NJ, 128], "uint16")
+    own("MO%d" % _h, "sbuf", [128, 64], "float32")
+    for _t in range(RO + 1):
+        own("Z%d%d" % (_t, _h), "sbuf", [128, 64], "bfloat16")
+    for _t in range(RO):
+        own("OUT%d%d" % (_t, _h), "sbuf", [128, 64], "bfloat16")
+    for _n in ("QK", "QU", "QX"):
+        own("%s%d" % (_n, _h), "psum", [128, 512], "float32")
+    own("QS%d" % _h, "psum", [128, 4, 8, 16] if AMAJ else [128, 512], "float32")
+    own("NI%d" % _h, "sbuf", [128, 4, 32] if AMAJ else [128, 128], "int32")
+    for _n, _w in (("UF", 20), ("Y", 20), ("SQ", 4), ("KM", 4), ("T", 64), ("C0F", 20), ("C0K", 20), ("HF", 4), ("E", 24), ("RK", 24), ("KS", 128),
+                   ("C0S", 20), ("RM", 4), ("XE", 20), ("NF1", 20), ("DE", 20), ("NC", 4), ("JC", 5), ("D15", 64), ("UX", 64), ("ZX", 64)):
+        alloc("%s%d" % (_n, _h), "PF", _w)
+    for _n, _w in (("Q", 4), ("KI", 4), ("OFI", 20), ("TI", 64), ("ZI", 4), ("HI", 4), ("HOI", 4), ("RI", 4), ("MI", 20), ("EI", 20)):
+        alloc("%s%d" % (_n, _h), "PI", _w)
+    for _n, _w in (("OU", 4), ("NL", 4), ("HO", 4), ("HU", 4), ("LRU", 64), ("O15", 4), ("RU", 4), ("MU", 20), ("EU", 24)):
+        alloc("%s%d" % (_n, _h), "PU", _w)
+    for _n, _w in (("M", 64), ("CM", 320), ("LRH", 64), ("EM", 384), ("MK", 128), ("SP", 64)):
+        alloc("%s%d" % (_n, _h), "PH", _w)
+    for _n, _w in (("MASK", 384), ("KG", 640)):
+        alloc("%s%d" % (_n, _h), "PB", _w)
+for _n, _w in (("XI", 144), ("BX", 128), ("CX", 64), ("DX", 96), ("G15", 1), ("B", 1), ("B16", 1), ("P1", 1), ("WF", 1), ("K15", 1), ("K1", 1),
+               ("LT", 16), ("INR", 16), ("TT", 16), ("TB", 32), ("I16", 64), ("KF", 2), ("KT", 31), ("K0", 1), ("K0J", 5), ("CJ", 5), ("AC", 1), ("AF", 1), ("SCN", 64), ("SC2", 64), ("DB", 64), ("B1", 1), ("THR", 20), ("C2K", 1), ("RST", 64)):
+    alloc(_n, "PF", _w)
+for _n, _w in (("PP", 1), ("PT", 1), ("PT2", 1), ("PT3", 1), ("KI32", 32), ("KI2", 32), ("KI3", 32), ("AI", 1)):
+    alloc(_n, "PI", _w)
+for _n, _w in (("CK", 128), ("CG", 64), ("KR", 32)):
+    alloc(_n, "PH", _w)
+for _n, _w in (("ZM", 144), ("ZA", 144), ("WB", 128), ("CN", 64), ("Z15", 144), ("IDW", 130), ("NID", 128), ("ONES", 128), ("BO", 128), ("TAB", 128), ("KW", 64), ("RL", 8)):
+    alloc(_n, "PB", _w)
+for _k in POOL:
+    SCRATCH[_k] = ("sbuf", [128, (USED[_k] + 15) // 16 * 16], POOL[_k])
+for _n, _w in (("rec", 4096), ("st", 2048), ("nm", 128), ("arr", 128), ("wt", 1), ("kap", 2), ("so", 2048), ("mo", 128), ("zo", 128)):
+    LAY[_n] = (_n, 0, _w)
+
+DMAS = ["arr0", "arr1", "st0", "st1", "rec0", "rec1", "nm", "wt", "kap", "so00", "so01", "so10", "so11", "mo0", "mo1", "zo0", "zo1"]
+SEMAPHORES = ["cV", "cS", "cP", "cG", "sent"] + ["d" + n for n in DMAS] + ["a%d%d" % (t, h) for t in range(RO) for h in range(2)]
+
+
+def r(name, a=0, b=None, s=1):
+    buf, o, n = LAY[name]
+    if b is None:
+        b = n
+    cnt = (b - a + s - 1) // s
+    mask = (((1 << (cnt * s)) - 1) // ((1 << s) - 1)) << (o + a)
+    idx = (slice(None), slice(o + a, o + b) if s == 1 else slice(o + a, o + a + (cnt - 1) * s + 1, s))
+    return ("@", buf, mask, idx, cnt)
+
+
+def nd(name, *ix):
+    cols = [0]
+    for d, x in zip(SCRATCH[name][1][1:], ix):
+        cols = [c * d + k for c in cols for k in (range(x[0], x[1]) if isinstance(x, tuple) else [x])]
+    idx = (slice(None),) + tuple(slice(x[0], x[1]) if isinstance(x, tuple) else x for x in ix)
+    return ("@", name, sum(1 << c for c in cols), idx, len(cols))
+
+
+def ind(win, off):
+    return ("#", win, off)
+
+
+def is_acc(x):
+    return isinstance(x, tuple) and len(x) > 0 and x[0] in ("@", "#")
+
+
+CFG = {"gather": 1.56, "pe": 0.7, "ls": 70, "lx": 110, "net": 3600, "pieces": [[512], [512], [512], [512]], "lists": [(0, 2), (2, 4)] if AMAJ else [(64, 128), (4, 64)],
+       "passes": 5, "mmsplit": 4, "fix": 6, "wl": 2}
+
+
+def build():
+    ops = []
+    gc_ = CFG["gather"]
+    lastd = {}
+
+    def add(eng, calls, busy, lat=0, sem=None, grp=None, after=None):
+        rd, wr = [], []
+        for c in calls:
+            for k, x in enumerate(c[1]):
+                if not is_acc(x):
+                    continue
+                if x[0] == "#":
+                    (wr if k == 0 else rd).append(x[1])
+                    rd.append(x[2])
+                else:
+                    (wr if k == 0 else rd).append(x)
+            for x in c[2].values():
+                if is_acc(x):
+                    rd.append(x)
+        ops.append({"eng": eng, "calls": calls, "busy": busy, "lat": lat, "sem": sem, "grp": grp, "rd": rd, "wr": wr, "after": after})
+        return len(ops) - 1
+
+    def vcost(out, ins, per):
+        if out[0] == "#":
+            return 60 + 3.8 * 16 * out[2][4]
+        if ins[0] == "#":
+            return 60 + gc_ * out[4]
+        return vc(per * out[4])
+
+    def vc(n):
+        return max(70, n + CFG["fix"])
+
+    def tt(out, a, b, op):
+        both = a[0] == "@" and a[1][0] != "Q" and b[1][0] != "Q"
+        return add("V", [("tt", (out, a, b, op), {})], vcost(out, a, 2 if both else 1))
+
+    def ts(out, a, s1, s2, op0, op1=None):
+        args = (out, a, s1, s2, op0) if op1 is None else (out, a, s1, s2, op0, op1)
+        return add("V", [("ts", args, {})], vcost(out, a, 1))
+
+    def cp(out, a):
+        return add("V", [("cp", (out, a), {})], vcost(out, a, 1))
+
+    def red(out, a, op):
+        return add("V", [("red", (out, a, AxisListType.X, op), {})], vc(a[4]))
+
+    def ms(out, v):
+        return add("V", [("ms", (out, v), {})], max(64, out[4] // 2) + 6)
+
+    def act(out, a, f, **kw):
+        return add("S", [("act", (out, a, f), kw)], 78 + gc_ * out[4] if a[0] == "#" else max(64, out[4]) + 40)
+
+    def mm(lst, start=True, stop=True, grp=None):
+        calls = [("mm", (o, l, x, start and k == 0, stop and k == len(lst) - 1), {}) for k, (o, l, x) in enumerate(lst)]
+        if grp is None:
+            grp = len(ops)
+        w = CFG["mmsplit"]
+        cuts = list(range(0, len(calls) - w // 2, w)) or [0]
+        for a, b in zip(cuts, cuts[1:] + [len(calls)]):
+            add("P", calls[a:b], sum(max(64, c[1][2][4]) for c in calls[a:b]) * CFG["pe"] + 5, lat=40, grp=grp)
+
+    def sel(z, b):
+        return r(z, 15 - b, 143 - b)
+
+    def mm16(out, z, name, a, b, extra=(), start=True, stop=True, grp=None):
+        return mm([(out, sel(z, q), r(name, a + q, b, 16)) for q in range(16)] + list(extra), start, stop, grp)
+
+    def dma(q, sem, out, src, nbytes):
+        lastd[q] = add(q, [("dma", (out, src), {})], 80, lat=2200 + nbytes // 200, sem="d" + sem, after=lastd.get(q) if sem[:2] not in ("so", "mo", "zo") else None)
+
+    def iota(out, pat, base, cm, flag=True):
+        n = out[4]
+        return add("G", [("iota", (out, pat, base, cm), {"allow_small_or_imprecise_dtypes": True} if flag else {})], 160 + 2 * n)
+
+    ID, SH, NID = r("IDW", 1, 129), r("IDW", 2, 130), r("NID")
+    XS = r("X", 64, 4160)
+
+    dma("Y", "arr0", r("Z00"), r("arr", 0, 64), 16384)
+    dma("S", "st0", r("SB0", 0, 1024), r("st", 0, 1024), 262144)
+    dma("Y", "wt", r("WTI"), ("@", "wt", 1, (slice(None),), 1), 4000)
+    dma("Y", "kap", r("KPI"), r("kap"), 4000)
+    dma("Y", "arr1", r("Z01"), r("arr", 64, 128), 16384)
+    dma("S", "nm", r("NMI"), r("nm"), 300000)
+    dma("Y", "rec0", r("X", 64, 2112), r("rec", 0, 2048), 1100000)
+    dma("S", "rec1", r("X", 2112, 4160), r("rec", 2048, 4096), 1100000)
+    dma("Y", "st1", r("SB1", 0, 1024), r("st", 1024, 2048), 1500000)
+    iota(r("PP"), [[1, 1]], 0, 1, False)
+    iota(r("XI"), [[1, 144]], 0, 0)
+    iota(r("CX"), [[1, 16], [256, 4]], 0, 0)
+    iota(r("DX"), [[1, 6], [1, 16]], 0, 0)
+    iota(r("BX"), [[16, 8], [0, 16]], 15, 0)
+    iota(r("IOTA"), [[1, 4096]], -2048, 0)
+    ts(r("PT"), r("PP"), 112, None, AL.bitwise_and)
+    ts(r("G15"), r("PT"), 15.0, None, AL.add)
+    ts(r("PT2"), r("PP"), 15, None, AL.bitwise_and)
+    cp(r("B"), r("PT2"))
+    ts(r("B16"), r("PT2"), 16.0, None, AL.mult)
+    ts(r("P1"), r("PP"), 1.0, None, AL.add)
+    ts(r("K15"), r("PT2"), 15.0, None, AL.is_equal)
+    ts(r("K1"), r("PT2"), 1.0, None, AL.is_ge)
+    ts(r("WF"), r("WTI"), 1.0 / 4096, None, AL.mult)
+    ts(r("IDW"), r("XI", 0, 130), r("P1"), None, AL.is_equal)
+    ts(r("NID"), r("XI", 1, 129), r("P1"), -1.0, AL.is_equal, AL.mult)
+    ts(r("ZM"), r("XI"), r("G15"), 4096.0, AL.is_equal, AL.mult)
+    ts(r("ZA"), r("XI"), r("G15"), -2048.0, AL.is_equal, AL.mult)
+    ts(r("WB"), r("BX"), r("G15"), r("WF"), AL.is_equal, AL.mult)
+    ts(r("Z15"), r("XI"), r("G15"), r("K15"), AL.is_equal, AL.mult)
+    ts(r("BO"), r("BX"), r("G15"), 1.0 / 16, AL.is_equal, AL.mult)
+    ms(r("ONES"), 1.0)
+    ms(r("CN"), -1024.0)
+    ms(r("C2K"), 2048.0)
+    iota(r("DB"), [[0, 4], [1, 16]], 0, 0)
+    ts(r("PT3"), r("PP"), 1.0, None, AL.add)
+    ts(r("PT3"), r("PT3"), 15, None, AL.bitwise_and)
+    cp(r("B1"), r("PT3"))
+    ts(r("SCN"), r("DB"), r("B"), 512.0, AL.is_equal, AL.mult)
+    ts(r("SC2"), r("DB"), r("B1"), -256.0, AL.is_equal, AL.mult)
+    tt(r("SCN"), r("SCN"), r("SC2"), AL.add)
+    ts(r("CK"), r("XI", 0, 128), 16.0, r("B"), AL.mult, AL.add)
+    if AMAJ:
+        iota(r("THR"), [[0, 5], [512, 4]], 16, 0)
+        ms(r("RST"), 0.0)
+        ms(r("RST", 0, 64, 32), 33554432.0)
+    ts(r("CG"), r("CX"), r("B16"), None, AL.add)
+    ts(r("I16"), r("XI", 0, 64), 16.0, None, AL.mult)
+    HX = r("XI", 0, 16)
+    ts(r("TAB", 0, 96), r("DX"), r("B"), None, AL.is_equal)
+    ts(r("TAB", 96, 112), HX, r("B"), r("K1"), AL.is_ge, AL.mult)
+    ts(r("TAB", 112, 128), HX, 5.0, r("B"), AL.add, AL.is_lt)
+    ts(r("LT"), HX, r("B"), None, AL.is_gt)
+    tt(r("INR"), r("LT"), r("TAB", 112, 128), AL.add)
+    ts(r("INR"), r("INR"), -1.0, 1.0, AL.mult, AL.add)
+    for par in range(2):
+        ts(r("TT"), HX, -1.0, 1024.0 if par == 0 else -1024.0, AL.mult, AL.add)
+        tt(r("TT"), r("TT"), r("INR"), AL.mult)
+        tt(r("TT"), r("TT"), r("LT"), AL.add)
+        ts(r("TB", 16 * par, 16 * par + 16), r("TT"), r("B"), 1024.0 * par, AL.add, AL.add)
+    cp(r("KF"), r("KPI"))
+    for q in range(2):
+        ts(r("KR", 16 * q, 16 * q + 16), HX, r("B"), r("KF", q, q + 1), AL.is_equal, AL.mult)
+    mm([(r("QX1", 0, 32), r("BO"), r("KR"))])
+    ts(r("KT"), r("QX1", 1, 32), 131072.0, None, AL.mult)
+    ts(r("K0"), r("QX1", 0, 1), 32.0, None, AL.mult)
+    ts(r("KI32"), r("QX1", 0, 32), 16.0, None, AL.mult)
+    ts(r("K0J"), r("XI", 1, 6), r("K0"), -16384.375, AL.mult, AL.add)
+    ts(r("KI2"), r("KI32"), 992, None, AL.bitwise_and)
+    ts(r("KW", 0, 32), r("KI2"), 0.125, None, AL.mult)
+    ts(r("KI3"), r("KI32"), 31, None, AL.bitwise_and)
+    ts(r("KW", 32, 64), r("KI3"), 0.125, None, AL.mult)
+    NONE = 15 * 16384 + 8192
+    RS = 1.0 / 524288
+    for h in range(2):
+        ms(r("SB%d" % h, 1024, 2048), 0.0)
+        ts(r("M%d" % h), r("NMI", 64 * h, 64 * h + 64), -2048.0, None, AL.add)
+        ts(r("NC%d" % h), r("CK", 0, 4), 64.0 * h, 32.0, AL.add, AL.mult)
+        ts(r("RK%d" % h, 0, 4), r("CK", 0, 4), float(NONE + 4096 * h), RS, AL.add, AL.mult)
+        ts(r("JC%d" % h), r("XI", 1, 6), (64.0 / 16384) * (1 - h), None, AL.add)
+
+    def mid(h, d):
+        n = lambda x: x + str(h)
+        dst = r(n("SB"), 1024 + d, 2048, 16)
+        ts(r(n("SP")), r(n("T")), 0.5, 1023.75, AL.mult, AL.add)
+        ts(dst, r(n("SP")), -1024.0, None, AL.add)
+
+    def scan(out, src):
+        add("V", [("scan", (out, r("SCN"), src, 0.0, AL.add, AL.min), {})], vc(64))
+
+    def store(t, h):
+        n = lambda x: x + str(h)
+        z = "Z%d%d" % (t, h)
+        mm([(r(n("QU"), 128, 192), r("BO"), r(z))])
+        scan(r(n("ZX")), r(n("QU"), 128, 192))
+        ts(r(n("ZI")), r(n("ZX"), 15, 64, 16), 16.0, None, AL.mult)
+        ts(r(n("ZI")), r(n("ZI")), 31, None, AL.bitwise_and)
+        tt(r(n("E"), 0, 4), r(n("ZI")), r(n("NC")), AL.add)
+        cp(r(n("NL")), r(n("E"), 0, 4))
+        cp(ind(XS, r(n("NL"))), r(z))
+
+    def gap(t, h):
+        n = lambda x: x + str(h)
+        z = r("Z%d%d" % (t, h))
+        so = 2048 * (t % 2)
+        for q, bank in enumerate(("QK", "QX")):
+            for k2 in range(2):
+                calls = []
+                for k in range(8 * q + 4 * k2, 8 * q + 4 * k2 + 4):
+                    o = r(n(bank), 64 * (k % 8), 64 * (k % 8) + 64)
+                    calls.append(("mm", (o, ID, r(n("SB"), so + k, so + 1024, 16), True, False), {}))
+                    calls.append(("mm", (o, NID, z, False, True), {}))
+                add("P", calls, 8 * 64 * CFG["pe"] + 20, lat=40)
+            act(r(n("MX"), 512 * q, 512 * q + 512), r(n(bank)), AF.Abs)
+        key = r(n("QU"), 192, 256)
+        mm16(key, "ZM", n("MX"), 0, 1024, [(key, ID, r("CG"))])
+        for a in range(4):
+            red(r(n("KM"), a, a + 1), r(n("QU"), 192 + a, 256, 4), AL.min)
+        cp(r(n("KI")), r(n("KM")))
+        ts(r(n("HOI")), r(n("KI")), 1023, None, AL.bitwise_and)
+        cp(r(n("HO")), r(n("HOI")))
+        tt(r(n("T")), ind(r(n("SB"), so, so + 1024), r(n("HO"))), z, AL.add)
+        mid(h, 0)
+        ts(r(n("HI")), r(n("KI")), 15, None, AL.bitwise_and)
+        cp(r(n("HU")), r(n("HI")))
+        ts(r(n("HF")), r(n("HI")), 16384.0 * RS, None, AL.mult)
+        hu = r(n("HU"))
+        for j in range(1, NJ + 1):
+            tt(r(n("CM"), 64 * j - 64, 64 * j), ind(r("TAB", 16 * j, 16 * j + 16), hu), r(n("M")), AL.mult)
+        mm16(r(n("QU"), 8, 28), "ZM", n("CM"), 0, 320)
+        ts(nd(n("NU"), (0, NJ), (0, 4), 0) if AMAJ else nd(n("NU"), (0, NJ), (0, 4)), r(n("QU"), 8, 28), 1.0 / 4096, 2048.0, AL.mult, AL.add)
+        act(r(n("C0F")), r(n("QU"), 8, 28), AF.Identity, scale=1.0 / 4096, bias=r("C2K"))
+        act(r(n("C0S")), r(n("C0F")), AF.Copy, scale=RS)
+        for a in range(4):
+            act(r(n("C0K"), a, 20, 4), r(n("JC")), AF.Identity, scale=16384.0 * RS, bias=r(n("HF"), a, a + 1))
+        tt(r(n("C0K")), r(n("C0K")), r(n("C0S")), AL.add)
+        par = t % 2
+        tt(r(n("LRH")), ind(r("TB", 16 * par, 16 * par + 16), hu), r("I16"), AL.add)
+        cp(r(n("LRU")), r(n("LRH")))
+        mm16(r(n("QU"), 28, 32), "Z15", n("LRH"), 0, 64)
+        cp(r(n("O15")), r(n("QU"), 28, 32))
+        for d in range(6):
+            act(r(n("MASK"), 64 * d, 64 * d + 64), ind(r("TAB", 16 * d, 16 * d + 16), hu), AF.Copy)
+        tt(r(n("MK"), 0, 64), ind(r("TAB", 96, 112), hu), r(n("M")), AL.mult)
+        tt(r(n("MK"), 64, 128), ind(r("TAB", 112, 128), hu), r(n("M")), AL.mult)
+
+    last = [None]
+
+    def corr(t, h, j):
+        n = lambda x: x + str(h)
+        s = r(n("SB"), 1024 + j - 1, 2048, 16)
+        mm([(r(n("QU"), 64, 128), r("WB"), r("CN", 0, 64)), (r(n("QU"), 64, 128), r("WB"), r(n("SP")))])
+        W = max(max(x) for x in CFG["pieces"])
+        if AMAJ:
+            add("P", [("mm", (nd(n("QS"), (0, 4), q, (0, 16)), ID, s, True, True), {}) for q in range(W // 16)], 4 * W * CFG["pe"] + 5, lat=40)
+        else:
+            add("P", [("mm", (r(n("QS"), 64 * q, 64 * q + 64), ID, s, True, True), {}) for q in range(W // 64)], W * CFG["pe"] + 5, lat=40)
+        scan(r(n("UX")), r(n("QU"), 64, 128))
+        pu = r(n("UX"), 15, 64, 16)
+        uf, y = r(n("UF"), 4 * j - 4, 4 * j), r(n("Y"), 4 * j - 4, 4 * j)
+        ts(r(n("Q")), pu, -0.5 + 1.0 / 8192, None, AL.add)
+        tt(uf, pu, r(n("Q")), AL.subtract)
+        tt(r(n("SQ")), uf, uf, AL.mult)
+        ts(y, r(n("SQ")), 1048576.0, r("K0J" if t == 0 else "CJ", j - 1, j), AL.mult, AL.add)
+        for a in range(4):
+            c = 4 * j - 4 + a
+            ts(nd(n("NI"), a, (1, 32)) if AMAJ else r(n("NI"), 4 + a, 128, 4), r("KT"), r(n("UF"), c, c + 1), r(n("Y"), c, c + 1), AL.mult, AL.add)
+        for ab in CFG["lists"]:
+            ni = nd(n("NI"), ab, (1, 32)) if AMAJ else r(n("NI"), ab[0], ab[1])
+            ts(ni, ni, 1, 4095, AL.arith_shift_right, AL.bitwise_and)
+            cp(nd(n("NU"), j - 1, ab, (1, 32)) if AMAJ else nd(n("NU"), j - 1, ab), ni)
+        for grp in ((0, 1) if AMAJ else (1, 0)):
+            key = r(n(("QK", "QX")[grp]), 0, 64) if AMAJ else r(n("QK"), 64 * grp, 64 * grp + 64)
+            for a in ((2 * grp, 2 * grp + 1) if AMAJ else (2 * grp + 1, 2 * grp)):
+                lst = nd(n("NU"), j - 1, a, (0, 32)) if AMAJ else nd(n("NU"), j - 1, (32 * a, 32 * a + 32))
+                k = act(r(n("G"), 512 * a, 512 * a + 512), ind(XS, lst), AF.Copy)
+                ops[k]["after"] = last[0]
+                last[0] = k
+                o = 512 * a
+                for w in CFG["pieces"][a if AMAJ else 3 - a]:
+                    tt(r(n("MX"), o, o + w), r(n("G"), o, o + w), nd(n("QS"), a, (0, w // 16), (0, 16)) if AMAJ else r(n("QS"), 0, w), AL.max)
+                    o += w
+            gid = (t, h, j, grp)
+            mm16(key, "ZA", n("G"), 1024 * grp, 1024 * grp + 1024, stop=False, grp=gid)
+            mm16(key, "ZM", n("MX"), 1024 * grp, 1024 * grp + 1024, [(key, ID, r("CK", 64 * grp, 64 * grp + 64))], start=False, grp=gid)
+            if AMAJ:
+                add("V", [("scan", (r(n("KS"), 64 * grp, 64 * grp + 64), r("RST"), key, 0.0, AL.add, AL.min), {})], vc(64))
+        if AMAJ:
+            cp(r(n("KI")), r(n("KS"), 31, 128, 32))
+        else:
+            for a in range(4):
+                red(r(n("KM"), a, a + 1), r(n("QK"), a, 128, 4), AL.min)
+            cp(r(n("KI")), r(n("KM")))
+        ofi = r(n("OFI"), 4 * j - 4, 4 * j)
+        ts(ofi, r(n("KI")), 2047, None, AL.bitwise_and)
+        cp(r(n("OU")), ofi)
+        tt(r(n("T")), ind(r(n("G")), r(n("OU"))), s, AL.add)
+        mid(h, j)
+
+    def release(t, h):
+        n = lambda x: x + str(h)
+        par = t % 2
+        win = r(n("SB"), 1024 * par, 1024 * par + 2048)
+        tt(r(n("D15")), ind(win, r(n("O15"))), r("Z%d%d" % (t, h)), AL.subtract)
+        act(r("X", 4160 * h, 4160 * h + 64), r(n("D15")), AF.Abs)
+        if AMAJ:
+            tt(r(n("NF1")), r(n("OFI")), r("THR"), AL.is_lt)
+        else:
+            ts(r(n("NF1")), r(n("OFI")), 64.0, None, AL.is_lt)
+        tt(r(n("RK"), 4, 24), r(n("NF1")), r(n("C0K")), AL.add)
+        for a in range(4):
+            red(r(n("RM"), a, a + 1), r(n("RK"), a, 24, 4), AL.min)
+        ts(r(n("RI")), r(n("RM")), 524288.0, None, AL.mult)
+        ts(r(n("RI")), r(n("RI")), 8191, None, AL.bitwise_and)
+        cp(r(n("RU")), r(n("RI")))
+        out = r("OUT%d%d" % (t, h))
+        act(out, ind(r("X", 64 * h, 64 * h + 4160), r(n("RU"))), AF.Copy)
+        land = r("Z%d%d" % (t + 1, h))
+        sid = add("G", [("send", (None, out, t, h), {})], 1200)
+        add("N", [("recv", (land,), {})], 0, lat=CFG["net"], sem="a%d%d" % (t, h), after=sid)
+        if t < RO - 1:
+            ts(r("RL", 4 * h, 4 * h + 4), r(n("RM")), NONE * RS, None, AL.is_lt)
+        else:
+            dma("Y", "zo%d" % h, r("zo", 64 * h, 64 * h + 64), land, 16384)
+
+    def renew(t, h):
+        n = lambda x: x + str(h)
+        par = t % 2
+        win = r(n("SB"), 1024 * par, 1024 * par + 2048)
+        nx = 2048 * (1 - par)
+        for q in range(2):
+            dst = r(n("SB"), nx + 512 * q, nx + 512 * q + 512)
+            act(dst, ind(win, r(n("LRU"), 32 * q, 32 * q + 32)), AF.Copy)
+            if t == RO - 1:
+                dma("Y", "so%d%d" % (h, q), r("so", 1024 * h + 512 * q, 1024 * h + 512 * q + 512), dst, 131072)
+        ts(r(n("MI")), r(n("OFI")), 4 if AMAJ else 6, 31, AL.arith_shift_right, AL.bitwise_and)
+        cp(r(n("MU")), r(n("MI")))
+        for q in range(2):
+            act(r(n("KG"), 320 * q, 320 * q + 320), ind(r("KW", 32 * q, 32 * q + 32), r(n("MU"))), AF.Copy)
+        pk = r(n("QX"), 0, 20)
+        mm([(pk, sel("ZM", b), r(n("KG"), 320 * q + b, 320 * q + 320, 16)) for q in range(2) for b in range(16)])
+        tt(r(n("XE")), pk, r(n("UF")), AL.mult)
+        tt(r(n("EI")), r(n("XE")), r(n("Y")), AL.add)
+        ts(r(n("EI")), r(n("EI")), 1, 4095, AL.arith_shift_right, AL.bitwise_and)
+        tt(r(n("DE")), r(n("C0F")), r(n("EI")), AL.subtract)
+        tt(r(n("DE")), r(n("DE")), r(n("NF1")), AL.mult)
+        tt(r(n("E"), 4, 24), r(n("DE")), r(n("EI")), AL.add)
+        cp(r(n("EU")), r(n("E")))
+        tt(r(n("EM")), ind(r("IOTA"), r(n("EU"))), r(n("MASK")), AL.mult)
+        pm = r(n("QX"), 64, 128)
+        mm([(pm, SH, r(n("MK"), 0, 64)), (pm, ID, r(n("MK"), 64, 128))] + [(pm, ID, r(n("EM"), 64 * d, 64 * d + 64)) for d in range(6)])
+        if t < RO - 1:
+            cp(r(n("M")), pm)
+        else:
+            act(r(n("MO")), pm, AF.Identity, bias=r("C2K"))
+            dma("Y", "mo%d" % h, r("mo", 64 * h, 64 * h + 64), r(n("MO")), 32768)
+
+    def count():
+        pa = r("QU1", 32, 40)
+        mm([(pa, r("ONES"), r("RL"))])
+        red(r("AC"), pa, AL.add)
+        cp(r("AI"), r("AC"))
+        ts(r("AI"), r("AI"), 63, None, AL.bitwise_and)
+        ts(r("AF"), r("AI"), 2.0, None, AL.mult)
+        ts(r("CJ"), r("K0J"), r("AF"), None, AL.add)
+
+    for t in range(RO):
+        store(t, 0)
+        store(t, 1)
+        gap(t, 0)
+        gap(t, 1)
+        for j in range(1, NJ + 1):
+            corr(t, 0, j)
+            corr(t, 1, j)
+        release(t, 0)
+        release(t, 1)
+        if t < RO - 1:
+            count()
+        renew(t, 0)
+        renew(t, 1)
+    return ops
+
+
+def depend(ops):
+    live = {}
+    bank = {}
+    deps = []
+    for i, o in enumerate(ops):
+        d = {}
+        for x in o["rd"]:
+            for e in live.get(x[1], []):
+                if e[2] and e[1] & x[2]:
+                    d[e[0]] = True
+        for x in o["wr"]:
+            for e in live.get(x[1], []):
+                if e[1] & x[2]:
+                    d[e[0]] = not (o["grp"] is not None and ops[e[0]]["grp"] == o["grp"])
+        for x in o["wr"]:
+            keep = []
+            for e in live.get(x[1], []):
+                m = e[1] & ~x[2]
+                if m:
+                    keep.append([e[0], m, e[2]])
+            live[x[1]] = keep
+        for x in o["wr"]:
+            live[x[1]].append([i, x[2], True])
+        for x in o["rd"]:
+            live.setdefault(x[1], []).append([i, x[2], False])
+        for b in set(x[1] for x in o["rd"] + o["wr"] if x[1][0] == "Q"):
+            st = bank.setdefault(b, {"eng": None, "cur": [], "prev": []})
+            if st["eng"] != o["eng"]:
+                st["prev"], st["cur"], st["eng"] = st["cur"], [], o["eng"]
+            for p in st["prev"]:
+                d[p] = True
+            if o["eng"] == "P" and st["cur"]:
+                d.setdefault(st["cur"][-1], False)
+            st["cur"].append(i)
+        if o["after"] is not None:
+            d.setdefault(o["after"], False)
+        d.pop(i, None)
+        deps.append(d)
+    return deps
+
+
+def schedule(ops, deps):
+    n = len(ops)
+    succ = [[] for _ in range(n)]
+    for i in range(n):
+        for p in deps[i]:
+            succ[p].append(i)
+
+    def gap_(p, i):
+        if not deps[i][p]:
+            return 0
+        return ops[p]["lat"] + (CFG["ls"] if ops[p]["eng"] == ops[i]["eng"] else CFG["lx"])
+
+    fw = [[(p, gap_(p, i)) for p in deps[i]] for i in range(n)]
+    bw = [[(s, gap_(i, s)) for s in succ[i]] for i in range(n)]
+    busy = [o["busy"] for o in ops]
+
+    def place(seq, pre, first):
+        fin = [0.0] * n
+        slots = {}
+        for i in seq:
+            t = max([fin[p] + d for p, d in pre[i]] + [first[i]])
+            sl = slots.setdefault(ops[i]["eng"], [])
+            k = len(sl)
+            while k > 0 and sl[k - 1][1] > t:
+                k -= 1
+            while k < len(sl) and sl[k][0] < t + busy[i]:
+                t = max(t, sl[k][1])
+                k += 1
+            sl.insert(k, (t, t + busy[i]))
+            fin[i] = t + busy[i]
+        return fin
+
+    prio = [0.0] * n
+    for i in range(n - 1, -1, -1):
+        prio[i] = busy[i] + max([d * CFG["wl"] + prio[s] for s, d in bw[i]] + [ops[i]["lat"]])
+    zero, tail = [0.0] * n, [o["lat"] for o in ops]
+    seq = sorted(range(n), key=lambda i: (-prio[i], i))
+    best = None
+    for _ in range(CFG["passes"]):
+        fin = place(seq, fw, zero)
+        end = max(fin[i] + tail[i] for i in range(n))
+        if best is None or end < best[0]:
+            best = (end, fin)
+        back = place(sorted(range(n), key=lambda i: (-fin[i], -i)), bw, tail)
+        seq = sorted(range(n), key=lambda i: (-back[i], i))
+    end, fin = best
+    return sorted(((i, fin[i] - busy[i]) for i in range(n)), key=lambda x: (x[1], x[0])), end
+
+
+def plan_waits(ops, deps, order):
+    pos, key = {}, {}
+    for k, (i, s) in enumerate(order):
+        pos[i] = k
+        key[i] = ops[i]["sem"] if ops[i]["sem"] else ops[i]["eng"]
+    known, clock, waits, signal = {}, {}, {}, set()
+    for i, s in order:
+        e = ops[i]["eng"]
+        kn = known.setdefault(e, {}) if e != "N" else {}
+        w = []
+        if e != "N":
+            for p in sorted((p for p in deps[i] if deps[i][p]), key=lambda p: -pos[p]):
+                if kn.get(key[p], -1) >= pos[p]:
+                    continue
+                w.append(p)
+                signal.add(p)
+                for k2, v in clock[p].items():
+                    if kn.get(k2, -1) < v:
+                        kn[k2] = v
+        waits[i] = w
+        c = dict(kn)
+        c[key[i]] = pos[i]
+        clock[i] = c
+    return waits, signal
+
+
+PLAN = {}
+
+
+def plan():
+    if not PLAN:
+        ops = build()
+        deps = depend(ops)
+        order, end = schedule(ops, deps)
+        waits, signal = plan_waits(ops, deps, order)
+        PLAN.update({"ops": ops, "order": order, "waits": waits, "signal": signal, "end": end})
+    return PLAN
+
+
+def rank_program(g, core, T, topo):
+    rank = T.rank_of(core)
+    if rank is None:
+        return
+    p = plan()
+    ops, waits, signal = p["ops"], p["waits"], p["signal"]
+    cores = list(T.cores)
+    nr = len(cores)
+    queue = {"V": g.vector, "S": g.scalar, "P": g.tensor, "G": g, "Y": g.sync}
+
+    def res(x):
+        if not is_acc(x):
+            return x
+        if x[0] == "#":
+            return res(x[1]).indirect(res(x[2]))
+        return T[x[1]][x[3]]
+
+    def call(q, name, a, kw):
+        a = [res(x) for x in a]
+        kw = {k: res(v) for k, v in kw.items()}
+        if name == "tt":
+            return q.tensor_tensor(*a)
+        if name == "ts":
+            return q.tensor_scalar(*a)
+        if name == "cp":
+            return q.tensor_copy(*a)
+        if name == "red":
+            return q.tensor_reduce(*a)
+        if name == "scan":
+            return q.tensor_tensor_scan(*a)
+        if name == "ms":
+            return q.memset(*a)
+        if name == "act":
+            return q.activation(*a, **kw)
+        if name == "mm":
+            return q.matmul(*a)
+        if name == "iota":
+            return q.iota(*a, **kw)
+        return q.dma_start(*a)
+
+    cnt = {"V": 0, "S": 0, "P": 0, "G": 0}
+    val = {}
+    sent = 0
+    outs = []
+    for i, s in p["order"]:
+        o = ops[i]
+        e = o["eng"]
+        if e == "N":
+            t = int(o["sem"][1])
+            src = cores[(rank - 1 - t % 3) % nr]
+            val[i] = (o["sem"], len(topo.engines(src, core)))
+            continue
+        q = queue[e]
+        for w in waits[i]:
+            q.wait_ge(T.sem[val[w][0]], val[w][1])
+        name = o["calls"][0][0]
+        if name == "send":
+            _, src, t, h = o["calls"][0][1]
+            dst = cores[(rank + 1 + t % 3) % nr]
+            rid, pid, _ = topo.addr(dst)
+            g.remote_dma(T["Z%d%d" % (t + 1, h)][:], res(src), T.sem["a%d%d" % (t, h)], T.sem["sent"], pid, rid, topo.mask(core, dst))
+            sent += len(topo.engines(core, dst))
+            continue
+        ins = None
+        for c in o["calls"]:
+            ins = call(q, c[0], c[1], c[2])
+        if name == "dma":
+            ins.then_inc(T.sem[o["sem"]], 16)
+            val[i] = (o["sem"], 16)
+            if i not in signal:
+                outs.append(o["sem"])
+        elif i in signal:
+            cnt[e] += 1
+            ins.then_inc(T.sem["c" + e], 1)
+            val[i] = ("c" + e, cnt[e])
+    g.wait_ge(T.sem["sent"], sent)
+    for sname in outs:
+        g.sync.wait_ge(T.sem[sname], 16)

@@ -3,6 +3,7 @@ from concourse.mybir import dt, AluOpType, AxisListType, ActivationFunctionType
 AL = AluOpType
 AF = ActivationFunctionType
 RO, NJ = 3, 5
+QUART = True
 AMAJ = False
 
 POOL = {"PF": "float32", "PI": "int32", "PU": "uint16", "PH": "float16", "PB": "bfloat16"}
@@ -31,7 +32,7 @@ for _h in range(2):
     own("SB%d" % _h, "sbuf", [128, 3072], "bfloat16")
     own("G%d" % _h, "sbuf", [128, 2048], "bfloat16")
     own("MX%d" % _h, "sbuf", [128, 2048], "bfloat16")
-    own("NU%d" % _h, "sbuf", [128, NJ, 4, 32] if AMAJ else [128, NJ, 128], "uint16")
+    own("NU%d" % _h, "sbuf", [128, NJ, 2, 64] if QUART else [128, NJ, 128], "uint16")
     own("MO%d" % _h, "sbuf", [128, 64], "float32")
     for _t in range(RO + 1):
         own("Z%d%d" % (_t, _h), "sbuf", [128, 64], "bfloat16")
@@ -42,24 +43,24 @@ for _h in range(2):
     own("QS%d" % _h, "psum", [128, 4, 8, 16] if AMAJ else [128, 512], "float32")
     own("NI%d" % _h, "sbuf", [128, 4, 32] if AMAJ else [128, 128], "int32")
     for _n, _w in (("UF", 20), ("Y", 20), ("SQ", 4), ("KM", 4), ("T", 64), ("C0F", 20), ("C0K", 20), ("HF", 4), ("E", 24), ("RK", 24), ("KS", 128),
-                   ("C0S", 20), ("RM", 4), ("XE", 20), ("NF1", 20), ("DE", 20), ("NC", 4), ("JC", 5), ("D15", 64), ("UX", 64), ("ZX", 64)):
+                   ("C0S", 20), ("RM", 4), ("XE", 20), ("NF1", 20), ("DE", 20), ("NC", 4), ("JC", 5), ("D15", 64), ("UX", 64), ("ZX", 64), ("SH", 64)):
         alloc("%s%d" % (_n, _h), "PF", _w)
     for _n, _w in (("Q", 4), ("KI", 4), ("OFI", 20), ("TI", 64), ("ZI", 4), ("HI", 4), ("HOI", 4), ("RI", 4), ("MI", 20), ("EI", 20)):
         alloc("%s%d" % (_n, _h), "PI", _w)
     for _n, _w in (("OU", 4), ("NL", 4), ("HO", 4), ("HU", 4), ("LRU", 64), ("O15", 4), ("RU", 4), ("MU", 20), ("EU", 24)):
         alloc("%s%d" % (_n, _h), "PU", _w)
-    for _n, _w in (("M", 64), ("CM", 320), ("LRH", 64), ("EM", 384), ("MK", 128), ("SP", 64)):
+    for _n, _w in (("M", 64), ("CM", 320), ("LRH", 64), ("EM", 384), ("MK", 128), ("SP", 64), ("SS", 4)):
         alloc("%s%d" % (_n, _h), "PH", _w)
     for _n, _w in (("MASK", 384), ("KG", 640)):
         alloc("%s%d" % (_n, _h), "PB", _w)
 for _n, _w in (("XI", 144), ("BX", 128), ("CX", 64), ("DX", 96), ("G15", 1), ("B", 1), ("B16", 1), ("P1", 1), ("WF", 1), ("K15", 1), ("K1", 1),
-               ("LT", 16), ("INR", 16), ("TT", 16), ("TB", 32), ("I16", 64), ("KF", 2), ("KT", 31), ("K0", 1), ("K0J", 5), ("CJ", 5), ("AC", 1), ("AF", 1), ("SCN", 64), ("SC2", 64), ("DB", 64), ("B1", 1), ("THR", 20), ("C2K", 1), ("RST", 64)):
+               ("LT", 16), ("INR", 16), ("TT", 16), ("TB", 32), ("I16", 64), ("KF", 2), ("KT", 31), ("K0", 1), ("K0J", 5), ("CJ", 5), ("AC", 1), ("AF", 1), ("SCN", 64), ("SC2", 64), ("DB", 64), ("B1", 1), ("THR", 20), ("C2K", 1), ("CSH", 1), ("RST", 64)):
     alloc(_n, "PF", _w)
 for _n, _w in (("PP", 1), ("PT", 1), ("PT2", 1), ("PT3", 1), ("KI32", 32), ("KI2", 32), ("KI3", 32), ("AI", 1)):
     alloc(_n, "PI", _w)
 for _n, _w in (("CK", 128), ("CG", 64), ("KR", 32)):
     alloc(_n, "PH", _w)
-for _n, _w in (("ZM", 144), ("ZA", 144), ("WB", 128), ("CN", 64), ("Z15", 144), ("IDW", 130), ("NID", 128), ("ONES", 128), ("BO", 128), ("TAB", 128), ("KW", 64), ("RL", 8)):
+for _n, _w in (("ZM", 144), ("ZA", 144), ("WB", 128), ("IDH", 128), ("NIH", 128), ("I2K", 128), ("ZM2", 144), ("C2B", 64), ("CN", 512), ("Z15", 144), ("IDW", 130), ("NID", 128), ("ONES", 128), ("BO", 128), ("TAB", 128), ("KW", 64), ("RL", 8)):
     alloc(_n, "PB", _w)
 for _k in POOL:
     SCRATCH[_k] = ("sbuf", [128, (USED[_k] + 15) // 16 * 16], POOL[_k])
@@ -96,8 +97,9 @@ def is_acc(x):
     return isinstance(x, tuple) and len(x) > 0 and x[0] in ("@", "#")
 
 
-CFG = {"gather": 1.56, "pe": 0.7, "ls": 70, "lx": 110, "net": 3600, "pieces": [[512], [512], [512], [512]], "lists": [(0, 2), (2, 4)] if AMAJ else [(64, 128), (4, 64)],
-       "passes": 5, "mmsplit": 4, "fix": 6, "wl": 2}
+CFG = {"gather": 1.9, "pe": 0.6, "ls": 200, "lx": 230, "net": 3600, "pieces": [[512], [512], [512], [512]], "lists": [(0, 2), (2, 4)] if AMAJ else [(64, 128), (4, 64)],
+       "passes": 4, "mmsplit": 8, "fix": 64, "wl": 1.5, "fe": 1.15, "sabs": 0,
+       "sbs": False, "w4": 512, "g4": [(32, 64), (0, 32)], "ord4": [(0, 0), (0, 1), (1, 0), (1, 1)]}
 
 
 def build():
@@ -130,7 +132,7 @@ def build():
         return vc(per * out[4])
 
     def vc(n):
-        return max(70, n + CFG["fix"])
+        return max(70, n * CFG["fe"] + CFG["fix"])
 
     def tt(out, a, b, op):
         both = a[0] == "@" and a[1][0] != "Q" and b[1][0] != "Q"
@@ -150,7 +152,7 @@ def build():
         return add("V", [("ms", (out, v), {})], max(64, out[4] // 2) + 6)
 
     def act(out, a, f, **kw):
-        return add("S", [("act", (out, a, f), kw)], 78 + gc_ * out[4] if a[0] == "#" else max(64, out[4]) + 40)
+        return add("S", [("act", (out, a, f), kw)], 78 + gc_ * out[4] if a[0] == "#" else out[4] * CFG["fe"] + 80)
 
     def mm(lst, start=True, stop=True, grp=None):
         calls = [("mm", (o, l, x, start and k == 0, stop and k == len(lst) - 1), {}) for k, (o, l, x) in enumerate(lst)]
@@ -204,12 +206,18 @@ def build():
     ts(r("IDW"), r("XI", 0, 130), r("P1"), None, AL.is_equal)
     ts(r("NID"), r("XI", 1, 129), r("P1"), -1.0, AL.is_equal, AL.mult)
     ts(r("ZM"), r("XI"), r("G15"), 4096.0, AL.is_equal, AL.mult)
-    ts(r("ZA"), r("XI"), r("G15"), -2048.0, AL.is_equal, AL.mult)
+    ts(r("ZA"), r("XI"), r("G15"), -4096.0, AL.is_equal, AL.mult)
     ts(r("WB"), r("BX"), r("G15"), r("WF"), AL.is_equal, AL.mult)
     ts(r("Z15"), r("XI"), r("G15"), r("K15"), AL.is_equal, AL.mult)
     ts(r("BO"), r("BX"), r("G15"), 1.0 / 16, AL.is_equal, AL.mult)
     ms(r("ONES"), 1.0)
     ms(r("CN"), -1024.0)
+    ts(r("IDH"), r("XI", 1, 129), r("P1"), 0.5, AL.is_equal, AL.mult)
+    ts(r("NIH"), r("XI", 1, 129), r("P1"), -0.5, AL.is_equal, AL.mult)
+    ts(r("I2K"), r("XI", 1, 129), r("P1"), 2048.0, AL.is_equal, AL.mult)
+    ts(r("ZM2"), r("XI"), r("G15"), 8192.0, AL.is_equal, AL.mult)
+    ms(r("C2B"), 2048.0)
+    ms(r("CSH"), 1023.75)
     ms(r("C2K"), 2048.0)
     iota(r("DB"), [[0, 4], [1, 16]], 0, 0)
     ts(r("PT3"), r("PP"), 1.0, None, AL.add)
@@ -307,7 +315,7 @@ def build():
         for j in range(1, NJ + 1):
             tt(r(n("CM"), 64 * j - 64, 64 * j), ind(r("TAB", 16 * j, 16 * j + 16), hu), r(n("M")), AL.mult)
         mm16(r(n("QU"), 8, 28), "ZM", n("CM"), 0, 320)
-        ts(nd(n("NU"), (0, NJ), (0, 4), 0) if AMAJ else nd(n("NU"), (0, NJ), (0, 4)), r(n("QU"), 8, 28), 1.0 / 4096, 2048.0, AL.mult, AL.add)
+        ts(nd(n("NU"), (0, NJ), (0, 2), (0, 2)) if QUART else nd(n("NU"), (0, NJ), (0, 4)), r(n("QU"), 8, 28), 1.0 / 4096, 2048.0, AL.mult, AL.add)
         act(r(n("C0F")), r(n("QU"), 8, 28), AF.Identity, scale=1.0 / 4096, bias=r("C2K"))
         act(r(n("C0S")), r(n("C0F")), AF.Copy, scale=RS)
         for a in range(4):
@@ -333,7 +341,12 @@ def build():
         if AMAJ:
             add("P", [("mm", (nd(n("QS"), (0, 4), q, (0, 16)), ID, s, True, True), {}) for q in range(W // 16)], 4 * W * CFG["pe"] + 5, lat=40)
         else:
-            add("P", [("mm", (r(n("QS"), 64 * q, 64 * q + 64), ID, s, True, True), {}) for q in range(W // 64)], W * CFG["pe"] + 5, lat=40)
+            add("P", [("mm", (r(n("QS"), 64 * q, 64 * q + 64), r("IDH"), s, True, True), {}) for q in range(W // 64)], W * CFG["pe"] + 5, lat=40)
+        act(r(n("SH")), s, AF.Identity, scale=0.5, bias=r("CSH"))
+        NS_ = CFG["sabs"]
+        if NS_:
+            mm([(r(n("QK"), 128, 132), sel("ZM", b), r(n("SB"), 1024 + j - 1 + 16 * b, 2048, 256)) for b in range(16)])
+            ts(r(n("SS")), r(n("QK"), 128, 132), 1.0 / 4096, -2048.0, AL.mult, AL.add)
         scan(r(n("UX")), r(n("QU"), 64, 128))
         pu = r(n("UX"), 15, 64, 16)
         uf, y = r(n("UF"), 4 * j - 4, 4 * j), r(n("Y"), 4 * j - 4, 4 * j)
@@ -352,16 +365,29 @@ def build():
             key = r(n(("QK", "QX")[grp]), 0, 64) if AMAJ else r(n("QK"), 64 * grp, 64 * grp + 64)
             for a in ((2 * grp, 2 * grp + 1) if AMAJ else (2 * grp + 1, 2 * grp)):
                 lst = nd(n("NU"), j - 1, a, (0, 32)) if AMAJ else nd(n("NU"), j - 1, (32 * a, 32 * a + 32))
-                k = act(r(n("G"), 512 * a, 512 * a + 512), ind(XS, lst), AF.Copy)
+                k = act(r(n("G"), 512 * a, 512 * a + 512), ind(XS, lst), AF.Copy, scale=0.5)
                 ops[k]["after"] = last[0]
                 last[0] = k
                 o = 512 * a
+                if a >= 4 - NS_:
+                    mm([(r(n("QX")), ID, r(n("G"), o, o + 512))] + [(r(n("QX"), 64 * q, 64 * q + 64), r("NIH"), s) for q in range(8)])
+                    act(r(n("MX"), o, o + 512), r(n("QX")), AF.Abs, scale=0.5)
+                    continue
                 for w in CFG["pieces"][a if AMAJ else 3 - a]:
                     tt(r(n("MX"), o, o + w), r(n("G"), o, o + w), nd(n("QS"), a, (0, w // 16), (0, 16)) if AMAJ else r(n("QS"), 0, w), AL.max)
                     o += w
             gid = (t, h, j, grp)
+            ck = (key, ID, r("CK", 64 * grp, 64 * grp + 64))
+            if grp == 1 and NS_:
+                lo = 128 - 32 * NS_
+                mm([ck, (r(n("QK"), lo, 128), r("I2K"), r("C2B", 0, 128 - lo))]
+                   + [(r(n("QK"), c, c + 4), r("I2K"), r(n("SS"))) for c in range(lo, 128, 4)], stop=False, grp=gid)
+                if NS_ == 1:
+                    mm16(r(n("QK"), 64, 96), "ZA", n("G"), 1024, 1536, start=False, stop=False, grp=gid)
+                mm16(key, "ZM2", n("MX"), 1024, 2048, start=False, grp=gid)
+                continue
             mm16(key, "ZA", n("G"), 1024 * grp, 1024 * grp + 1024, stop=False, grp=gid)
-            mm16(key, "ZM", n("MX"), 1024 * grp, 1024 * grp + 1024, [(key, ID, r("CK", 64 * grp, 64 * grp + 64))], start=False, grp=gid)
+            mm16(key, "ZM2", n("MX"), 1024 * grp, 1024 * grp + 1024, [ck], start=False, grp=gid)
             if AMAJ:
                 add("V", [("scan", (r(n("KS"), 64 * grp, 64 * grp + 64), r("RST"), key, 0.0, AL.add, AL.min), {})], vc(64))
         if AMAJ:
@@ -373,8 +399,60 @@ def build():
         ofi = r(n("OFI"), 4 * j - 4, 4 * j)
         ts(ofi, r(n("KI")), 2047, None, AL.bitwise_and)
         cp(r(n("OU")), ofi)
-        tt(r(n("T")), ind(r(n("G")), r(n("OU"))), s, AL.add)
-        mid(h, j)
+        tt(r(n("SP")), ind(r(n("G")), r(n("OU"))), r(n("SH")), AL.add)
+        ts(r(n("SB"), 1024 + j, 2048, 16), r(n("SP")), -1024.0, None, AL.add)
+
+    def corr4(t, h, q, j):
+        n = lambda x: x + str(h)
+        base = 1024 + j - 1 + 512 * q
+        s = r(n("SB"), base, 1024 + 512 * q + 512, 16)
+        sp, sh = r(n("SP"), 32 * q, 32 * q + 32), r(n("SH"), 32 * q, 32 * q + 32)
+        pq = r(n("QU"), 64 + 32 * q, 96 + 32 * q)
+        mm([(pq, r("WB"), r("CN", 0, 32)), (pq, r("WB"), sp)])
+        W = CFG["w4"]
+        qs = n(("QS", "QX")[q])
+        late = CFG["sbs"] and j > 1
+        if late:
+            mm([(r(qs, 0, W), r("IDH"), r("CN", 0, W))] + [(r(qs, 32 * k, 32 * k + 32), r("IDH"), sp) for k in range(W // 32)])
+            act(s, r(qs, 0, 32), AF.Copy, scale=2.0)
+            act(sh, r(qs, 0, 32), AF.Identity, bias=r("CSH"))
+        else:
+            add("P", [("mm", (r(qs, 32 * k, 32 * k + 32), r("IDH"), s, True, True), {}) for k in range(W // 32)], 2 * W * CFG["pe"] + 5, lat=40)
+            act(sh, s, AF.Identity, scale=0.5, bias=r("CSH"))
+        add("V", [("scan", (r(n("UX"), 32 * q, 32 * q + 32), r("SCN", 0, 32), pq, 0.0, AL.add, AL.min), {})], vc(32))
+        pu = r(n("UX"), 32 * q + 15, 32 * q + 32, 16)
+        c0 = 4 * j - 4 + 2 * q
+        two = lambda x: r(n(x), 2 * q, 2 * q + 2)
+        uf, y = r(n("UF"), c0, c0 + 2), r(n("Y"), c0, c0 + 2)
+        ts(two("Q"), pu, -0.5 + 1.0 / 8192, None, AL.add)
+        tt(uf, pu, two("Q"), AL.subtract)
+        tt(two("SQ"), uf, uf, AL.mult)
+        ts(y, two("SQ"), 1048576.0, r("K0J" if t == 0 else "CJ", j - 1, j), AL.mult, AL.add)
+        for a in range(2):
+            ts(r(n("NI"), 64 * q + 2 + a, 64 * q + 64, 2), r("KT"), r(n("UF"), c0 + a, c0 + a + 1), r(n("Y"), c0 + a, c0 + a + 1), AL.mult, AL.add)
+        ni = r(n("NI"), 64 * q + 2, 64 * q + 64)
+        ts(ni, ni, 1, 4095, AL.arith_shift_right, AL.bitwise_and)
+        cp(nd(n("NU"), j - 1, q, (2, 64)), ni)
+        g0 = 1024 * q
+        for a, b in CFG["g4"]:
+            k = act(r(n("G"), g0 + 16 * a, g0 + 16 * b), ind(XS, nd(n("NU"), j - 1, q, (a, b))), AF.Copy, scale=0.5)
+            ops[k]["after"] = last[0]
+            last[0] = k
+            for o in range(g0 + 16 * a, g0 + 16 * b, W):
+                tt(r(n("MX"), o, o + W), r(n("G"), o, o + W), r(qs, 0, W), AL.max)
+        key = r(n("QK"), 64 * q, 64 * q + 64)
+        gid = (t, h, j, q)
+        mm16(key, "ZA", n("G"), g0, g0 + 1024, stop=False, grp=gid)
+        mm16(key, "ZM2", n("MX"), g0, g0 + 1024, [(key, ID, r("CK", 0, 64))], start=False, grp=gid)
+        for a in range(2):
+            red(r(n("KM"), 2 * q + a, 2 * q + a + 1), r(n("QK"), 64 * q + a, 64 * q + 64, 2), AL.min)
+        cp(two("KI"), two("KM"))
+        ofi = r(n("OFI"), c0, c0 + 2)
+        ts(ofi, two("KI"), 2047, None, AL.bitwise_and)
+        cp(two("OU"), ofi)
+        tt(sp, ind(r(n("G"), g0, g0 + 1024), two("OU")), sh, AL.add)
+        if j == NJ or not CFG["sbs"]:
+            ts(r(n("SB"), base + 1, 1024 + 512 * q + 512, 16), sp, -1024.0, None, AL.add)
 
     def release(t, h):
         n = lambda x: x + str(h)
@@ -385,7 +463,7 @@ def build():
         if AMAJ:
             tt(r(n("NF1")), r(n("OFI")), r("THR"), AL.is_lt)
         else:
-            ts(r(n("NF1")), r(n("OFI")), 64.0, None, AL.is_lt)
+            ts(r(n("NF1")), r(n("OFI")), 32.0 if QUART else 64.0, None, AL.is_lt)
         tt(r(n("RK"), 4, 24), r(n("NF1")), r(n("C0K")), AL.add)
         for a in range(4):
             red(r(n("RM"), a, a + 1), r(n("RK"), a, 24, 4), AL.min)
@@ -412,7 +490,7 @@ def build():
             act(dst, ind(win, r(n("LRU"), 32 * q, 32 * q + 32)), AF.Copy)
             if t == RO - 1:
                 dma("Y", "so%d%d" % (h, q), r("so", 1024 * h + 512 * q, 1024 * h + 512 * q + 512), dst, 131072)
-        ts(r(n("MI")), r(n("OFI")), 4 if AMAJ else 6, 31, AL.arith_shift_right, AL.bitwise_and)
+        ts(r(n("MI")), r(n("OFI")), 5 if QUART else 6, 31, AL.arith_shift_right, AL.bitwise_and)
         cp(r(n("MU")), r(n("MI")))
         for q in range(2):
             act(r(n("KG"), 320 * q, 320 * q + 320), ind(r("KW", 32 * q, 32 * q + 32), r(n("MU"))), AF.Copy)
@@ -449,8 +527,12 @@ def build():
         gap(t, 0)
         gap(t, 1)
         for j in range(1, NJ + 1):
-            corr(t, 0, j)
-            corr(t, 1, j)
+            if QUART:
+                for h, q in CFG["ord4"]:
+                    corr4(t, h, q, j)
+            else:
+                corr(t, 0, j)
+                corr(t, 1, j)
         release(t, 0)
         release(t, 1)
         if t < RO - 1:

@@ -42,7 +42,7 @@ for _h in range(2):
         own("%s%d" % (_n, _h), "psum", [128, 512], "float32")
     own("QS%d" % _h, "psum", [128, 4, 8, 16] if AMAJ else [128, 512], "float32")
     own("NI%d" % _h, "sbuf", [128, 4, 32] if AMAJ else [128, 128], "int32")
-    for _n, _w in (("UF", 20), ("Y", 20), ("SQ", 4), ("KM", 4), ("T", 64), ("C0F", 20), ("C0K", 20), ("HF", 4), ("E", 24), ("RK", 24), ("KS", 128),
+    for _n, _w in (("UF", 20), ("Y", 20), ("SQ", 4), ("KM", 4), ("KY", 4), ("T", 64), ("C0F", 20), ("C0K", 20), ("HF", 4), ("E", 24), ("RK", 24), ("KS", 128),
                    ("C0S", 20), ("RM", 4), ("XE", 20), ("NF1", 20), ("DE", 20), ("NC", 4), ("JC", 5), ("D15", 64), ("UX", 64), ("ZX", 64), ("SH", 64)):
         alloc("%s%d" % (_n, _h), "PF", _w)
     for _n, _w in (("Q", 4), ("KI", 4), ("OFI", 20), ("TI", 64), ("ZI", 4), ("HI", 4), ("HOI", 4), ("RI", 4), ("MI", 20), ("EI", 20)):
@@ -54,13 +54,13 @@ for _h in range(2):
     for _n, _w in (("MASK", 384), ("KG", 640)):
         alloc("%s%d" % (_n, _h), "PB", _w)
 for _n, _w in (("XI", 144), ("BX", 128), ("CX", 64), ("DX", 96), ("G15", 1), ("B", 1), ("B16", 1), ("P1", 1), ("WF", 1), ("K15", 1), ("K1", 1),
-               ("LT", 16), ("INR", 16), ("TT", 16), ("TB", 32), ("I16", 64), ("KF", 2), ("KT", 31), ("K0", 1), ("K0J", 5), ("CJ", 5), ("AC", 1), ("AF", 1), ("SCN", 64), ("SC2", 64), ("DB", 64), ("B1", 1), ("THR", 20), ("C2K", 1), ("CSH", 1), ("RST", 64)):
+               ("LT", 16), ("INR", 16), ("TT", 16), ("TB", 32), ("I16", 64), ("KF", 2), ("KT", 31), ("K0", 1), ("K0J", 5), ("CJ", 5), ("AC", 1), ("AF", 1), ("SCN", 64), ("SC2", 64), ("SCU", 32), ("DB", 64), ("B1", 1), ("THR", 20), ("C2K", 1), ("CSH", 1), ("RST", 64)):
     alloc(_n, "PF", _w)
 for _n, _w in (("PP", 1), ("PT", 1), ("PT2", 1), ("PT3", 1), ("KI32", 32), ("KI2", 32), ("KI3", 32), ("AI", 1)):
     alloc(_n, "PI", _w)
 for _n, _w in (("CK", 128), ("CG", 64), ("KR", 32)):
     alloc(_n, "PH", _w)
-for _n, _w in (("ZM", 144), ("ZA", 144), ("WB", 128), ("IDH", 128), ("NIH", 128), ("I2K", 128), ("ZM2", 144), ("C2B", 64), ("CN", 512), ("Z15", 144), ("IDW", 130), ("NID", 128), ("ONES", 128), ("BO", 128), ("TAB", 128), ("KW", 64), ("RL", 8)):
+for _n, _w in (("ZM", 144), ("ZA", 144), ("WB", 128), ("IDH", 128), ("NIH", 128), ("I2K", 128), ("ZM2", 144), ("CQ", 32), ("CN", 512), ("Z15", 144), ("IDW", 130), ("NID", 128), ("ONES", 128), ("BO", 128), ("TAB", 128), ("KW", 64), ("RL", 8)):
     alloc(_n, "PB", _w)
 for _k in POOL:
     SCRATCH[_k] = ("sbuf", [128, (USED[_k] + 15) // 16 * 16], POOL[_k])
@@ -97,9 +97,9 @@ def is_acc(x):
     return isinstance(x, tuple) and len(x) > 0 and x[0] in ("@", "#")
 
 
-CFG = {"gather": 1.9, "pe": 0.6, "ls": 200, "lx": 230, "net": 3600, "pieces": [[512], [512], [512], [512]], "lists": [(0, 2), (2, 4)] if AMAJ else [(64, 128), (4, 64)],
-       "passes": 4, "mmsplit": 8, "fix": 64, "wl": 1.5, "fe": 1.15, "sabs": 0,
-       "sbs": False, "w4": 512, "g4": [(32, 64), (0, 32)], "ord4": [(0, 0), (0, 1), (1, 0), (1, 1)]}
+CFG = {"gather": 1.9, "pe": 0.3, "ls": 280, "lx": 280, "net": 3600, "pieces": [[512], [512], [512], [512]], "lists": [(0, 2), (2, 4)] if AMAJ else [(64, 128), (4, 64)],
+       "passes": 3, "mmsplit": 8, "fix": 0, "wl": 1.1, "fe": 0.8, "sabs": 0,
+       "vg": 16, "mn": 64, "sbs": False, "w4": 128, "g4": [(32, 64), (0, 32)], "ord4": [(0, 0), (0, 1), (1, 0), (1, 1)]}
 
 
 def build():
@@ -132,7 +132,7 @@ def build():
         return vc(per * out[4])
 
     def vc(n):
-        return max(70, n * CFG["fe"] + CFG["fix"])
+        return max(CFG["mn"], n * CFG["fe"] + CFG["fix"])
 
     def tt(out, a, b, op):
         both = a[0] == "@" and a[1][0] != "Q" and b[1][0] != "Q"
@@ -202,7 +202,7 @@ def build():
     ts(r("P1"), r("PP"), 1.0, None, AL.add)
     ts(r("K15"), r("PT2"), 15.0, None, AL.is_equal)
     ts(r("K1"), r("PT2"), 1.0, None, AL.is_ge)
-    ts(r("WF"), r("WTI"), 1.0 / 4096, None, AL.mult)
+    ts(r("WF"), r("WTI"), 0.25, None, AL.mult)
     ts(r("IDW"), r("XI", 0, 130), r("P1"), None, AL.is_equal)
     ts(r("NID"), r("XI", 1, 129), r("P1"), -1.0, AL.is_equal, AL.mult)
     ts(r("ZM"), r("XI"), r("G15"), 4096.0, AL.is_equal, AL.mult)
@@ -213,10 +213,8 @@ def build():
     ms(r("ONES"), 1.0)
     ms(r("CN"), -1024.0)
     ts(r("IDH"), r("XI", 1, 129), r("P1"), 0.5, AL.is_equal, AL.mult)
-    ts(r("NIH"), r("XI", 1, 129), r("P1"), -0.5, AL.is_equal, AL.mult)
-    ts(r("I2K"), r("XI", 1, 129), r("P1"), 2048.0, AL.is_equal, AL.mult)
     ts(r("ZM2"), r("XI"), r("G15"), 8192.0, AL.is_equal, AL.mult)
-    ms(r("C2B"), 2048.0)
+    ms(r("CQ"), 0.25)
     ms(r("CSH"), 1023.75)
     ms(r("C2K"), 2048.0)
     iota(r("DB"), [[0, 4], [1, 16]], 0, 0)
@@ -226,6 +224,7 @@ def build():
     ts(r("SCN"), r("DB"), r("B"), 512.0, AL.is_equal, AL.mult)
     ts(r("SC2"), r("DB"), r("B1"), -256.0, AL.is_equal, AL.mult)
     tt(r("SCN"), r("SCN"), r("SC2"), AL.add)
+    ts(r("SCU"), r("SCN", 0, 32), 1024.0, None, AL.mult)
     ts(r("CK"), r("XI", 0, 128), 16.0, r("B"), AL.mult, AL.add)
     if AMAJ:
         iota(r("THR"), [[0, 5], [512, 4]], 16, 0)
@@ -249,14 +248,14 @@ def build():
     for q in range(2):
         ts(r("KR", 16 * q, 16 * q + 16), HX, r("B"), r("KF", q, q + 1), AL.is_equal, AL.mult)
     mm([(r("QX1", 0, 32), r("BO"), r("KR"))])
-    ts(r("KT"), r("QX1", 1, 32), 131072.0, None, AL.mult)
+    ts(r("KT"), r("QX1", 1, 32), 128.0, None, AL.mult)
     ts(r("K0"), r("QX1", 0, 1), 32.0, None, AL.mult)
     ts(r("KI32"), r("QX1", 0, 32), 16.0, None, AL.mult)
     ts(r("K0J"), r("XI", 1, 6), r("K0"), -16384.375, AL.mult, AL.add)
     ts(r("KI2"), r("KI32"), 992, None, AL.bitwise_and)
-    ts(r("KW", 0, 32), r("KI2"), 0.125, None, AL.mult)
+    ts(r("KW", 0, 32), r("KI2"), 1.0 / 8192, None, AL.mult)
     ts(r("KI3"), r("KI32"), 31, None, AL.bitwise_and)
-    ts(r("KW", 32, 64), r("KI3"), 0.125, None, AL.mult)
+    ts(r("KW", 32, 64), r("KI3"), 1.0 / 8192, None, AL.mult)
     NONE = 15 * 16384 + 8192
     RS = 1.0 / 524288
     for h in range(2):
@@ -408,7 +407,7 @@ def build():
         s = r(n("SB"), base, 1024 + 512 * q + 512, 16)
         sp, sh = r(n("SP"), 32 * q, 32 * q + 32), r(n("SH"), 32 * q, 32 * q + 32)
         pq = r(n("QU"), 64 + 32 * q, 96 + 32 * q)
-        mm([(pq, r("WB"), r("CN", 0, 32)), (pq, r("WB"), sp)])
+        mm([(pq, r("WB"), r("CN", 0, 32)), (pq, r("IDH"), r("CN", 0, 32)), (pq, r("IDH"), r("CQ")), (pq, r("WB"), sp)])
         W = CFG["w4"]
         qs = n(("QS", "QX")[q])
         late = CFG["sbs"] and j > 1
@@ -419,15 +418,18 @@ def build():
         else:
             add("P", [("mm", (r(qs, 32 * k, 32 * k + 32), r("IDH"), s, True, True), {}) for k in range(W // 32)], 2 * W * CFG["pe"] + 5, lat=40)
             act(sh, s, AF.Identity, scale=0.5, bias=r("CSH"))
-        add("V", [("scan", (r(n("UX"), 32 * q, 32 * q + 32), r("SCN", 0, 32), pq, 0.0, AL.add, AL.min), {})], vc(32))
+        add("V", [("scan", (r(n("UX"), 32 * q, 32 * q + 32), r("SCU"), pq, 0.0, AL.add, AL.min), {})], vc(32))
         pu = r(n("UX"), 32 * q + 15, 32 * q + 32, 16)
         c0 = 4 * j - 4 + 2 * q
         two = lambda x: r(n(x), 2 * q, 2 * q + 2)
         uf, y = r(n("UF"), c0, c0 + 2), r(n("Y"), c0, c0 + 2)
-        ts(two("Q"), pu, -0.5 + 1.0 / 8192, None, AL.add)
-        tt(uf, pu, two("Q"), AL.subtract)
-        tt(two("SQ"), uf, uf, AL.mult)
-        ts(y, two("SQ"), 1048576.0, r("K0J" if t == 0 else "CJ", j - 1, j), AL.mult, AL.add)
+        ts(two("SQ"), pu, 1.5 * 2.0 ** 33, 1.5 * 2.0 ** 33, AL.add, AL.subtract)
+        for a in range(2):
+            c = 32 * q + 16 * a + 15
+            ts(r(n("UF"), c0 + a, c0 + a + 1), r(n("UX"), c, c + 1), r(n("SQ"), 2 * q + a, 2 * q + a + 1), 511.875, AL.subtract, AL.add)
+        for a in range(2):
+            ua = r(n("UF"), c0 + a, c0 + a + 1)
+            ts(r(n("Y"), c0 + a, c0 + a + 1), ua, ua, r("K0J" if t == 0 else "CJ", j - 1, j), AL.mult, AL.add)
         for a in range(2):
             ts(r(n("NI"), 64 * q + 2 + a, 64 * q + 64, 2), r("KT"), r(n("UF"), c0 + a, c0 + a + 1), r(n("Y"), c0 + a, c0 + a + 1), AL.mult, AL.add)
         ni = r(n("NI"), 64 * q + 2, 64 * q + 64)
@@ -435,21 +437,25 @@ def build():
         cp(nd(n("NU"), j - 1, q, (2, 64)), ni)
         g0 = 1024 * q
         for a, b in CFG["g4"]:
-            k = act(r(n("G"), g0 + 16 * a, g0 + 16 * b), ind(XS, nd(n("NU"), j - 1, q, (a, b))), AF.Copy, scale=0.5)
-            ops[k]["after"] = last[0]
-            last[0] = k
+            if b - a <= CFG["vg"]:
+                ts(r(n("G"), g0 + 16 * a, g0 + 16 * b), ind(XS, nd(n("NU"), j - 1, q, (a, b))), 0.5, None, AL.mult)
+            else:
+                k = act(r(n("G"), g0 + 16 * a, g0 + 16 * b), ind(XS, nd(n("NU"), j - 1, q, (a, b))), AF.Copy, scale=0.5)
+                ops[k]["after"] = last[0]
+                last[0] = k
             for o in range(g0 + 16 * a, g0 + 16 * b, W):
-                tt(r(n("MX"), o, o + W), r(n("G"), o, o + W), r(qs, 0, W), AL.max)
+                w = min(W, g0 + 16 * b - o)
+                tt(r(n("MX"), o, o + w), r(n("G"), o, o + w), r(qs, 0, w), AL.max)
         key = r(n("QK"), 64 * q, 64 * q + 64)
         gid = (t, h, j, q)
         mm16(key, "ZA", n("G"), g0, g0 + 1024, stop=False, grp=gid)
         mm16(key, "ZM2", n("MX"), g0, g0 + 1024, [(key, ID, r("CK", 0, 64))], start=False, grp=gid)
         for a in range(2):
             red(r(n("KM"), 2 * q + a, 2 * q + a + 1), r(n("QK"), 64 * q + a, 64 * q + 64, 2), AL.min)
-        cp(two("KI"), two("KM"))
-        ofi = r(n("OFI"), c0, c0 + 2)
-        ts(ofi, two("KI"), 2047, None, AL.bitwise_and)
-        cp(two("OU"), ofi)
+        ts(two("KY"), two("KM"), 1.5 * 2.0 ** 34, 1.5 * 2.0 ** 34, AL.add, AL.subtract)
+        for a in range(2 * q, 2 * q + 2):
+            ts(r(n("OU"), a, a + 1), r(n("KM"), a, a + 1), r(n("KY"), a, a + 1), None, AL.subtract)
+        tt(r(n("OFI"), c0, c0 + 2), two("KM"), two("KY"), AL.subtract)
         tt(sp, ind(r(n("G"), g0, g0 + 1024), two("OU")), sh, AL.add)
         if j == NJ or not CFG["sbs"]:
             ts(r(n("SB"), base + 1, 1024 + 512 * q + 512, 16), sp, -1024.0, None, AL.add)

@@ -3,8 +3,11 @@ from concourse.mybir import dt, AluOpType, AxisListType, ActivationFunctionType
 AL = AluOpType
 AF = ActivationFunctionType
 RO, NJ = 3, 5
-QUART = True
-AMAJ = False
+CFG = {"gather": 1.4, "pe": 0.42, "ls": 220, "lx": 220, "net": 2600, "passes": 3, "mmsplit": 8, "wl": 1.0, "fe": 0.83, "mn": 53, "sfix": 0,
+       "A": 2, "rep": 4, "pieces": [(0, 8), (8, 16)], "sh": "V", "cev": "V", "cod": "S", "st": 0, "ren": "SSSS", "w": "S", "kg": "S", "xc": "S", "vp": {}}
+A = CFG["A"]
+STREAMS = [(h, tb) for h in range(2) for tb in range(0, 64, 16 * A)]
+T1 = 6144
 
 POOL = {"PF": "float32", "PI": "int32", "PU": "uint16", "PH": "float16", "PB": "bfloat16"}
 USED = {k: 0 for k in POOL}
@@ -23,8 +26,12 @@ def alloc(name, pool, n):
     USED[pool] = o + n
 
 
-own("X", "sbuf", [128, 4224], "bfloat16")
+own("X", "sbuf", [128, 8320], "bfloat16")
+own("TBL", "sbuf", [128, T1 + 4104], "float32")
 own("IOTA", "sbuf", [128, 4096], "float32")
+own("CC", "sbuf", [128, NJ * 256], "float32")
+own("CT", "sbuf", [128, 1024], "float16")
+own("RR", "sbuf", [128, 1280], "float16")
 own("NMI", "sbuf", [128, 128], "int32")
 own("WTI", "sbuf", [128, 1], "int32")
 own("KPI", "sbuf", [128, 2], "int32")
@@ -32,42 +39,37 @@ for _h in range(2):
     own("SB%d" % _h, "sbuf", [128, 3072], "bfloat16")
     own("G%d" % _h, "sbuf", [128, 2048], "bfloat16")
     own("MX%d" % _h, "sbuf", [128, 2048], "bfloat16")
-    own("NU%d" % _h, "sbuf", [128, NJ, 2, 64] if QUART else [128, NJ, 128], "uint16")
-    own("MO%d" % _h, "sbuf", [128, 64], "float32")
     for _t in range(RO + 1):
         own("Z%d%d" % (_t, _h), "sbuf", [128, 64], "bfloat16")
     for _t in range(RO):
         own("OUT%d%d" % (_t, _h), "sbuf", [128, 64], "bfloat16")
-    for _n in ("QK", "QU", "QX"):
-        own("%s%d" % (_n, _h), "psum", [128, 512], "float32")
-    own("QS%d" % _h, "psum", [128, 4, 8, 16] if AMAJ else [128, 512], "float32")
-    own("NI%d" % _h, "sbuf", [128, 4, 32] if AMAJ else [128, 128], "int32")
-    for _n, _w in (("UF", 20), ("Y", 20), ("SQ", 4), ("KM", 4), ("KY", 4), ("T", 64), ("C0F", 20), ("C0K", 20), ("HF", 4), ("E", 24), ("RK", 24), ("KS", 128),
-                   ("C0S", 20), ("RM", 4), ("XE", 20), ("NF1", 20), ("DE", 20), ("NC", 4), ("JC", 5), ("D15", 64), ("UX", 64), ("ZX", 64), ("SH", 64)):
-        alloc("%s%d" % (_n, _h), "PF", _w)
-    for _n, _w in (("Q", 4), ("KI", 4), ("OFI", 20), ("TI", 64), ("ZI", 4), ("HI", 4), ("HOI", 4), ("RI", 4), ("MI", 20), ("EI", 20)):
-        alloc("%s%d" % (_n, _h), "PI", _w)
-    for _n, _w in (("OU", 4), ("NL", 4), ("HO", 4), ("HU", 4), ("LRU", 64), ("O15", 4), ("RU", 4), ("MU", 20), ("EU", 24)):
-        alloc("%s%d" % (_n, _h), "PU", _w)
-    for _n, _w in (("M", 64), ("CM", 320), ("LRH", 64), ("EM", 384), ("MK", 128), ("SP", 64), ("SS", 4)):
-        alloc("%s%d" % (_n, _h), "PH", _w)
-    for _n, _w in (("MASK", 384), ("KG", 640)):
-        alloc("%s%d" % (_n, _h), "PB", _w)
-for _n, _w in (("XI", 144), ("BX", 128), ("CX", 64), ("DX", 96), ("G15", 1), ("B", 1), ("B16", 1), ("P1", 1), ("WF", 1), ("K15", 1), ("K1", 1),
-               ("LT", 16), ("INR", 16), ("TT", 16), ("TB", 32), ("I16", 64), ("KF", 2), ("KT", 31), ("K0", 1), ("K0J", 5), ("CJ", 5), ("AC", 1), ("AF", 1), ("SCN", 64), ("SC2", 64), ("SCU", 32), ("DB", 64), ("B1", 1), ("THR", 20), ("C2K", 1), ("CSH", 1), ("RST", 64)):
+    for _n in ("QK", "QR"):
+        for _q in range(2):
+            own("%s%d%d" % (_n, _h, _q), "psum", [128, 512], "float32")
+own("MO", "sbuf", [128, 128], "float32")
+for _n, _w in (("QQ", 16), ("S1", 256), ("S2", 256), ("S3", 256), ("KM", 8), ("HO", 8), ("T", 128), ("C0F", 40), ("C0K", 40), ("C0S", 40), ("RK", 40), ("M1", 16), ("M3", 8),
+               ("NP", 8), ("NK", 8), ("PQ", 16), ("RM", 8), ("NF", 40), ("KU", 40), ("YI", 40), ("DE", 40), ("NC", 8), ("D15", 128), ("SH", 128),
+               ("XI", 144), ("XH", 144), ("BX", 128), ("DX", 16), ("DJ", 40), ("DA", 40), ("RA", 128), ("NN", 256), ("NQ", 256), ("G15", 1), ("G7", 1), ("B", 1), ("P1", 1), ("WF", 1),
+               ("K15", 1), ("K1", 1), ("M2", 1), ("BA", 1), ("E0", 1), ("E13", 1), ("E2", 1), ("ES", 4), ("S16", 1), ("K2K", 1), ("LT", 16), ("INR", 16), ("TT", 16), ("TB", 32),
+               ("I16", 128), ("KF", 2), ("KM16", 2), ("KW", 32), ("W1K", 1), ("NB", 16), ("K0J", 40), ("AF", 1), ("OF", 5), ("OF0", 5), ("C2K", 1), ("CSH", 1), ("B19", 1),
+               ("BM19", 1), ("CK", 8), ("HB", 4), ("BASE", 40), ("D1", 128), ("D3", 256), ("ZERO", 128), ("DG", 64)):
     alloc(_n, "PF", _w)
-for _n, _w in (("PP", 1), ("PT", 1), ("PT2", 1), ("PT3", 1), ("KI32", 32), ("KI2", 32), ("KI3", 32), ("AI", 1)):
+for _n, _w in (("ZI", 8), ("RI", 16), ("UI", 40), ("SQ", 40), ("EI", 40), ("OI", 40),
+               ("PP", 1), ("PT", 1), ("PT2", 1), ("PT3", 1), ("PT4", 1), ("PT5", 1), ("PT6", 1), ("K16", 2), ("BI", 16), ("NI", 256), ("AI", 1)):
     alloc(_n, "PI", _w)
-for _n, _w in (("CK", 128), ("CG", 64), ("KR", 32)):
+for _n, _w in (("NU", 256), ("UL", 16), ("OU", 40), ("NL", 8), ("HU", 8), ("HV", 8), ("LRU", 128), ("O15", 8), ("RU", 16), ("RV", 8), ("C5", 8), ("MU", 40), ("EU", 48)):
+    alloc(_n, "PU", _w)
+for _n, _w in (("M", 128), ("CM", 640), ("LRH", 128), ("EM", 768), ("MK", 256), ("SP", 768), ("SS", 128), ("KG", 640), ("KR", 32), ("CF", 156), ("R1", 256), ("R2", 256)):
     alloc(_n, "PH", _w)
-for _n, _w in (("ZM", 144), ("ZA", 144), ("WB", 128), ("IDH", 128), ("NIH", 128), ("I2K", 128), ("ZM2", 144), ("CQ", 32), ("CN", 512), ("Z15", 144), ("IDW", 130), ("NID", 128), ("ONES", 128), ("BO", 128), ("TAB", 128), ("KW", 64), ("RL", 8)):
+for _n, _w in (("MASK", 768), ("XC", 128), ("W", 256), ("HR", 128), ("ZA", 144), ("ZM", 144), ("Z15", 144), ("ZW1", 144), ("ZW2", 144), ("IDW", 130), ("NID", 128), ("IDH", 128),
+               ("ONES", 128), ("BO", 128), ("TAB", 48), ("RAMP", 128), ("WM4", 1), ("RL", 8)):
     alloc(_n, "PB", _w)
 for _k in POOL:
     SCRATCH[_k] = ("sbuf", [128, (USED[_k] + 15) // 16 * 16], POOL[_k])
 for _n, _w in (("rec", 4096), ("st", 2048), ("nm", 128), ("arr", 128), ("wt", 1), ("kap", 2), ("so", 2048), ("mo", 128), ("zo", 128)):
     LAY[_n] = (_n, 0, _w)
 
-DMAS = ["arr0", "arr1", "st0", "st1", "rec0", "rec1", "nm", "wt", "kap", "so00", "so01", "so10", "so11", "mo0", "mo1", "zo0", "zo1"]
+DMAS = ["arr0", "arr1", "st0", "st1", "rec0", "rec1", "nm", "wt", "kap", "so00", "so01", "so10", "so11", "mo", "zo0", "zo1"]
 SEMAPHORES = ["cV", "cS", "cP", "cG", "sent"] + ["d" + n for n in DMAS] + ["a%d%d" % (t, h) for t in range(RO) for h in range(2)]
 
 
@@ -81,14 +83,6 @@ def r(name, a=0, b=None, s=1):
     return ("@", buf, mask, idx, cnt)
 
 
-def nd(name, *ix):
-    cols = [0]
-    for d, x in zip(SCRATCH[name][1][1:], ix):
-        cols = [c * d + k for c in cols for k in (range(x[0], x[1]) if isinstance(x, tuple) else [x])]
-    idx = (slice(None),) + tuple(slice(x[0], x[1]) if isinstance(x, tuple) else x for x in ix)
-    return ("@", name, sum(1 << c for c in cols), idx, len(cols))
-
-
 def ind(win, off):
     return ("#", win, off)
 
@@ -97,9 +91,8 @@ def is_acc(x):
     return isinstance(x, tuple) and len(x) > 0 and x[0] in ("@", "#")
 
 
-CFG = {"gather": 1.9, "pe": 0.3, "ls": 280, "lx": 280, "net": 3600, "pieces": [[512], [512], [512], [512]], "lists": [(0, 2), (2, 4)] if AMAJ else [(64, 128), (4, 64)],
-       "passes": 3, "mmsplit": 8, "fix": 0, "wl": 1.1, "fe": 0.8, "sabs": 0,
-       "vg": 16, "mn": 64, "sbs": False, "w4": 128, "g4": [(32, 64), (0, 32)], "ord4": [(0, 0), (0, 1), (1, 0), (1, 1)]}
+def landing(t, h):
+    return r("Z%d%d" % (t + 1, h))
 
 
 def build():
@@ -124,15 +117,21 @@ def build():
         ops.append({"eng": eng, "calls": calls, "busy": busy, "lat": lat, "sem": sem, "grp": grp, "rd": rd, "wr": wr, "after": after})
         return len(ops) - 1
 
+    def short(x):
+        return SCRATCH[x[1]][2] in ("bfloat16", "float16", "uint16")
+
     def vcost(out, ins, per):
         if out[0] == "#":
-            return 60 + 3.8 * 16 * out[2][4]
+            return 50 + 3.2 * 16 * out[2][4]
         if ins[0] == "#":
-            return 60 + gc_ * out[4]
+            return 50 + gc_ * out[4]
         return vc(per * out[4])
 
     def vc(n):
-        return max(CFG["mn"], n * CFG["fe"] + CFG["fix"])
+        return max(CFG["mn"], n * CFG["fe"])
+
+    def rate(out, a):
+        return 0.5 if out[0] == "@" and a[0] == "@" and short(out) and short(a) else 1
 
     def tt(out, a, b, op):
         both = a[0] == "@" and a[1][0] != "Q" and b[1][0] != "Q"
@@ -140,19 +139,32 @@ def build():
 
     def ts(out, a, s1, s2, op0, op1=None):
         args = (out, a, s1, s2, op0) if op1 is None else (out, a, s1, s2, op0, op1)
-        return add("V", [("ts", args, {})], vcost(out, a, 1))
+        return add("V", [("ts", args, {})], vcost(out, a, rate(out, a)))
 
     def cp(out, a):
-        return add("V", [("cp", (out, a), {})], vcost(out, a, 1))
+        return add("V", [("cp", (out, a), {})], vcost(out, a, rate(out, a)))
 
     def red(out, a, op):
         return add("V", [("red", (out, a, AxisListType.X, op), {})], vc(a[4]))
 
+    def scan(out, a, b):
+        return add("V", [("scan", (out, a, b, 1.0e9, AL.min, AL.add), {})], vc(out[4]))
+
     def ms(out, v):
-        return add("V", [("ms", (out, v), {})], max(64, out[4] // 2) + 6)
+        return add("V", [("ms", (out, v), {})], vc(out[4] * (0.5 if short(out) else 1)))
 
     def act(out, a, f, **kw):
-        return add("S", [("act", (out, a, f), kw)], 78 + gc_ * out[4] if a[0] == "#" else out[4] * CFG["fe"] + 80)
+        return add("S", [("act", (out, a, f), kw)], 65 + gc_ * out[4] if a[0] == "#" else vc(out[4]) + CFG["sfix"])
+
+    def lin(eng, out, a, scale, col):
+        if eng == "S":
+            return act(out, a, AF.Identity, scale=scale, bias=col)
+        return ts(out, a, scale, col, AL.mult, AL.add)
+
+    def pick(eng, out, a, scale=1.0):
+        if eng == "S":
+            return act(out, a, AF.Copy, scale=scale)
+        return cp(out, a) if scale == 1.0 else ts(out, a, scale, None, AL.mult)
 
     def mm(lst, start=True, stop=True, grp=None):
         calls = [("mm", (o, l, x, start and k == 0, stop and k == len(lst) - 1), {}) for k, (o, l, x) in enumerate(lst)]
@@ -163,81 +175,97 @@ def build():
         for a, b in zip(cuts, cuts[1:] + [len(calls)]):
             add("P", calls[a:b], sum(max(64, c[1][2][4]) for c in calls[a:b]) * CFG["pe"] + 5, lat=40, grp=grp)
 
+    def mms(lst):
+        add("P", [("mm", (o, l, x, True, True), {}) for o, l, x in lst], sum(max(64, x[4]) for o, l, x in lst) * CFG["pe"] + 5, lat=40)
+
     def sel(z, b):
         return r(z, 15 - b, 143 - b)
 
-    def mm16(out, z, name, a, b, extra=(), start=True, stop=True, grp=None):
-        return mm([(out, sel(z, q), r(name, a + q, b, 16)) for q in range(16)] + list(extra), start, stop, grp)
+    def mm16(out, z, name, a, b):
+        return mm([(out, sel(z, q), r(name, a + q, b, 16)) for q in range(16)])
 
     def dma(q, sem, out, src, nbytes):
-        lastd[q] = add(q, [("dma", (out, src), {})], 80, lat=2200 + nbytes // 200, sem="d" + sem, after=lastd.get(q) if sem[:2] not in ("so", "mo", "zo") else None)
+        lastd[q] = add(q, [("dma", (out, src), {})], 60, lat=2000 + nbytes // 300, sem="d" + sem, after=lastd.get(q) if sem[:2] not in ("so", "mo", "zo") else None)
 
     def iota(out, pat, base, cm, flag=True):
-        n = out[4]
-        return add("G", [("iota", (out, pat, base, cm), {"allow_small_or_imprecise_dtypes": True} if flag else {})], 160 + 2 * n)
+        k = add("G", [("iota", (out, pat, base, cm), {"allow_small_or_imprecise_dtypes": True} if flag else {})], 130 + 1.66 * out[4], after=lastd.get("G"))
+        lastd["G"] = k
+        return k
 
-    ID, SH, NID = r("IDW", 1, 129), r("IDW", 2, 130), r("NID")
-    XS = r("X", 64, 4160)
+    ID, SH1, NID, IDH = r("IDW", 1, 129), r("IDW", 2, 130), r("NID"), r("IDH")
+    XS = r("X", 0, 8192)
+    HX = r("XI", 0, 16)
+    OFC = 524288.0 + 2048.0
 
-    dma("Y", "arr0", r("Z00"), r("arr", 0, 64), 16384)
-    dma("S", "st0", r("SB0", 0, 1024), r("st", 0, 1024), 262144)
-    dma("Y", "wt", r("WTI"), ("@", "wt", 1, (slice(None),), 1), 4000)
     dma("Y", "kap", r("KPI"), r("kap"), 4000)
-    dma("Y", "arr1", r("Z01"), r("arr", 64, 128), 16384)
-    dma("S", "nm", r("NMI"), r("nm"), 300000)
-    dma("Y", "rec0", r("X", 64, 2112), r("rec", 0, 2048), 1100000)
-    dma("S", "rec1", r("X", 2112, 4160), r("rec", 2048, 4096), 1100000)
-    dma("Y", "st1", r("SB1", 0, 1024), r("st", 1024, 2048), 1500000)
+    dma("S", "wt", r("WTI"), ("@", "wt", 1, (slice(None),), 1), 4000)
+    dma("Y", "arr0", r("Z00"), r("arr", 0, 64), 30000)
+    dma("S", "st0", r("SB0", 0, 1024), r("st", 0, 1024), 300000)
+    dma("Y", "arr1", r("Z01"), r("arr", 64, 128), 60000)
+    dma("S", "nm", r("NMI"), r("nm"), 400000)
+    dma("Y", "st1", r("SB1", 0, 1024), r("st", 1024, 2048), 700000)
+    dma("S", "rec0", r("X", 0, 4096), r("rec"), 2000000)
+    dma("Y", "rec1", r("X", 4096, 8192), r("rec"), 2700000)
     iota(r("PP"), [[1, 1]], 0, 1, False)
     iota(r("XI"), [[1, 144]], 0, 0)
-    iota(r("CX"), [[1, 16], [256, 4]], 0, 0)
-    iota(r("DX"), [[1, 6], [1, 16]], 0, 0)
     iota(r("BX"), [[16, 8], [0, 16]], 15, 0)
+    iota(r("NN"), [[-1, 256]], 255, 0)
+    iota(r("NB"), [[-1, 16]], 16391, 0)
+    iota(r("XH"), [[1, 72], [0, 2]], 0, 0)
+    iota(r("DJ"), [[1, 5], [0, 8]], 1, 0)
+    iota(r("DG"), [[0, 64]], -1, 0)
+    iota(r("ZERO"), [[0, 128]], 0, 0)
+    iota(r("DA"), [[0, 40 // A], [32, A]], 0, 0)
+    iota(r("RA"), [[1, 4], [0, 32]], 0, 0)
+    iota(r("D1", 0, 32 * A), [[0, 32 * A]], -1, 0)
+    iota(r("SB0", 1024, 2048), [[0, 1024]], 0, 0)
+    iota(r("SB1", 1024, 2048), [[0, 1024]], 0, 0)
+    iota(r("TBL", 4097, T1), [[0, T1 - 4097]], 0, 0)
+    iota(r("I16"), [[0, 2], [16, 64]], 0, 0)
+    iota(r("D3"), [[0, 256]], 0, 0)
+    iota(r("ONES"), [[0, 128]], 1, 0)
     iota(r("IOTA"), [[1, 4096]], -2048, 0)
     ts(r("PT"), r("PP"), 112, None, AL.bitwise_and)
     ts(r("G15"), r("PT"), 15.0, None, AL.add)
+    ts(r("G7"), r("PT"), 0.5, 7.0, AL.mult, AL.add)
     ts(r("PT2"), r("PP"), 15, None, AL.bitwise_and)
     cp(r("B"), r("PT2"))
-    ts(r("B16"), r("PT2"), 16.0, None, AL.mult)
+    ts(r("BA"), r("PT2"), 32.0 * A, None, AL.mult)
     ts(r("P1"), r("PP"), 1.0, None, AL.add)
     ts(r("K15"), r("PT2"), 15.0, None, AL.is_equal)
     ts(r("K1"), r("PT2"), 1.0, None, AL.is_ge)
-    ts(r("WF"), r("WTI"), 0.25, None, AL.mult)
+    ts(r("S16"), r("PT2"), 1.0, 16.0, AL.is_ge, AL.mult)
+    ts(r("K2K"), r("PT2"), 1.0, 2048.0, AL.is_ge, AL.mult)
+    ts(r("PT3"), r("PP"), 1, None, AL.bitwise_and)
+    ts(r("M2"), r("PT3"), -float(T1), 2.0 ** 35 - 2048.0, AL.mult, AL.add)
+    cp(r("WF"), r("WTI"))
+    ts(r("WM4"), r("WTI"), -4.0, None, AL.mult)
     ts(r("IDW"), r("XI", 0, 130), r("P1"), None, AL.is_equal)
-    ts(r("NID"), r("XI", 1, 129), r("P1"), -1.0, AL.is_equal, AL.mult)
-    ts(r("ZM"), r("XI"), r("G15"), 4096.0, AL.is_equal, AL.mult)
-    ts(r("ZA"), r("XI"), r("G15"), -4096.0, AL.is_equal, AL.mult)
-    ts(r("WB"), r("BX"), r("G15"), r("WF"), AL.is_equal, AL.mult)
+    act(r("NID"), ID, AF.Copy, scale=-1.0)
+    act(r("IDH"), ID, AF.Copy, scale=0.5)
+    ts(r("ZM"), r("XI"), r("G15"), 1024.0, AL.is_equal, AL.mult)
+    act(r("ZA"), r("ZM"), AF.Copy, scale=-0.5)
     ts(r("Z15"), r("XI"), r("G15"), r("K15"), AL.is_equal, AL.mult)
-    ts(r("BO"), r("BX"), r("G15"), 1.0 / 16, AL.is_equal, AL.mult)
-    ms(r("ONES"), 1.0)
-    ms(r("CN"), -1024.0)
-    ts(r("IDH"), r("XI", 1, 129), r("P1"), 0.5, AL.is_equal, AL.mult)
-    ts(r("ZM2"), r("XI"), r("G15"), 8192.0, AL.is_equal, AL.mult)
-    ms(r("CQ"), 0.25)
-    ms(r("CSH"), 1023.75)
+    ts(r("ZW1"), r("XI"), r("G15"), r("WF"), AL.is_equal, AL.mult)
+    ts(r("ZW2"), r("XH"), r("G7"), r("WF"), AL.is_equal, AL.mult)
+    ts(r("BO"), r("BX"), r("G15"), None, AL.is_equal)
+    act(r("RAMP"), r("RA"), AF.Copy, scale=-4194304.0)
+    ms(r("CSH"), 511.75)
     ms(r("C2K"), 2048.0)
-    iota(r("DB"), [[0, 4], [1, 16]], 0, 0)
-    ts(r("PT3"), r("PP"), 1.0, None, AL.add)
-    ts(r("PT3"), r("PT3"), 15, None, AL.bitwise_and)
-    cp(r("B1"), r("PT3"))
-    ts(r("SCN"), r("DB"), r("B"), 512.0, AL.is_equal, AL.mult)
-    ts(r("SC2"), r("DB"), r("B1"), -256.0, AL.is_equal, AL.mult)
-    tt(r("SCN"), r("SCN"), r("SC2"), AL.add)
-    ts(r("SCU"), r("SCN", 0, 32), 1024.0, None, AL.mult)
-    ts(r("CK"), r("XI", 0, 128), 16.0, r("B"), AL.mult, AL.add)
-    if AMAJ:
-        iota(r("THR"), [[0, 5], [512, 4]], 16, 0)
-        ms(r("RST"), 0.0)
-        ms(r("RST", 0, 64, 32), 33554432.0)
-    ts(r("CG"), r("CX"), r("B16"), None, AL.add)
-    ts(r("I16"), r("XI", 0, 64), 16.0, None, AL.mult)
-    HX = r("XI", 0, 16)
-    ts(r("TAB", 0, 96), r("DX"), r("B"), None, AL.is_equal)
-    ts(r("TAB", 96, 112), HX, r("B"), r("K1"), AL.is_ge, AL.mult)
-    ts(r("TAB", 112, 128), HX, 5.0, r("B"), AL.add, AL.is_lt)
+    ms(r("B19"), 524288.0)
+    ms(r("AF"), 0.0)
+    ts(r("CK"), r("XI", 0, 8), 16.0, r("B"), AL.mult, AL.add)
+    ts(r("HB"), r("CK", 0, 4), 16.0, None, AL.mult)
+    ts(r("BASE"), r("DA"), r("BA"), None, AL.add)
+    ts(r("D1", 31, 32 * A, 32), r("BASE", 0, A), 31.0, None, AL.add)
+    ms(r("D3", 0, 256, 32), -128.0)
+    ts(r("D3", 31, 256, 32), r("CK"), 128.0, None, AL.add)
+    ts(r("DG", 15, 64, 16), r("HB"), 15.0, None, AL.add)
+    ts(r("TAB", 0, 16), HX, 1.0, r("B"), AL.add, AL.is_equal)
+    ts(r("TAB", 16, 32), HX, r("B"), r("K1"), AL.is_ge, AL.mult)
+    ts(r("TAB", 32, 48), HX, 5.0, r("B"), AL.add, AL.is_lt)
     ts(r("LT"), HX, r("B"), None, AL.is_gt)
-    tt(r("INR"), r("LT"), r("TAB", 112, 128), AL.add)
+    tt(r("INR"), r("LT"), r("TAB", 32, 48), AL.add)
     ts(r("INR"), r("INR"), -1.0, 1.0, AL.mult, AL.add)
     for par in range(2):
         ts(r("TT"), HX, -1.0, 1024.0 if par == 0 else -1024.0, AL.mult, AL.add)
@@ -247,243 +275,244 @@ def build():
     cp(r("KF"), r("KPI"))
     for q in range(2):
         ts(r("KR", 16 * q, 16 * q + 16), HX, r("B"), r("KF", q, q + 1), AL.is_equal, AL.mult)
-    mm([(r("QX1", 0, 32), r("BO"), r("KR"))])
-    ts(r("KT"), r("QX1", 1, 32), 128.0, None, AL.mult)
-    ts(r("K0"), r("QX1", 0, 1), 32.0, None, AL.mult)
-    ts(r("KI32"), r("QX1", 0, 32), 16.0, None, AL.mult)
-    ts(r("K0J"), r("XI", 1, 6), r("K0"), -16384.375, AL.mult, AL.add)
-    ts(r("KI2"), r("KI32"), 992, None, AL.bitwise_and)
-    ts(r("KW", 0, 32), r("KI2"), 1.0 / 8192, None, AL.mult)
-    ts(r("KI3"), r("KI32"), 31, None, AL.bitwise_and)
-    ts(r("KW", 32, 64), r("KI3"), 1.0 / 8192, None, AL.mult)
+    mms([(r("QK11", 0, 1), r("BO"), r("WM4"))])
+    ts(r("BI"), r("NB"), r("QK11", 0, 1), None, AL.add)
+    ts(r("W1K"), r("QK11", 0, 1), 256.0, None, AL.mult)
+    mms([(r("QK10", 0, 32), r("BO"), r("KR"))])
+    cp(r("KW"), r("QK10", 0, 32))
+    ts(r("K0J"), r("DJ"), r("KW", 0, 1), None, AL.mult)
+    ms(r("KW", 0, 1), 0.0)
+
+    ts(r("BI"), r("BI"), 15, None, AL.bitwise_and)
+    ts(r("K16"), r("KPI"), 15, None, AL.bitwise_and)
+    ts(r("KM16", 0, 1), r("K16", 0, 1), 256.0, r("K1"), AL.mult, AL.mult)
+    ts(r("KM16", 1, 2), r("K16", 1, 2), 256.0, None, AL.mult)
+    ts(r("KF", 0, 1), r("KF", 0, 1), r("K1"), None, AL.mult)
+    for q in range(2):
+        ts(r("CF", 64 * q, 64 * q + 64, 4), r("BI"), r("S16") if q == 0 else 16.0, r("KF", q, q + 1), AL.mult, AL.add)
+        ts(r("CF", 64 * q + 1, 64 * q + 64, 4), r("BI"), r("KM16", q, q + 1), None, AL.mult)
+        ts(r("CF", 64 * q + 2, 64 * q + 64, 4), HX, 0.0, r("K1") if q == 0 else 1.0, AL.mult, AL.add)
+        ts(r("CF", 64 * q + 7, 64 * q + 64, 8), r("XI", 0, 8), 0.0, r("K2K") if q == 0 else 2048.0, AL.mult, AL.add)
+    ts(r("CF", 3, 128, 8), HX, 0.0, None, AL.mult)
+    ts(r("CF", 128, 156), r("XI", 0, 28), 0.0, None, AL.mult)
+    ts(r("PT4"), r("PP"), 31, None, AL.bitwise_and)
+    ts(r("PT5"), r("PP"), 29, None, AL.bitwise_and)
+    ts(r("PT6"), r("PP"), 5, None, AL.arith_shift_right)
+    ts(r("E0"), r("PT4"), 0.0, None, AL.is_equal)
+    ts(r("E2"), r("PT4"), 2.0, None, AL.is_equal)
+    ts(r("E13"), r("PT5"), 1.0, None, AL.is_equal)
+    cp(r("BM19"), r("PT6"))
+    ts(r("ES"), r("XI", 0, 4), r("BM19"), None, AL.is_equal)
+    act(r("NQ"), r("NN"), AF.Square)
+    ts(r("NI"), r("NQ"), 1.0 / 32, -0.484375, AL.mult, AL.add)
+    act(r("R1"), r("NN"), AF.Identity, scale=r("E0"), bias=r("E13"))
+    ts(r("R2"), r("NI"), r("E2"), None, AL.mult)
+    tt(r("RR", 1024, 1280), r("R1"), r("R2"), AL.add)
+    for s in range(4):
+        ts(r("RR", 256 * s, 256 * s + 256), r("RR", 1024, 1280), r("ES", s, s + 1), None, AL.mult)
+    for q in range(2):
+        mms([(r("QK0%d" % q, 128 * i, 128 * i + 128), r("CF", 16 * q + 4 * i, 16 * q + 4 * i + 128), ID) for i in range(4)])
+        act(r("CT", 512 * q, 512 * q + 512), r("QK0%d" % q), AF.Copy)
+    for x in range(16):
+        bank, tmp = ("QK10", "QK11", "QK00", "QK01")[x % 4], r("G%d" % (x % 2), 512 * (x // 2 % 4), 512 * (x // 2 % 4) + 512)
+        s, i = x // 4, 2 * x % 8
+        blocks = [(r(bank, 256 * k, 256 * k + 256), r("CT", 128 * (i + k), 128 * (i + k) + 128), r("RR", 256 * s, 256 * s + 256)) for k in range(2)]
+        mms(blocks)
+        act(tmp, r(bank), AF.Identity, bias=r("B19"))
+        o = T1 * (x // 8) + 1 + 512 * (x % 8)
+        if CFG["st"] and x % CFG["st"] == CFG["st"] - 1:
+            add("P", [("mm", (r(bank), NID, tmp, True, False), {})] + [("mm", b + (False, k == 1), {}) for k, b in enumerate(blocks)], 1024 * CFG["pe"], lat=40)
+            act(r("TBL", o, o + 512), r(bank), AF.Copy)
+        else:
+            tt(r("TBL", o, o + 512), r(bank), tmp, AL.subtract)
+    cp(r("TBL", 0, T1 + 1, T1), r("TBL", 4096, T1 + 4097, T1))
+    TW = r("TBL", 0, T1 + 4097)
+
     NONE = 15 * 16384 + 8192
     RS = 1.0 / 524288
-    for h in range(2):
-        ms(r("SB%d" % h, 1024, 2048), 0.0)
-        ts(r("M%d" % h), r("NMI", 64 * h, 64 * h + 64), -2048.0, None, AL.add)
-        ts(r("NC%d" % h), r("CK", 0, 4), 64.0 * h, 32.0, AL.add, AL.mult)
-        ts(r("RK%d" % h, 0, 4), r("CK", 0, 4), float(NONE + 4096 * h), RS, AL.add, AL.mult)
-        ts(r("JC%d" % h), r("XI", 1, 6), (64.0 / 16384) * (1 - h), None, AL.add)
+    ts(r("M"), r("NMI"), -2048.0, None, AL.add)
+    ts(r("NC"), r("CK"), 32.0, None, AL.mult)
+    ts(r("NK"), r("CK"), float(NONE + 4096), RS, AL.add, AL.mult)
 
-    def mid(h, d):
-        n = lambda x: x + str(h)
-        dst = r(n("SB"), 1024 + d, 2048, 16)
-        ts(r(n("SP")), r(n("T")), 0.5, 1023.75, AL.mult, AL.add)
-        ts(dst, r(n("SP")), -1024.0, None, AL.add)
-
-    def scan(out, src):
-        add("V", [("scan", (out, r("SCN"), src, 0.0, AL.add, AL.min), {})], vc(64))
+    def offsets():
+        ts(r("OI"), r("K0J"), r("AF"), None, AL.add)
+        ts(r("OI"), r("OI"), 4095, None, AL.bitwise_and)
+        ts(r("OF0"), r("OI", 0, 40, 8), r("K1"), OFC, AL.mult, AL.add)
+        ts(r("OF"), r("OI", 0, 40, 8), OFC, None, AL.add)
+        for j in range(NJ):
+            lin(CFG["cod"], r("CC", 256 * j + 1, 256 * j + 256, 2), r("ZERO"), 1.0, r("OF", j, j + 1))
 
     def store(t, h):
-        n = lambda x: x + str(h)
         z = "Z%d%d" % (t, h)
-        mm([(r(n("QU"), 128, 192), r("BO"), r(z))])
-        scan(r(n("ZX")), r(n("QU"), 128, 192))
-        ts(r(n("ZI")), r(n("ZX"), 15, 64, 16), 16.0, None, AL.mult)
-        ts(r(n("ZI")), r(n("ZI")), 31, None, AL.bitwise_and)
-        tt(r(n("E"), 0, 4), r(n("ZI")), r(n("NC")), AL.add)
-        cp(r(n("NL")), r(n("E"), 0, 4))
-        cp(ind(XS, r(n("NL"))), r(z))
+        four = lambda x: r(x, 4 * h, 4 * h + 4)
+        ps = r("QR%d0" % h, 0, 4)
+        mm16(ps, "ZM", z, 0, 64)
+        ts(four("ZI"), ps, 1.0 / 1024, None, AL.mult)
+        ts(four("ZI"), four("ZI"), 31, None, AL.bitwise_and)
+        tt(four("NL"), four("ZI"), four("NC"), AL.add)
+        cp(ind(r("X", 0, 4096), four("NL")), r(z))
+        cp(ind(r("X", 4096, 8192), four("NL")), r(z))
+
+    def slot(h, tb, nt, d):
+        return r("SB%d" % h, 1024 + 16 * tb + d, 1024 + 16 * (tb + nt), 16)
+
+    def after_mid(h, tb, nt, d):
+        o = 64 * h + tb
+        sp = r("SP", 128 * d + o, 128 * d + o + nt)
+        ts(slot(h, tb, nt, d), sp, -1024.0, None, AL.add)
+        if d < NJ:
+            lin(CFG["sh"], r("SH", o, o + nt), sp, 0.5, r("CSH"))
+
+    def lanes(bank, j, t0, t1):
+        w = t1 - t0
+        return [(r(bank[0], bank[1] + tb + a, bank[1] + tb + 16 * A, A), sel("ZM", 0), r("CM", 128 * j + t0 + tb + 16 * a, 128 * j + t0 + tb + 16 * a + 16))
+                for tb in range(0, w, 16 * A) for a in range(A)]
+
+    def even(bank, j, t0, t1):
+        lin(CFG["cev"], r("CC", 256 * j + 2 * t0, 256 * j + 2 * t1, 2), r(bank[0], bank[1], bank[1] + t1 - t0), 1.0 / 1024, r("OF0", j, j + 1))
 
     def gap(t, h):
         n = lambda x: x + str(h)
+        four = lambda x: r(x, 4 * h, 4 * h + 4)
+        half = lambda x, o=0: r(x, o + 64 * h, o + 64 * h + 64)
         z = r("Z%d%d" % (t, h))
         so = 2048 * (t % 2)
-        for q, bank in enumerate(("QK", "QX")):
+        for q in (1, 0):
+            bank = n("QR") + str(q)
             for k2 in range(2):
                 calls = []
                 for k in range(8 * q + 4 * k2, 8 * q + 4 * k2 + 4):
-                    o = r(n(bank), 64 * (k % 8), 64 * (k % 8) + 64)
+                    o = r(bank, 64 * (k % 8), 64 * (k % 8) + 64)
                     calls.append(("mm", (o, ID, r(n("SB"), so + k, so + 1024, 16), True, False), {}))
                     calls.append(("mm", (o, NID, z, False, True), {}))
-                add("P", calls, 8 * 64 * CFG["pe"] + 20, lat=40)
-            act(r(n("MX"), 512 * q, 512 * q + 512), r(n(bank)), AF.Abs)
-        key = r(n("QU"), 192, 256)
-        mm16(key, "ZM", n("MX"), 0, 1024, [(key, ID, r("CG"))])
+                add("P", calls, 8 * 64 * CFG["pe"] + 5, lat=40)
+            act(r(n("MX"), 512 * q, 512 * q + 512), r(bank), AF.Abs)
+        kb = n("QR") + "1"
+        mm16(r(kb, 0, 64), "ZM", n("MX"), 0, 1024)
+        o = 128 * h
         for a in range(4):
-            red(r(n("KM"), a, a + 1), r(n("QU"), 192 + a, 256, 4), AL.min)
-        cp(r(n("KI")), r(n("KM")))
-        ts(r(n("HOI")), r(n("KI")), 1023, None, AL.bitwise_and)
-        cp(r(n("HO")), r(n("HOI")))
-        tt(r(n("T")), ind(r(n("SB"), so, so + 1024), r(n("HO"))), z, AL.add)
-        mid(h, 0)
-        ts(r(n("HI")), r(n("KI")), 15, None, AL.bitwise_and)
-        cp(r(n("HU")), r(n("HI")))
-        ts(r(n("HF")), r(n("HI")), 16384.0 * RS, None, AL.mult)
-        hu = r(n("HU"))
-        for j in range(1, NJ + 1):
-            tt(r(n("CM"), 64 * j - 64, 64 * j), ind(r("TAB", 16 * j, 16 * j + 16), hu), r(n("M")), AL.mult)
-        mm16(r(n("QU"), 8, 28), "ZM", n("CM"), 0, 320)
-        ts(nd(n("NU"), (0, NJ), (0, 2), (0, 2)) if QUART else nd(n("NU"), (0, NJ), (0, 4)), r(n("QU"), 8, 28), 1.0 / 4096, 2048.0, AL.mult, AL.add)
-        act(r(n("C0F")), r(n("QU"), 8, 28), AF.Identity, scale=1.0 / 4096, bias=r("C2K"))
-        act(r(n("C0S")), r(n("C0F")), AF.Copy, scale=RS)
-        for a in range(4):
-            act(r(n("C0K"), a, 20, 4), r(n("JC")), AF.Identity, scale=16384.0 * RS, bias=r(n("HF"), a, a + 1))
-        tt(r(n("C0K")), r(n("C0K")), r(n("C0S")), AL.add)
+            scan(r("S1", o + 16 * a, o + 16 * a + 16), r(kb, a, 64, 4), r("DG", 16 * a, 16 * a + 16))
+            red(r("KM", 4 * h + a, 4 * h + a + 1), r(kb, a, 64, 4), AL.min)
+        tt(four("HV"), r("S1", o + 15, o + 64, 16), four("KM"), AL.subtract)
+        tt(half("T"), ind(r(n("SB"), so, so + 1024), four("HV")), z, AL.add)
+        ts(half("SP"), half("T"), 0.5, 1023.75, AL.mult, AL.add)
+        after_mid(h, 0, 64, 0)
+        tt(four("HU"), four("HV"), r("HB"), AL.subtract)
+        tt(half("CM"), ind(r("TAB", 0, 16), four("HU")), half("M"), AL.mult)
+        bank = (n("QK") + "1", 0)
+        mms(lanes(bank, 0, 64 * h, 64 * h + 64))
+        even(bank, 0, 64 * h, 64 * h + 64)
+
+    def masks(t, kb):
+        hu = r("HU")
+        cp(r("HR"), ind(HX, hu))
+        for d in (2, 3, 4, 5, 0, 1):
+            ts(r("MASK", 128 * d, 128 * d + 128), r("HR"), float(d), r("B"), AL.add, AL.is_equal)
+        for j in range(1, NJ):
+            tt(r("CM", 128 * j, 128 * j + 128), r("MASK", 128 * j + 128, 128 * j + 256), r("M"), AL.mult)
+            mms(lanes((kb, 128 * j - 128), j, 0, 128))
+        for j in range(1, NJ):
+            even((kb, 128 * j - 128), j, 0, 128)
         par = t % 2
-        tt(r(n("LRH")), ind(r("TB", 16 * par, 16 * par + 16), hu), r("I16"), AL.add)
-        cp(r(n("LRU")), r(n("LRH")))
-        mm16(r(n("QU"), 28, 32), "Z15", n("LRH"), 0, 64)
-        cp(r(n("O15")), r(n("QU"), 28, 32))
-        for d in range(6):
-            act(r(n("MASK"), 64 * d, 64 * d + 64), ind(r("TAB", 16 * d, 16 * d + 16), hu), AF.Copy)
-        tt(r(n("MK"), 0, 64), ind(r("TAB", 96, 112), hu), r(n("M")), AL.mult)
-        tt(r(n("MK"), 64, 128), ind(r("TAB", 112, 128), hu), r(n("M")), AL.mult)
+        tt(r("LRH"), ind(r("TB", 16 * par, 16 * par + 16), hu), r("I16"), AL.add)
+        cp(r("LRU"), r("LRH"))
+        tt(r("MK", 0, 128), ind(r("TAB", 16, 32), hu), r("M"), AL.mult)
+        tt(r("MK", 128, 256), ind(r("TAB", 32, 48), hu), r("M"), AL.mult)
+        cp(r("EU", 0, 8), r("NL"))
+
+    def names(t, cb):
+        mm16(r(cb, 320, 360), "ZM", "CM", 0, 640)
+        mm16(r(cb, 360, 368), "Z15", "LRH", 0, 128)
+        act(r("C0F"), r(cb, 320, 360), AF.Identity, scale=1.0 / 1024, bias=r("C2K"))
+        cp(r("O15"), r(cb, 360, 368))
+        cp(r("C5"), r("C0F", 32, 40))
+        act(r("C0S"), r("C0F"), AF.Copy, scale=RS)
+        for j in range(NJ):
+            ts(r("C0K", 8 * j, 8 * j + 8), r("HU"), j + 1.0, 16384.0 * RS, AL.add, AL.mult)
+        tt(r("C0K"), r("C0K"), r("C0S"), AL.add)
+        tt(r("NP"), r("NK"), r("C0K", 32, 40), AL.min)
+        pick(CFG["xc"], r("XC"), ind(XS, r("C5")), 0.5)
 
     last = [None]
 
-    def corr(t, h, j):
+    def corr(t, h, tb, j, hook):
         n = lambda x: x + str(h)
-        s = r(n("SB"), 1024 + j - 1, 2048, 16)
-        mm([(r(n("QU"), 64, 128), r("WB"), r("CN", 0, 64)), (r(n("QU"), 64, 128), r("WB"), r(n("SP")))])
-        W = max(max(x) for x in CFG["pieces"])
-        if AMAJ:
-            add("P", [("mm", (nd(n("QS"), (0, 4), q, (0, 16)), ID, s, True, True), {}) for q in range(W // 16)], 4 * W * CFG["pe"] + 5, lat=40)
-        else:
-            add("P", [("mm", (r(n("QS"), 64 * q, 64 * q + 64), r("IDH"), s, True, True), {}) for q in range(W // 64)], W * CFG["pe"] + 5, lat=40)
-        act(r(n("SH")), s, AF.Identity, scale=0.5, bias=r("CSH"))
-        NS_ = CFG["sabs"]
-        if NS_:
-            mm([(r(n("QK"), 128, 132), sel("ZM", b), r(n("SB"), 1024 + j - 1 + 16 * b, 2048, 256)) for b in range(16)])
-            ts(r(n("SS")), r(n("QK"), 128, 132), 1.0 / 4096, -2048.0, AL.mult, AL.add)
-        scan(r(n("UX")), r(n("QU"), 64, 128))
-        pu = r(n("UX"), 15, 64, 16)
-        uf, y = r(n("UF"), 4 * j - 4, 4 * j), r(n("Y"), 4 * j - 4, 4 * j)
-        ts(r(n("Q")), pu, -0.5 + 1.0 / 8192, None, AL.add)
-        tt(uf, pu, r(n("Q")), AL.subtract)
-        tt(r(n("SQ")), uf, uf, AL.mult)
-        ts(y, r(n("SQ")), 1048576.0, r("K0J" if t == 0 else "CJ", j - 1, j), AL.mult, AL.add)
-        for a in range(4):
-            c = 4 * j - 4 + a
-            ts(nd(n("NI"), a, (1, 32)) if AMAJ else r(n("NI"), 4 + a, 128, 4), r("KT"), r(n("UF"), c, c + 1), r(n("Y"), c, c + 1), AL.mult, AL.add)
-        for ab in CFG["lists"]:
-            ni = nd(n("NI"), ab, (1, 32)) if AMAJ else r(n("NI"), ab[0], ab[1])
-            ts(ni, ni, 1, 4095, AL.arith_shift_right, AL.bitwise_and)
-            cp(nd(n("NU"), j - 1, ab, (1, 32)) if AMAJ else nd(n("NU"), j - 1, ab), ni)
-        for grp in ((0, 1) if AMAJ else (1, 0)):
-            key = r(n(("QK", "QX")[grp]), 0, 64) if AMAJ else r(n("QK"), 64 * grp, 64 * grp + 64)
-            for a in ((2 * grp, 2 * grp + 1) if AMAJ else (2 * grp + 1, 2 * grp)):
-                lst = nd(n("NU"), j - 1, a, (0, 32)) if AMAJ else nd(n("NU"), j - 1, (32 * a, 32 * a + 32))
-                k = act(r(n("G"), 512 * a, 512 * a + 512), ind(XS, lst), AF.Copy, scale=0.5)
+        kb, rb = "QK%d%d" % (h, tb // 32), "QR%d%d" % (h, tb // 32)
+        nt, bn, rep = 16 * A, 8 // A, CFG["rep"]
+        o = 64 * h + tb
+        sv, u0, g0, c0 = 128 * (j - 1) + o, o // 8, 32 * tb, 8 * (j - 1) + o // 16
+        pu = r(kb, 448, 448 + 2 * A)
+        mm([(pu, r("ZW2", 14 - 2 * i, 142 - 2 * i), r("SP", sv + 16 * (i % A) + i // A, sv + 16 * (i % A) + 16, bn)) for i in range(8)])
+        mms([(r(rb, rep * a + i, rep * nt, rep * A), IDH, slot(h, tb + 16 * a, 16, j - 1)) for a in range(A) for i in range(rep)])
+        qq, ul = r("QQ", u0, u0 + 2 * A), r("UL", u0, u0 + 2 * A)
+        ts(qq, pu, 2.0 ** 35, r("M2"), AL.add, AL.subtract)
+        tt(ul, qq, pu, AL.subtract)
+        cc = 256 * (j - 1) + 2 * o
+        tt(r("NU", 2 * o, 2 * o + 2 * nt), ind(TW, ul), r("CC", cc, cc + 2 * nt), AL.add)
+        if hook:
+            hook(kb)
+        key = r(kb, 0, 32 * A)
+        gid = (t, h, j, tb)
+        mm([(key, ID, r("RAMP", 0, 32 * A))], stop=False, grp=gid)
+        st = 32 // rep
+        pieces = CFG["vp"].get(o // 32, [p + ("S",) for p in CFG["pieces"]])
+        for x, (b0, b1, eng) in enumerate(pieces):
+            lo, hi = g0 + 32 * A * b0, g0 + 32 * A * b1
+            k = pick(eng, r(n("G"), lo, hi), ind(XS, r("NU", 128 * h + lo // 16, 128 * h + hi // 16)), 0.5)
+            if eng == "S":
                 ops[k]["after"] = last[0]
                 last[0] = k
-                o = 512 * a
-                if a >= 4 - NS_:
-                    mm([(r(n("QX")), ID, r(n("G"), o, o + 512))] + [(r(n("QX"), 64 * q, 64 * q + 64), r("NIH"), s) for q in range(8)])
-                    act(r(n("MX"), o, o + 512), r(n("QX")), AF.Abs, scale=0.5)
-                    continue
-                for w in CFG["pieces"][a if AMAJ else 3 - a]:
-                    tt(r(n("MX"), o, o + w), r(n("G"), o, o + w), nd(n("QS"), a, (0, w // 16), (0, 16)) if AMAJ else r(n("QS"), 0, w), AL.max)
-                    o += w
-            gid = (t, h, j, grp)
-            ck = (key, ID, r("CK", 64 * grp, 64 * grp + 64))
-            if grp == 1 and NS_:
-                lo = 128 - 32 * NS_
-                mm([ck, (r(n("QK"), lo, 128), r("I2K"), r("C2B", 0, 128 - lo))]
-                   + [(r(n("QK"), c, c + 4), r("I2K"), r(n("SS"))) for c in range(lo, 128, 4)], stop=False, grp=gid)
-                if NS_ == 1:
-                    mm16(r(n("QK"), 64, 96), "ZA", n("G"), 1024, 1536, start=False, stop=False, grp=gid)
-                mm16(key, "ZM2", n("MX"), 1024, 2048, start=False, grp=gid)
-                continue
-            mm16(key, "ZA", n("G"), 1024 * grp, 1024 * grp + 1024, stop=False, grp=gid)
-            mm16(key, "ZM2", n("MX"), 1024 * grp, 1024 * grp + 1024, [ck], start=False, grp=gid)
-            if AMAJ:
-                add("V", [("scan", (r(n("KS"), 64 * grp, 64 * grp + 64), r("RST"), key, 0.0, AL.add, AL.min), {})], vc(64))
-        if AMAJ:
-            cp(r(n("KI")), r(n("KS"), 31, 128, 32))
-        else:
-            for a in range(4):
-                red(r(n("KM"), a, a + 1), r(n("QK"), a, 128, 4), AL.min)
-            cp(r(n("KI")), r(n("KM")))
-        ofi = r(n("OFI"), 4 * j - 4, 4 * j)
-        ts(ofi, r(n("KI")), 2047, None, AL.bitwise_and)
-        cp(r(n("OU")), ofi)
-        tt(r(n("SP")), ind(r(n("G")), r(n("OU"))), r(n("SH")), AL.add)
-        ts(r(n("SB"), 1024 + j, 2048, 16), r(n("SP")), -1024.0, None, AL.add)
+            for y in range(st):
+                tt(r(n("MX"), lo + y, hi, st), r(n("G"), lo + y, hi, st), r(rb, rep * A * b0, rep * A * b1), AL.max)
+            for z, src, end in (("ZA", "G", False), ("ZM", "MX", x == len(pieces) - 1)):
+                mm([(key, sel(z, b), r(n(src), g0 + 32 * A * b, g0 + 32 * A * (b + 1))) for b in range(b0, b1)], start=False, stop=end, grp=gid)
+        row = lambda x: r(x, 2 * o, 2 * o + 32 * A)
+        ends = lambda x: r(x, 2 * o + 31, 2 * o + 32 * A, 32)
+        scan(row("S2"), key, r("ZERO", 0, 32 * A))
+        if j == NJ:
+            scan(row("S3"), key, row("D3"))
+            tt(r("RV", o // 16, o // 16 + A), ends("S3"), ends("S2"), AL.subtract)
+        scan(row("S1"), key, r("D1", 0, 32 * A))
+        ou = r("OU", c0, c0 + A)
+        tt(ou, ends("S1"), ends("S2"), AL.subtract)
+        tt(r("SP", 128 * j + o, 128 * j + o + nt), ind(r(n("G"), g0, g0 + 32 * nt), ou), r("SH", o, o + nt), AL.add)
+        after_mid(h, tb, nt, j)
 
-    def corr4(t, h, q, j):
-        n = lambda x: x + str(h)
-        base = 1024 + j - 1 + 512 * q
-        s = r(n("SB"), base, 1024 + 512 * q + 512, 16)
-        sp, sh = r(n("SP"), 32 * q, 32 * q + 32), r(n("SH"), 32 * q, 32 * q + 32)
-        pq = r(n("QU"), 64 + 32 * q, 96 + 32 * q)
-        mm([(pq, r("WB"), r("CN", 0, 32)), (pq, r("IDH"), r("CN", 0, 32)), (pq, r("IDH"), r("CQ")), (pq, r("WB"), sp)])
-        W = CFG["w4"]
-        qs = n(("QS", "QX")[q])
-        late = CFG["sbs"] and j > 1
-        if late:
-            mm([(r(qs, 0, W), r("IDH"), r("CN", 0, W))] + [(r(qs, 32 * k, 32 * k + 32), r("IDH"), sp) for k in range(W // 32)])
-            act(s, r(qs, 0, 32), AF.Copy, scale=2.0)
-            act(sh, r(qs, 0, 32), AF.Identity, bias=r("CSH"))
-        else:
-            add("P", [("mm", (r(qs, 32 * k, 32 * k + 32), r("IDH"), s, True, True), {}) for k in range(W // 32)], 2 * W * CFG["pe"] + 5, lat=40)
-            act(sh, s, AF.Identity, scale=0.5, bias=r("CSH"))
-        add("V", [("scan", (r(n("UX"), 32 * q, 32 * q + 32), r("SCU"), pq, 0.0, AL.add, AL.min), {})], vc(32))
-        pu = r(n("UX"), 32 * q + 15, 32 * q + 32, 16)
-        c0 = 4 * j - 4 + 2 * q
-        two = lambda x: r(n(x), 2 * q, 2 * q + 2)
-        uf, y = r(n("UF"), c0, c0 + 2), r(n("Y"), c0, c0 + 2)
-        ts(two("SQ"), pu, 1.5 * 2.0 ** 33, 1.5 * 2.0 ** 33, AL.add, AL.subtract)
-        for a in range(2):
-            c = 32 * q + 16 * a + 15
-            ts(r(n("UF"), c0 + a, c0 + a + 1), r(n("UX"), c, c + 1), r(n("SQ"), 2 * q + a, 2 * q + a + 1), 511.875, AL.subtract, AL.add)
-        for a in range(2):
-            ua = r(n("UF"), c0 + a, c0 + a + 1)
-            ts(r(n("Y"), c0 + a, c0 + a + 1), ua, ua, r("K0J" if t == 0 else "CJ", j - 1, j), AL.mult, AL.add)
-        for a in range(2):
-            ts(r(n("NI"), 64 * q + 2 + a, 64 * q + 64, 2), r("KT"), r(n("UF"), c0 + a, c0 + a + 1), r(n("Y"), c0 + a, c0 + a + 1), AL.mult, AL.add)
-        ni = r(n("NI"), 64 * q + 2, 64 * q + 64)
-        ts(ni, ni, 1, 4095, AL.arith_shift_right, AL.bitwise_and)
-        cp(nd(n("NU"), j - 1, q, (2, 64)), ni)
-        g0 = 1024 * q
-        for a, b in CFG["g4"]:
-            if b - a <= CFG["vg"]:
-                ts(r(n("G"), g0 + 16 * a, g0 + 16 * b), ind(XS, nd(n("NU"), j - 1, q, (a, b))), 0.5, None, AL.mult)
-            else:
-                k = act(r(n("G"), g0 + 16 * a, g0 + 16 * b), ind(XS, nd(n("NU"), j - 1, q, (a, b))), AF.Copy, scale=0.5)
-                ops[k]["after"] = last[0]
-                last[0] = k
-            for o in range(g0 + 16 * a, g0 + 16 * b, W):
-                w = min(W, g0 + 16 * b - o)
-                tt(r(n("MX"), o, o + w), r(n("G"), o, o + w), r(qs, 0, w), AL.max)
-        key = r(n("QK"), 64 * q, 64 * q + 64)
-        gid = (t, h, j, q)
-        mm16(key, "ZA", n("G"), g0, g0 + 1024, stop=False, grp=gid)
-        mm16(key, "ZM2", n("MX"), g0, g0 + 1024, [(key, ID, r("CK", 0, 64))], start=False, grp=gid)
-        for a in range(2):
-            red(r(n("KM"), 2 * q + a, 2 * q + a + 1), r(n("QK"), 64 * q + a, 64 * q + 64, 2), AL.min)
-        ts(two("KY"), two("KM"), 1.5 * 2.0 ** 34, 1.5 * 2.0 ** 34, AL.add, AL.subtract)
-        for a in range(2 * q, 2 * q + 2):
-            ts(r(n("OU"), a, a + 1), r(n("KM"), a, a + 1), r(n("KY"), a, a + 1), None, AL.subtract)
-        tt(r(n("OFI"), c0, c0 + 2), two("KM"), two("KY"), AL.subtract)
-        tt(sp, ind(r(n("G"), g0, g0 + 1024), two("OU")), sh, AL.add)
-        if j == NJ or not CFG["sbs"]:
-            ts(r(n("SB"), base + 1, 1024 + 512 * q + 512, 16), sp, -1024.0, None, AL.add)
+    def prepare(t):
+        par = t % 2
+        tt(r("SS"), r("XC"), r("SH"), AL.add)
+        for h in range(2):
+            ts(slot(h, 0, 64, NJ), r("SS", 64 * h, 64 * h + 64), -1024.0, None, AL.add)
+            win = r("SB%d" % h, 1024 * par, 1024 * par + 2048)
+            tt(r("D15", 64 * h, 64 * h + 64), ind(win, r("O15", 4 * h, 4 * h + 4)), r("Z%d%d" % (t, h)), AL.subtract)
+        act(r("X", 8192, 8320), r("D15"), AF.Abs)
+        tt(r("NF", 0, 32), r("OU", 0, 32), r("BASE", 0, 32), AL.is_equal)
+        tt(r("RK", 0, 32), r("NF", 0, 32), r("C0K", 0, 32), AL.add)
+        tt(r("M1"), r("RK", 0, 16), r("RK", 16, 32), AL.min)
+        tt(r("M3"), r("M1", 0, 8), r("M1", 8, 16), AL.min)
+        tt(r("PQ", 0, 8), r("M3"), r("NK"), AL.min)
+        tt(r("PQ", 8, 16), r("M3"), r("NP"), AL.min)
+        ts(r("RI"), r("PQ"), 524288.0, None, AL.mult)
+        ts(r("RI"), r("RI"), 8191, None, AL.bitwise_and)
+        cp(r("RU"), r("RI"))
+        pick(CFG["w"], r("W"), ind(r("X", 4096, 8320), r("RU")))
+
+    def squares(t, kb):
+        mm16(r(kb, 128, 168), "ZW1", "SP", 0, 640)
+        ts(r("UI"), r(kb, 128, 168), r("W1K"), None, AL.add)
+        ts(r("UI"), r("UI"), 4095, None, AL.bitwise_and)
+        tt(r("SQ"), r("UI"), r("UI"), AL.mult)
+        ts(r("SQ"), r("SQ"), 5, None, AL.arith_shift_right)
+        tt(r("YI"), r("SQ"), r("OI"), AL.add)
+        tt(r("DE"), r("C0F"), r("YI"), AL.subtract)
 
     def release(t, h):
-        n = lambda x: x + str(h)
-        par = t % 2
-        win = r(n("SB"), 1024 * par, 1024 * par + 2048)
-        tt(r(n("D15")), ind(win, r(n("O15"))), r("Z%d%d" % (t, h)), AL.subtract)
-        act(r("X", 4160 * h, 4160 * h + 64), r(n("D15")), AF.Abs)
-        if AMAJ:
-            tt(r(n("NF1")), r(n("OFI")), r("THR"), AL.is_lt)
-        else:
-            ts(r(n("NF1")), r(n("OFI")), 32.0 if QUART else 64.0, None, AL.is_lt)
-        tt(r(n("RK"), 4, 24), r(n("NF1")), r(n("C0K")), AL.add)
-        for a in range(4):
-            red(r(n("RM"), a, a + 1), r(n("RK"), a, 24, 4), AL.min)
-        ts(r(n("RI")), r(n("RM")), 524288.0, None, AL.mult)
-        ts(r(n("RI")), r(n("RI")), 8191, None, AL.bitwise_and)
-        cp(r(n("RU")), r(n("RI")))
         out = r("OUT%d%d" % (t, h))
-        act(out, ind(r("X", 64 * h, 64 * h + 4160), r(n("RU"))), AF.Copy)
-        land = r("Z%d%d" % (t + 1, h))
+        cp(out, ind(r("W"), r("RV", 4 * h, 4 * h + 4)))
+        land = landing(t, h)
         sid = add("G", [("send", (None, out, t, h), {})], 1200)
         add("N", [("recv", (land,), {})], 0, lat=CFG["net"], sem="a%d%d" % (t, h), after=sid)
-        if t < RO - 1:
-            ts(r("RL", 4 * h, 4 * h + 4), r(n("RM")), NONE * RS, None, AL.is_lt)
-        else:
+        if t == RO - 1:
             dma("Y", "zo%d" % h, r("zo", 64 * h, 64 * h + 64), land, 16384)
 
     def renew(t, h):
@@ -493,58 +522,73 @@ def build():
         nx = 2048 * (1 - par)
         for q in range(2):
             dst = r(n("SB"), nx + 512 * q, nx + 512 * q + 512)
-            act(dst, ind(win, r(n("LRU"), 32 * q, 32 * q + 32)), AF.Copy)
+            pick(CFG["ren"][2 * h + q], dst, ind(win, r("LRU", 64 * h + 32 * q, 64 * h + 32 * q + 32)))
             if t == RO - 1:
                 dma("Y", "so%d%d" % (h, q), r("so", 1024 * h + 512 * q, 1024 * h + 512 * q + 512), dst, 131072)
-        ts(r(n("MI")), r(n("OFI")), 5 if QUART else 6, 31, AL.arith_shift_right, AL.bitwise_and)
-        cp(r(n("MU")), r(n("MI")))
-        for q in range(2):
-            act(r(n("KG"), 320 * q, 320 * q + 320), ind(r("KW", 32 * q, 32 * q + 32), r(n("MU"))), AF.Copy)
-        pk = r(n("QX"), 0, 20)
-        mm([(pk, sel("ZM", b), r(n("KG"), 320 * q + b, 320 * q + 320, 16)) for q in range(2) for b in range(16)])
-        tt(r(n("XE")), pk, r(n("UF")), AL.mult)
-        tt(r(n("EI")), r(n("XE")), r(n("Y")), AL.add)
-        ts(r(n("EI")), r(n("EI")), 1, 4095, AL.arith_shift_right, AL.bitwise_and)
-        tt(r(n("DE")), r(n("C0F")), r(n("EI")), AL.subtract)
-        tt(r(n("DE")), r(n("DE")), r(n("NF1")), AL.mult)
-        tt(r(n("E"), 4, 24), r(n("DE")), r(n("EI")), AL.add)
-        cp(r(n("EU")), r(n("E")))
-        tt(r(n("EM")), ind(r("IOTA"), r(n("EU"))), r(n("MASK")), AL.mult)
-        pm = r(n("QX"), 64, 128)
-        mm([(pm, SH, r(n("MK"), 0, 64)), (pm, ID, r(n("MK"), 64, 128))] + [(pm, ID, r(n("EM"), 64 * d, 64 * d + 64)) for d in range(6)])
+
+    def elected(t, a, b, bank):
+        c = lambda x: r(x, a, b)
+        tt(c("MU"), c("OU"), c("BASE"), AL.subtract)
+        pick(CFG["kg"], r("KG", 16 * a, 16 * b), ind(r("KW"), c("MU")))
+        pk = r(bank, 128, 128 + b - a)
+        mm16(pk, "Z15", "KG", 16 * a, 16 * b)
+        tt(c("DE"), c("DE"), c("NF"), AL.mult)
+        tt(c("YI"), c("YI"), c("DE"), AL.add)
+        tt(c("KU"), pk, c("UI"), AL.mult)
+        tt(c("EI"), c("KU"), c("YI"), AL.add)
+        ts(c("EI"), c("EI"), 4095, None, AL.bitwise_and)
+        cp(r("EU", a + 8, b + 8), c("EI"))
+        lo = 0 if a == 0 else a + 8
+        tt(r("EM", 16 * lo, 16 * b + 128), ind(r("IOTA"), r("EU", lo, b + 8)), r("MASK", 16 * lo, 16 * b + 128), AL.mult)
+        pm = r("QK00", 256, 384)
+        more = [(pm, SH1, r("MK", 0, 128)), (pm, ID, r("MK", 128, 256))] if a == 0 else []
+        mm(more + [(pm, ID, r("EM", 16 * d, 16 * d + 128)) for d in range(lo, b + 8, 8)], start=a == 0, stop=a > 0, grp=(t, "pm"))
+        if a == 0:
+            return
         if t < RO - 1:
-            cp(r(n("M")), pm)
+            cp(r("M"), pm)
         else:
-            act(r(n("MO")), pm, AF.Identity, bias=r("C2K"))
-            dma("Y", "mo%d" % h, r("mo", 64 * h, 64 * h + 64), r(n("MO")), 32768)
+            act(r("MO"), pm, AF.Identity, bias=r("C2K"))
+            dma("Y", "mo", r("mo"), r("MO"), 65536)
 
     def count():
-        pa = r("QU1", 32, 40)
-        mm([(pa, r("ONES"), r("RL"))])
-        red(r("AC"), pa, AL.add)
-        cp(r("AI"), r("AC"))
+        tt(r("RK", 32, 40), r("NF", 32, 40), r("C0K", 32, 40), AL.add)
+        tt(r("RM"), r("RK", 32, 40), r("PQ", 0, 8), AL.min)
+        ts(r("RL"), r("RM"), NONE * RS, None, AL.is_lt)
+        pa = r("QK11", 480, 481)
+        mm([(pa, r("ONES"), r("RL", k, k + 1)) for k in range(8)])
+        cp(r("AI"), pa)
         ts(r("AI"), r("AI"), 63, None, AL.bitwise_and)
-        ts(r("AF"), r("AI"), 2.0, None, AL.mult)
-        ts(r("CJ"), r("K0J"), r("AF"), None, AL.add)
+        cp(r("AF"), r("AI"))
 
     for t in range(RO):
+        offsets()
         store(t, 0)
         store(t, 1)
         gap(t, 0)
         gap(t, 1)
         for j in range(1, NJ + 1):
-            if QUART:
-                for h, q in CFG["ord4"]:
-                    corr4(t, h, q, j)
-            else:
-                corr(t, 0, j)
-                corr(t, 1, j)
-        release(t, 0)
-        release(t, 1)
+            for h, tb in STREAMS:
+                end = (h, tb) == STREAMS[-1]
+                hook = None
+                if (h, tb, j) == (1, 0, 1):
+                    hook = lambda kb, t=t: masks(t, kb if A == 2 else "QK11")
+                if end and j == 2:
+                    hook = lambda kb, t=t: names(t, kb)
+                if (h, tb, j) == (1, 0, NJ):
+                    hook = lambda kb, t=t: squares(t, kb)
+                corr(t, h, tb, j, hook)
+                if end and j == NJ - 1:
+                    prepare(t)
+                if j == NJ and tb + 16 * A == 64:
+                    release(t, h)
+                    renew(t, h)
+                if (h, tb, j) == (1, 0, NJ):
+                    elected(t, 0, 32, "QK00")
+        tt(r("NF", 32, 40), r("OU", 32, 40), r("BASE", 32, 40), AL.is_equal)
         if t < RO - 1:
             count()
-        renew(t, 0)
-        renew(t, 1)
+        elected(t, 32, 40, "QK01")
     return ops
 
 
@@ -737,7 +781,7 @@ def rank_program(g, core, T, topo):
             _, src, t, h = o["calls"][0][1]
             dst = cores[(rank + 1 + t % 3) % nr]
             rid, pid, _ = topo.addr(dst)
-            g.remote_dma(T["Z%d%d" % (t + 1, h)][:], res(src), T.sem["a%d%d" % (t, h)], T.sem["sent"], pid, rid, topo.mask(core, dst))
+            g.remote_dma(res(landing(t, h)), res(src), T.sem["a%d%d" % (t, h)], T.sem["sent"], pid, rid, topo.mask(core, dst))
             sent += len(topo.engines(core, dst))
             continue
         ins = None

@@ -1,10 +1,14 @@
+import math
+import numpy as np
 from concourse.mybir import dt, AluOpType, AxisListType, ActivationFunctionType
 
 AL = AluOpType
 AF = ActivationFunctionType
 RO, NJ = 3, 5
-CFG = {"gather": 1.4, "pe": 0.42, "ls": 220, "lx": 220, "net": 2600, "passes": 3, "mmsplit": 8, "wl": 1.0, "fe": 0.83, "mn": 53, "sfix": 0,
-       "A": 2, "rep": 4, "pieces": [(0, 8), (8, 16)], "sh": "V", "cev": "V", "cod": "S", "st": 0, "ren": "SSSS", "w": "S", "kg": "S", "xc": "S", "vp": {}}
+CFG = {"gather": 1.4, "pe": 0.42, "ls": 240, "lx": 240, "net": 2600, "passes": 3, "mmsplit": 4, "wl": 1.0, "fe": 0.83, "mn": 53, "sfix": 0,
+       "A": 2, "rep": 2, "pieces": [(0, 16)], "sh": "V", "cev": "V", "cod": "S", "st": 0, "ren": "SSSS", "renl": "SSSS", "w": "S", "kg": "SS", "xc": "S", "vp": {},
+       "cases": [(1.0, 1.3, 180, 1.0), (1.2, 1.75, 200, 1.2), (1.2, 1.75, 200, 1.2), (1.2, 0.9, 260, 1.2), (1.1, 1.5, 320, 1.1), (1.1, 1.15, 200, 1.45)], "inner": 2, "iters": 700, "seed": 7, "sig": 300, "rsp": True,
+       "pre": True, "ct": "SSSS", "sn": False, "bit": False, "fine": {(3, 5): (8, [(0, 8), (8, 12), (12, 16)])}, "one": False, "g6": False, "mg": 1, "r1": 1, "pka": False, "views": [(1.3, 220), (1.45, 240), (1.6, 220)], "local": 800, "wmin": 150, "wmax": 600, "sigl": 500, "turns": 1, "hold": None, "hold2": None, "kga": True, "pk": False, "md": True, "half": True, "out": "V", "hr": "V", "ce1": "V", "byphase": 0.3, "sigp": 1500, "pp": 0.3, "sb0": "S", "pad": 1500, "rrv": 4}
 A = CFG["A"]
 STREAMS = [(h, tb) for h in range(2) for tb in range(0, 64, 16 * A)]
 T1 = 6144
@@ -28,10 +32,10 @@ def alloc(name, pool, n):
 
 own("X", "sbuf", [128, 8320], "bfloat16")
 own("TBL", "sbuf", [128, T1 + 4104], "float32")
-own("IOTA", "sbuf", [128, 4096], "float32")
+own("ZR", "sbuf", [128, 2048], "bfloat16")
 own("CC", "sbuf", [128, NJ * 256], "float32")
 own("CT", "sbuf", [128, 1024], "float16")
-own("RR", "sbuf", [128, 1280], "float16")
+own("RR", "sbuf", [128, 256], "float16")
 own("NMI", "sbuf", [128, 128], "int32")
 own("WTI", "sbuf", [128, 1], "int32")
 own("KPI", "sbuf", [128, 2], "int32")
@@ -40,29 +44,33 @@ for _h in range(2):
     own("G%d" % _h, "sbuf", [128, 2048], "bfloat16")
     own("MX%d" % _h, "sbuf", [128, 2048], "bfloat16")
     for _t in range(RO + 1):
-        own("Z%d%d" % (_t, _h), "sbuf", [128, 64], "bfloat16")
+        own("Z%d%d" % (_t, _h), "sbuf", [128, 68 if CFG["sn"] and 0 < _t < RO else 64], "bfloat16")
     for _t in range(RO):
-        own("OUT%d%d" % (_t, _h), "sbuf", [128, 64], "bfloat16")
+        own("OUT%d%d" % (_t, _h), "sbuf", [128, 68 if CFG["sn"] and _t < RO - 1 else 64], "bfloat16")
     for _n in ("QK", "QR"):
         for _q in range(2):
             own("%s%d%d" % (_n, _h, _q), "psum", [128, 512], "float32")
 own("MO", "sbuf", [128, 128], "float32")
-for _n, _w in (("QQ", 16), ("S1", 256), ("S2", 256), ("S3", 256), ("KM", 8), ("HO", 8), ("T", 128), ("C0F", 40), ("C0K", 40), ("C0S", 40), ("RK", 40), ("M1", 16), ("M3", 8),
+own("CM", "sbuf", [128, 40, 16], "float16")
+LAY["CM"] = ("CM", 0, 640)
+for _n in ("S1", "S2", "S3", "S4"):
+    alloc(_n, "PF", 264)
+for _n, _w in (("QQ", 16), ("D4", 264), ("KM", 8), ("HO", 8), ("T", 128), ("C0F", 40), ("C0K", 40), ("C0S", 40), ("RK", 40), ("M1", 16), ("M3", 8),
                ("NP", 8), ("NK", 8), ("PQ", 16), ("RM", 8), ("NF", 40), ("KU", 40), ("YI", 40), ("DE", 40), ("NC", 8), ("D15", 128), ("SH", 128),
                ("XI", 144), ("XH", 144), ("BX", 128), ("DX", 16), ("DJ", 40), ("DA", 40), ("RA", 128), ("NN", 256), ("NQ", 256), ("G15", 1), ("G7", 1), ("B", 1), ("P1", 1), ("WF", 1),
                ("K15", 1), ("K1", 1), ("M2", 1), ("BA", 1), ("E0", 1), ("E13", 1), ("E2", 1), ("ES", 4), ("S16", 1), ("K2K", 1), ("LT", 16), ("INR", 16), ("TT", 16), ("TB", 32),
                ("I16", 128), ("KF", 2), ("KM16", 2), ("KW", 32), ("W1K", 1), ("NB", 16), ("K0J", 40), ("AF", 1), ("OF", 5), ("OF0", 5), ("C2K", 1), ("CSH", 1), ("B19", 1),
-               ("BM19", 1), ("CK", 8), ("HB", 4), ("BASE", 40), ("D1", 128), ("D3", 256), ("ZERO", 128), ("DG", 64)):
+               ("C1K", 1), ("B16", 1), ("CKB", 1), ("KB", 1), ("CZH", 1), ("CZ2", 1), ("CK", 8), ("HB", 4), ("B15", 16), ("BASE", 40), ("D1", 64), ("D3", 256), ("ZERO", 128), ("DG", 64)):
     alloc(_n, "PF", _w)
 for _n, _w in (("ZI", 8), ("RI", 16), ("UI", 40), ("SQ", 40), ("EI", 40), ("OI", 40),
                ("PP", 1), ("PT", 1), ("PT2", 1), ("PT3", 1), ("PT4", 1), ("PT5", 1), ("PT6", 1), ("K16", 2), ("BI", 16), ("NI", 256), ("AI", 1)):
     alloc(_n, "PI", _w)
-for _n, _w in (("NU", 256), ("UL", 16), ("OU", 40), ("NL", 8), ("HU", 8), ("HV", 8), ("LRU", 128), ("O15", 8), ("RU", 16), ("RV", 8), ("C5", 8), ("MU", 40), ("EU", 48)):
+for _n, _w in (("NU", 256), ("UL", 16), ("OU", 40), ("NL", 8), ("HU", 8), ("HV", 8), ("LRU", 128), ("O15", 8), ("RU", 16), ("RV", 8), ("C5", 8), ("MU", 40)):
     alloc(_n, "PU", _w)
-for _n, _w in (("M", 128), ("CM", 640), ("LRH", 128), ("EM", 768), ("MK", 256), ("SP", 768), ("SS", 128), ("KG", 640), ("KR", 32), ("CF", 156), ("R1", 256), ("R2", 256)):
+for _n, _w in (("CG", 64), ("EH", 48), ("M", 128), ("CM1", 128), ("LRH", 128), ("EM", 768), ("MK", 256), ("SP", 768), ("SS", 128), ("KG", 640), ("KR", 32), ("CF", 156), ("R1", 256), ("R2", 256)):
     alloc(_n, "PH", _w)
 for _n, _w in (("MASK", 768), ("XC", 128), ("W", 256), ("HR", 128), ("ZA", 144), ("ZM", 144), ("Z15", 144), ("ZW1", 144), ("ZW2", 144), ("IDW", 130), ("NID", 128), ("IDH", 128),
-               ("ONES", 128), ("BO", 128), ("TAB", 48), ("RAMP", 128), ("WM4", 1), ("RL", 8)):
+               ("NIH", 128), ("ZK", 144), ("ZX", 144), ("LG", 256), ("CN", 256), ("ONES", 128), ("BO", 128), ("TAB", 48), ("RAMP", 64), ("WM4", 1), ("RL", 8)):
     alloc(_n, "PB", _w)
 for _k in POOL:
     SCRATCH[_k] = ("sbuf", [128, (USED[_k] + 15) // 16 * 16], POOL[_k])
@@ -83,6 +91,16 @@ def r(name, a=0, b=None, s=1):
     return ("@", buf, mask, idx, cnt)
 
 
+def cmr(a, b, s=1):
+    x = r("CM", a, b, s)
+    return x[:3] + (((slice(None), slice(a // 16, b // 16), slice(None)) if s == 1 else (slice(None), slice(None), a)), x[4])
+
+
+def cm4(j, q0, q1, a):
+    mask = sum(r("CM", 128 * j + 32 * q + 16 * a, 128 * j + 32 * q + 16 * a + 16)[2] for q in range(q0, q1))
+    return ("@", "CM", mask, (slice(None), slice(8 * j + 2 * q0 + a, 8 * j + 2 * q1, 2), slice(None)), 16 * (q1 - q0))
+
+
 def ind(win, off):
     return ("#", win, off)
 
@@ -98,7 +116,10 @@ def landing(t, h):
 def build():
     ops = []
     gc_ = CFG["gather"]
-    lastd = {}
+    lastd = {"phase": 0}
+
+    def step():
+        lastd["phase"] += 1
 
     def add(eng, calls, busy, lat=0, sem=None, grp=None, after=None):
         rd, wr = [], []
@@ -114,7 +135,8 @@ def build():
             for x in c[2].values():
                 if is_acc(x):
                     rd.append(x)
-        ops.append({"eng": eng, "calls": calls, "busy": busy, "lat": lat, "sem": sem, "grp": grp, "rd": rd, "wr": wr, "after": after})
+        ge = sum(16 * x[2][4] for c in calls for x in c[1][1:2] if is_acc(x) and x[0] == "#")
+        ops.append({"phase": lastd["phase"], "ge": ge, "eng": eng, "calls": calls, "busy": busy, "lat": lat, "sem": sem, "grp": grp, "rd": rd, "wr": wr, "after": after})
         return len(ops) - 1
 
     def short(x):
@@ -207,35 +229,46 @@ def build():
     dma("S", "rec0", r("X", 0, 4096), r("rec"), 2000000)
     dma("Y", "rec1", r("X", 4096, 8192), r("rec"), 2700000)
     iota(r("PP"), [[1, 1]], 0, 1, False)
+    iota(r("NN"), [[-1, 256]], 255, 0)
     iota(r("XI"), [[1, 144]], 0, 0)
     iota(r("BX"), [[16, 8], [0, 16]], 15, 0)
-    iota(r("NN"), [[-1, 256]], 255, 0)
     iota(r("NB"), [[-1, 16]], 16391, 0)
     iota(r("XH"), [[1, 72], [0, 2]], 0, 0)
+    iota(r("B19"), [[0, 1]], 524288, 0)
+    iota(r("AF"), [[0, 1]], 0, 0)
+    iota(r("C1K"), [[0, 1]], 1024, 0)
     iota(r("DJ"), [[1, 5], [0, 8]], 1, 0)
-    iota(r("DG"), [[0, 64]], -1, 0)
+    iota(r("DG"), [[1, 16], [256, 4]], 0, 0) if CFG["g6"] else iota(r("DG"), [[0, 64]], -1, 0)
     iota(r("ZERO"), [[0, 128]], 0, 0)
     iota(r("DA"), [[0, 40 // A], [32, A]], 0, 0)
-    iota(r("RA"), [[1, 4], [0, 32]], 0, 0)
-    iota(r("D1", 0, 32 * A), [[0, 32 * A]], -1, 0)
+    iota(r("D1"), [[0, 64]], -1, 0)
+    iota(r("RAMP", 0, 32), [[0, 32]], 0, 0)
+    iota(r("RAMP", 32, 64), [[0, 32]], -8388608, 0)
+    iota(r("CN"), [[0, 256]], -1024, 0)
     iota(r("SB0", 1024, 2048), [[0, 1024]], 0, 0)
     iota(r("SB1", 1024, 2048), [[0, 1024]], 0, 0)
     iota(r("TBL", 4097, T1), [[0, T1 - 4097]], 0, 0)
     iota(r("I16"), [[0, 2], [16, 64]], 0, 0)
+    iota(r("C2K"), [[0, 1]], 2048, 0)
     iota(r("D3"), [[0, 256]], 0, 0)
+    iota(r("D3", 0, 256, 32), [[0, 8]], -128, 0)
+    if CFG["sn"]:
+        iota(r("D4"), [[0, 256]], 0, 0)
     iota(r("ONES"), [[0, 128]], 1, 0)
-    iota(r("IOTA"), [[1, 4096]], -2048, 0)
+    iota(r("ZR"), [[0, 2048]], 1, 0)
+    lastd["G"] = add("G", [("asel", (r("ZR"), r("ZR"), [[-1, 16], [-16, 8], [0, 16]], AL.is_equal, 0.0, 0, 1), {})], 170 + 1.66 * 2048, after=lastd["G"])
     ts(r("PT"), r("PP"), 112, None, AL.bitwise_and)
     ts(r("G15"), r("PT"), 15.0, None, AL.add)
     ts(r("G7"), r("PT"), 0.5, 7.0, AL.mult, AL.add)
+    ts(r("CF", 71, 128, 8), r("XI", 0, 8), 0.0, 2048.0, AL.mult, AL.add)
     ts(r("PT2"), r("PP"), 15, None, AL.bitwise_and)
     cp(r("B"), r("PT2"))
-    ts(r("BA"), r("PT2"), 32.0 * A, None, AL.mult)
+    act(r("BA"), r("B"), AF.Copy, scale=32.0 * A)
     ts(r("P1"), r("PP"), 1.0, None, AL.add)
     ts(r("K15"), r("PT2"), 15.0, None, AL.is_equal)
     ts(r("K1"), r("PT2"), 1.0, None, AL.is_ge)
-    ts(r("S16"), r("PT2"), 1.0, 16.0, AL.is_ge, AL.mult)
-    ts(r("K2K"), r("PT2"), 1.0, 2048.0, AL.is_ge, AL.mult)
+    act(r("S16"), r("K1"), AF.Copy, scale=16.0)
+    act(r("K2K"), r("K1"), AF.Copy, scale=2048.0)
     ts(r("PT3"), r("PP"), 1, None, AL.bitwise_and)
     ts(r("M2"), r("PT3"), -float(T1), 2.0 ** 35 - 2048.0, AL.mult, AL.add)
     cp(r("WF"), r("WTI"))
@@ -244,34 +277,37 @@ def build():
     act(r("NID"), ID, AF.Copy, scale=-1.0)
     act(r("IDH"), ID, AF.Copy, scale=0.5)
     ts(r("ZM"), r("XI"), r("G15"), 1024.0, AL.is_equal, AL.mult)
-    act(r("ZA"), r("ZM"), AF.Copy, scale=-0.5)
+    act(r("ZA"), r("ZM"), AF.Copy, scale=-2.0)
+    act(r("ZX"), r("ZM"), AF.Copy, scale=4.0)
     ts(r("Z15"), r("XI"), r("G15"), r("K15"), AL.is_equal, AL.mult)
     ts(r("ZW1"), r("XI"), r("G15"), r("WF"), AL.is_equal, AL.mult)
     ts(r("ZW2"), r("XH"), r("G7"), r("WF"), AL.is_equal, AL.mult)
     ts(r("BO"), r("BX"), r("G15"), None, AL.is_equal)
-    act(r("RAMP"), r("RA"), AF.Copy, scale=-4194304.0)
-    ms(r("CSH"), 511.75)
-    ms(r("C2K"), 2048.0)
-    ms(r("B19"), 524288.0)
-    ms(r("AF"), 0.0)
-    ts(r("CK"), r("XI", 0, 8), 16.0, r("B"), AL.mult, AL.add)
-    ts(r("HB"), r("CK", 0, 4), 16.0, None, AL.mult)
-    ts(r("BASE"), r("DA"), r("BA"), None, AL.add)
-    ts(r("D1", 31, 32 * A, 32), r("BASE", 0, A), 31.0, None, AL.add)
-    ms(r("D3", 0, 256, 32), -128.0)
-    ts(r("D3", 31, 256, 32), r("CK"), 128.0, None, AL.add)
-    ts(r("DG", 15, 64, 16), r("HB"), 15.0, None, AL.add)
+    act(r("CSH"), r("C1K"), AF.Copy, scale=511.75 / 1024)
+    act(r("CZH"), r("C1K"), AF.Copy, scale=1023.75 / 1024)
+    act(r("CZ2"), r("C1K"), AF.Copy, scale=2047.5 / 1024)
+    act(r("NIH"), ID, AF.Copy, scale=-0.5)
+    lin("S", r("CK"), r("XI", 0, 8), 16.0, r("B"))
+    act(r("HB"), r("CK", 0, 4), AF.Copy, scale=16.0)
+    lin("S", r("BASE"), r("DA"), 1.0, r("BA"))
+    lin("S", r("D1", 31, 64, 32), r("BASE", 0, A), 1.0, r("XI", 31, 32))
+    lin("S", r("D3", 31, 256, 32), r("CK"), 1.0, r("XI", 128, 129))
+    if CFG["g6"]:
+        act(r("B16"), r("B"), AF.Copy, scale=16.0)
+        lin("S", r("CG"), r("DG"), 1.0, r("B16"))
+    else:
+        lin("S", r("DG", 15, 64, 16), r("HB"), 1.0, r("XI", 15, 16))
     ts(r("TAB", 0, 16), HX, 1.0, r("B"), AL.add, AL.is_equal)
-    ts(r("TAB", 16, 32), HX, r("B"), r("K1"), AL.is_ge, AL.mult)
     ts(r("TAB", 32, 48), HX, 5.0, r("B"), AL.add, AL.is_lt)
     ts(r("LT"), HX, r("B"), None, AL.is_gt)
     tt(r("INR"), r("LT"), r("TAB", 32, 48), AL.add)
-    ts(r("INR"), r("INR"), -1.0, 1.0, AL.mult, AL.add)
-    for par in range(2):
-        ts(r("TT"), HX, -1.0, 1024.0 if par == 0 else -1024.0, AL.mult, AL.add)
-        tt(r("TT"), r("TT"), r("INR"), AL.mult)
-        tt(r("TT"), r("TT"), r("LT"), AL.add)
-        ts(r("TB", 16 * par, 16 * par + 16), r("TT"), r("B"), 1024.0 * par, AL.add, AL.add)
+    lin("S", r("INR"), r("INR"), -1.0, r("XI", 1, 2))
+    lin("S", r("TT"), HX, -1.0, r("C1K"))
+    tt(r("TT"), r("TT"), r("INR"), AL.mult)
+    lin("S", r("LT"), r("LT"), 1.0, r("B"))
+    tt(r("TB", 0, 16), r("TT"), r("LT"), AL.add)
+    lin("S", r("INR"), r("INR"), -2048.0, r("C1K"))
+    tt(r("TB", 16, 32), r("TB", 0, 16), r("INR"), AL.add)
     cp(r("KF"), r("KPI"))
     for q in range(2):
         ts(r("KR", 16 * q, 16 * q + 16), HX, r("B"), r("KF", q, q + 1), AL.is_equal, AL.mult)
@@ -291,32 +327,34 @@ def build():
     for q in range(2):
         ts(r("CF", 64 * q, 64 * q + 64, 4), r("BI"), r("S16") if q == 0 else 16.0, r("KF", q, q + 1), AL.mult, AL.add)
         ts(r("CF", 64 * q + 1, 64 * q + 64, 4), r("BI"), r("KM16", q, q + 1), None, AL.mult)
-        ts(r("CF", 64 * q + 2, 64 * q + 64, 4), HX, 0.0, r("K1") if q == 0 else 1.0, AL.mult, AL.add)
-        ts(r("CF", 64 * q + 7, 64 * q + 64, 8), r("XI", 0, 8), 0.0, r("K2K") if q == 0 else 2048.0, AL.mult, AL.add)
-    ts(r("CF", 3, 128, 8), HX, 0.0, None, AL.mult)
-    ts(r("CF", 128, 156), r("XI", 0, 28), 0.0, None, AL.mult)
+    lin("S", r("CF", 2, 64, 4), HX, 0.0, r("K1"))
+    lin("S", r("CF", 66, 128, 4), HX, 0.0, r("XI", 1, 2))
+    lin("S", r("CF", 7, 64, 8), r("XI", 0, 8), 0.0, r("K2K"))
+    act(r("CF", 3, 128, 8), HX, AF.Copy, scale=0.0)
+    act(r("CF", 128, 156), r("XI", 0, 28), AF.Copy, scale=0.0)
     ts(r("PT4"), r("PP"), 31, None, AL.bitwise_and)
     ts(r("PT5"), r("PP"), 29, None, AL.bitwise_and)
-    ts(r("PT6"), r("PP"), 5, None, AL.arith_shift_right)
     ts(r("E0"), r("PT4"), 0.0, None, AL.is_equal)
-    ts(r("E2"), r("PT4"), 2.0, None, AL.is_equal)
+    ts(r("E2"), r("PT4"), 2.0, 1.0 / 32, AL.is_equal, AL.mult)
     ts(r("E13"), r("PT5"), 1.0, None, AL.is_equal)
-    cp(r("BM19"), r("PT6"))
-    ts(r("ES"), r("XI", 0, 4), r("BM19"), None, AL.is_equal)
     act(r("NQ"), r("NN"), AF.Square)
-    ts(r("NI"), r("NQ"), 1.0 / 32, -0.484375, AL.mult, AL.add)
+    ts(r("NI"), r("NQ"), r("E2"), -0.484375, AL.mult, AL.add)
     act(r("R1"), r("NN"), AF.Identity, scale=r("E0"), bias=r("E13"))
-    ts(r("R2"), r("NI"), r("E2"), None, AL.mult)
-    tt(r("RR", 1024, 1280), r("R1"), r("R2"), AL.add)
-    for s in range(4):
-        ts(r("RR", 256 * s, 256 * s + 256), r("RR", 1024, 1280), r("ES", s, s + 1), None, AL.mult)
+    tt(r("RR"), r("R1"), r("NI"), AL.add)
+
+    def part(x, s):
+        return x[:3] + ((slice(32 * s, 32 * s + 32), x[3][1]), x[4])
+
     for q in range(2):
-        mms([(r("QK0%d" % q, 128 * i, 128 * i + 128), r("CF", 16 * q + 4 * i, 16 * q + 4 * i + 128), ID) for i in range(4)])
-        act(r("CT", 512 * q, 512 * q + 512), r("QK0%d" % q), AF.Copy)
+        for k in range(2):
+            bank = "QK%d%d" % (q, k)
+            mms([(r(bank, 128 * i, 128 * i + 128), r("CF", 16 * q + 8 * k + 4 * i, 16 * q + 8 * k + 4 * i + 128), ID) for i in range(2)])
+            o, src = r("CT", 512 * q + 256 * k, 512 * q + 256 * k + 256), r(bank, 0, 256)
+            act(o, src, AF.Copy) if CFG["ct"][2 * q + k] == "S" else cp(o, src)
     for x in range(16):
-        bank, tmp = ("QK10", "QK11", "QK00", "QK01")[x % 4], r("G%d" % (x % 2), 512 * (x // 2 % 4), 512 * (x // 2 % 4) + 512)
+        bank, tmp = ("QK00", "QK01", "QK10", "QK11")[x % 4], r("G%d" % (x % 2), 512 * (x // 2 % 4), 512 * (x // 2 % 4) + 512)
         s, i = x // 4, 2 * x % 8
-        blocks = [(r(bank, 256 * k, 256 * k + 256), r("CT", 128 * (i + k), 128 * (i + k) + 128), r("RR", 256 * s, 256 * s + 256)) for k in range(2)]
+        blocks = [(r(bank, 256 * k, 256 * k + 256), part(r("CT", 128 * (i + k), 128 * (i + k) + 128), s), part(r("RR"), s)) for k in range(2)]
         mms(blocks)
         act(tmp, r(bank), AF.Identity, bias=r("B19"))
         o = T1 * (x // 8) + 1 + 512 * (x % 8)
@@ -331,8 +369,18 @@ def build():
     NONE = 15 * 16384 + 8192
     RS = 1.0 / 524288
     ts(r("M"), r("NMI"), -2048.0, None, AL.add)
-    ts(r("NC"), r("CK"), 32.0, None, AL.mult)
+    PM = r("QK11", 320, 448)
+    mms([(PM, ID, r("M"))])
+    act(r("NC"), r("CK"), AF.Copy, scale=32.0)
+    for h in range(2):
+        lin("S", r("B15", 4 * h, 4 * h + 4), r("HB"), 1.0, r("XI", 15, 16))
+    lin("S", r("B15", 8, 16), r("B15", 0, 8), 1.0, r("C1K"))
     ts(r("NK"), r("CK"), float(NONE + 4096), RS, AL.add, AL.mult)
+    if CFG["pk"]:
+        act(r("CKB"), r("C1K"), AF.Copy, scale=(32 * 16384 + 2048) * RS / 1024)
+        act(r("KB"), r("B19"), AF.Copy, scale=-1.0)
+        lin("S", r("KB"), r("B"), 16384.0, r("KB"))
+        act(r("ZK"), r("ZM"), AF.Copy, scale=r("KB"))
 
     def offsets():
         ts(r("OI"), r("K0J"), r("AF"), None, AL.add)
@@ -345,91 +393,134 @@ def build():
     def store(t, h):
         z = "Z%d%d" % (t, h)
         four = lambda x: r(x, 4 * h, 4 * h + 4)
-        ps = r("QR%d0" % h, 0, 4)
-        mm16(ps, "ZM", z, 0, 64)
-        ts(four("ZI"), ps, 1.0 / 1024, None, AL.mult)
-        ts(four("ZI"), four("ZI"), 31, None, AL.bitwise_and)
-        tt(four("NL"), four("ZI"), four("NC"), AL.add)
-        cp(ind(r("X", 0, 4096), four("NL")), r(z))
-        cp(ind(r("X", 4096, 8192), four("NL")), r(z))
+        if t == 0 or not CFG["sn"]:
+            ps = r("QR%d0" % h, 0, 4)
+            mm16(ps, "ZM", z, 0, 64)
+            ts(four("ZI"), ps, 1.0 / 1024, None, AL.mult)
+            ts(four("ZI"), four("ZI"), 31, None, AL.bitwise_and)
+            tt(four("NL"), four("ZI"), four("NC"), AL.add)
+        else:
+            tt(four("NL"), r(z, 64, 68), four("NC"), AL.add)
+        cp(ind(r("X", 0, 4096), four("NL")), r(z, 0, 64))
+        cp(ind(r("X", 4096, 8192), four("NL")), r(z, 0, 64))
 
     def slot(h, tb, nt, d):
         return r("SB%d" % h, 1024 + 16 * tb + d, 1024 + 16 * (tb + nt), 16)
 
-    def after_mid(h, tb, nt, d):
+    def halved(t):
+        return CFG["half"] and t > 0
+
+    def after_mid(t, h, tb, nt, d):
         o = 64 * h + tb
         sp = r("SP", 128 * d + o, 128 * d + o + nt)
-        ts(slot(h, tb, nt, d), sp, -1024.0, None, AL.add)
-        if d < NJ:
-            lin(CFG["sh"], r("SH", o, o + nt), sp, 0.5, r("CSH"))
+        if tb + nt == 64:
+            c = 0.5 if halved(t) else 1.0
+            lastd["slot"] = ts(slot(h, 0, 64, d), r("SP", 128 * d + 64 * h, 128 * d + 64 * h + 64), -1024.0, c, AL.add, AL.mult)
+            if d < NJ:
+                lin(CFG["sh"] if d else CFG["sb0"], r("SH", 64 * h, 64 * h + 64), r("SP", 128 * d + 64 * h, 128 * d + 64 * h + 64), 0.5, r("CSH"))
 
     def lanes(bank, j, t0, t1):
         w = t1 - t0
-        return [(r(bank[0], bank[1] + tb + a, bank[1] + tb + 16 * A, A), sel("ZM", 0), r("CM", 128 * j + t0 + tb + 16 * a, 128 * j + t0 + tb + 16 * a + 16))
+        if j:
+            return [(r(bank[0], bank[1] + a, bank[1] + w, 2), sel("ZM", 0), cm4(j, t0 // 32, t1 // 32, a)) for a in range(2)]
+        return [(r(bank[0], bank[1] + tb + a, bank[1] + tb + 16 * A, A), sel("ZM", 0), r("CM1", t0 + tb + 16 * a, t0 + tb + 16 * a + 16))
                 for tb in range(0, w, 16 * A) for a in range(A)]
 
     def even(bank, j, t0, t1):
-        lin(CFG["cev"], r("CC", 256 * j + 2 * t0, 256 * j + 2 * t1, 2), r(bank[0], bank[1], bank[1] + t1 - t0), 1.0 / 1024, r("OF0", j, j + 1))
+        lin(CFG["cev"] if j else CFG["ce1"], r("CC", 256 * j + 2 * t0, 256 * j + 2 * t1, 2), r(bank[0], bank[1], bank[1] + t1 - t0), 1.0 / 1024, r("OF0", j, j + 1))
 
     def gap(t, h):
         n = lambda x: x + str(h)
         four = lambda x: r(x, 4 * h, 4 * h + 4)
         half = lambda x, o=0: r(x, o + 64 * h, o + 64 * h + 64)
-        z = r("Z%d%d" % (t, h))
+        z = r("Z%d%d" % (t, h), 0, 64)
         so = 2048 * (t % 2)
+        if halved(t):
+            lin("S", half("T"), z, 0.5, r("CZH"))
         for q in (1, 0):
             bank = n("QR") + str(q)
-            for k2 in range(2):
-                calls = []
-                for k in range(8 * q + 4 * k2, 8 * q + 4 * k2 + 4):
-                    o = r(bank, 64 * (k % 8), 64 * (k % 8) + 64)
-                    calls.append(("mm", (o, ID, r(n("SB"), so + k, so + 1024, 16), True, False), {}))
-                    calls.append(("mm", (o, NID, z, False, True), {}))
-                add("P", calls, 8 * 64 * CFG["pe"] + 5, lat=40)
-            act(r(n("MX"), 512 * q, 512 * q + 512), r(bank), AF.Abs)
+            rows = [(r(bank, 64 * k, 64 * k + 64), ID, r(n("SB"), so + 8 * q + k, so + 1024, 16)) for k in range(8)]
+            less = [(r(bank, 64 * k, 64 * k + 64), r("NIH") if halved(t) else NID, z) for k in range(8)]
+            if CFG["pre"]:
+                mm(less + rows if h == 0 else rows + less)
+            else:
+                for k2 in (0, 4):
+                    add("P", [("mm", x[k] + (x is rows, x is less), {}) for k in range(k2, k2 + 4) for x in (rows, less)], 8 * 64 * CFG["pe"] + 5, lat=40)
+            if q == 0:
+                ops[-1]["after"] = lastd["diff"]
+            lastd["diff"] = len(ops) - 1
+            k = act(r(n("MX"), 512 * q, 512 * q + 512), r(bank), AF.Abs, scale=2.0 if halved(t) else 1.0)
+            if q == 0:
+                ops[k]["after"] = lastd["abs"]
+            lastd["abs"] = k
         kb = n("QR") + "1"
-        mm16(r(kb, 0, 64), "ZM", n("MX"), 0, 1024)
         o = 128 * h
-        for a in range(4):
+        if CFG["g6"]:
+            mm([(r(kb, 0, 64), ID, r("CG"))] + [(r(kb, 0, 64), sel("ZX", q), r(n("MX"), q, 1024, 16)) for q in range(16)])
+            for a in range(4):
+                red(r("KM", 4 * h + a, 4 * h + a + 1), r(kb, a, 64, 4), AL.min)
+            ts(four("HO"), four("KM"), 1.5 * 2.0 ** 35, 1.5 * 2.0 ** 35, AL.add, AL.subtract)
+            tt(four("HV"), four("KM"), four("HO"), AL.subtract)
+        else:
+            mm16(r(kb, 0, 64), "ZM", n("MX"), 0, 1024)
+        for a in range(0 if CFG["g6"] else 4):
             scan(r("S1", o + 16 * a, o + 16 * a + 16), r(kb, a, 64, 4), r("DG", 16 * a, 16 * a + 16))
-            red(r("KM", 4 * h + a, 4 * h + a + 1), r(kb, a, 64, 4), AL.min)
-        tt(four("HV"), r("S1", o + 15, o + 64, 16), four("KM"), AL.subtract)
-        tt(half("T"), ind(r(n("SB"), so, so + 1024), four("HV")), z, AL.add)
-        ts(half("SP"), half("T"), 0.5, 1023.75, AL.mult, AL.add)
-        after_mid(h, 0, 64, 0)
+            if not CFG["bit"]:
+                red(r("KM", 4 * h + a, 4 * h + a + 1), r(kb, a, 64, 4), AL.min)
+        if not CFG["g6"]:
+            tt(four("HV"), r("S1", o + 15, o + 64, 16), four("KM"), AL.subtract)
+        if halved(t):
+            tt(half("SP"), ind(r(n("SB"), so, so + 1024), four("HV")), half("T"), AL.add)
+        else:
+            tt(half("T"), ind(r(n("SB"), so, so + 1024), four("HV")), z, AL.add)
+            ts(half("SP"), half("T"), 0.5, 1023.75, AL.mult, AL.add)
+        after_mid(t, h, 0, 64, 0)
+
+    def own_name(t, h):
+        n = lambda x: x + str(h)
+        four = lambda x: r(x, 4 * h, 4 * h + 4)
+        half = lambda x, o=0: r(x, o + 64 * h, o + 64 * h + 64)
         tt(four("HU"), four("HV"), r("HB"), AL.subtract)
-        tt(half("CM"), ind(r("TAB", 0, 16), four("HU")), half("M"), AL.mult)
+        tt(half("CM1"), ind(r("TAB", 0, 16), four("HU")), half("M"), AL.mult)
         bank = (n("QK") + "1", 0)
         mms(lanes(bank, 0, 64 * h, 64 * h + 64))
         even(bank, 0, 64 * h, 64 * h + 64)
 
     def masks(t, kb):
         hu = r("HU")
-        cp(r("HR"), ind(HX, hu))
+        pick(CFG["hr"], r("HR"), ind(HX, hu))
         for d in (2, 3, 4, 5, 0, 1):
             ts(r("MASK", 128 * d, 128 * d + 128), r("HR"), float(d), r("B"), AL.add, AL.is_equal)
         for j in range(1, NJ):
-            tt(r("CM", 128 * j, 128 * j + 128), r("MASK", 128 * j + 128, 128 * j + 256), r("M"), AL.mult)
+            tt(cmr(128 * j, 128 * j + 128), PM, r("MASK", 128 * j + 128, 128 * j + 256), AL.mult)
             mms(lanes((kb, 128 * j - 128), j, 0, 128))
+        ts(r("LG", 0, 128), r("HR"), r("B"), r("K1"), AL.is_ge, AL.mult)
+        ts(r("LG", 128, 256), r("HR"), 5.0, r("B"), AL.add, AL.is_lt)
+        for q in range(2):
+            tt(r("MK", 128 * q, 128 * q + 128), PM, r("LG", 128 * q, 128 * q + 128), AL.mult)
         for j in range(1, NJ):
             even((kb, 128 * j - 128), j, 0, 128)
         par = t % 2
-        tt(r("LRH"), ind(r("TB", 16 * par, 16 * par + 16), hu), r("I16"), AL.add)
-        cp(r("LRU"), r("LRH"))
-        tt(r("MK", 0, 128), ind(r("TAB", 16, 32), hu), r("M"), AL.mult)
-        tt(r("MK", 128, 256), ind(r("TAB", 32, 48), hu), r("M"), AL.mult)
-        cp(r("EU", 0, 8), r("NL"))
+        tt(r("LRU"), ind(r("TB", 16 * par, 16 * par + 16), hu), r("I16"), AL.add)
+        ts(r("EH", 0, 8), r("NL"), -2048.0, None, AL.add)
 
     def names(t, cb):
-        mm16(r(cb, 320, 360), "ZM", "CM", 0, 640)
-        mm16(r(cb, 360, 368), "Z15", "LRH", 0, 128)
+        cp(cmr(0, 128), r("CM1"))
+        mm([(r(cb, 320, 360), sel("ZM", q), cmr(q, 640, 16)) for q in range(16)])
+        ts(r("M1", 0, 8), r("HU"), -1.0, 1024.0 - 2048.0 * (t % 2), AL.mult, AL.add)
+        ts(r("M1", 8, 16), r("HU"), 10.0, None, AL.is_ge)
+        tt(r("M3"), r("M1", 0, 8), r("M1", 8, 16), AL.mult)
+        tt(r("O15"), r("M3"), r("B15", 8 * (t % 2), 8 * (t % 2) + 8), AL.add)
+        if CFG["pk"]:
+            mm([(r(cb, 368, 408), sel("ZM", q), cmr(q, 640, 16)) for q in range(16)] + [(r(cb, 368, 408), sel("ZK", q), r("MASK", 128 + q, 768, 16)) for q in range(16)])
+            act(r("C0K"), r(cb, 368, 408), AF.Identity, scale=RS / 1024, bias=r("CKB"))
+        else:
+            for j in range(NJ):
+                ts(r("C0S", 8 * j, 8 * j + 8), r("HU"), j + 1.125, 16384.0 * RS, AL.add, AL.mult)
+            act(r("C0K"), r(cb, 320, 360), AF.Copy, scale=RS / 1024)
+            tt(r("C0K"), r("C0K"), r("C0S"), AL.add)
         act(r("C0F"), r(cb, 320, 360), AF.Identity, scale=1.0 / 1024, bias=r("C2K"))
-        cp(r("O15"), r(cb, 360, 368))
         cp(r("C5"), r("C0F", 32, 40))
-        act(r("C0S"), r("C0F"), AF.Copy, scale=RS)
-        for j in range(NJ):
-            ts(r("C0K", 8 * j, 8 * j + 8), r("HU"), j + 1.0, 16384.0 * RS, AL.add, AL.mult)
-        tt(r("C0K"), r("C0K"), r("C0S"), AL.add)
         tt(r("NP"), r("NK"), r("C0K", 32, 40), AL.min)
         pick(CFG["xc"], r("XC"), ind(XS, r("C5")), 0.5)
 
@@ -437,55 +528,77 @@ def build():
 
     def corr(t, h, tb, j, hook):
         n = lambda x: x + str(h)
-        kb, rb = "QK%d%d" % (h, tb // 32), "QR%d%d" % (h, tb // 32)
+        kb, rb = "QK%d%d" % (h, tb // 32), "QR0%d" % (tb // 32 if A == 2 else h)
         nt, bn, rep = 16 * A, 8 // A, CFG["rep"]
         o = 64 * h + tb
+        gp, pieces = CFG["vp"].get(o // 32, [p + ("S",) for p in CFG["pieces"]]), CFG.get("mp") or CFG["pieces"]
+        if (o // 32, j) in CFG["fine"]:
+            rep, pieces = CFG["fine"][(o // 32, j)][:2]
+            gp = [p + ("S",) for p in pieces] if len(CFG["fine"][(o // 32, j)]) == 2 else CFG["fine"][(o // 32, j)][2]
         sv, u0, g0, c0 = 128 * (j - 1) + o, o // 8, 32 * tb, 8 * (j - 1) + o // 16
+        step()
         pu = r(kb, 448, 448 + 2 * A)
         mm([(pu, r("ZW2", 14 - 2 * i, 142 - 2 * i), r("SP", sv + 16 * (i % A) + i // A, sv + 16 * (i % A) + 16, bn)) for i in range(8)])
-        mms([(r(rb, rep * a + i, rep * nt, rep * A), IDH, slot(h, tb + 16 * a, 16, j - 1)) for a in range(A) for i in range(rep)])
+        mm([(r(rb, 0, rep * nt), IDH, r("CN", 0, rep * nt))]
+           + [(r(rb, rep * a + i, rep * nt, rep * A), IDH, r("SP", sv + 16 * a, sv + 16 * a + 16)) for a in range(A) for i in range(rep)])
         qq, ul = r("QQ", u0, u0 + 2 * A), r("UL", u0, u0 + 2 * A)
         ts(qq, pu, 2.0 ** 35, r("M2"), AL.add, AL.subtract)
         tt(ul, qq, pu, AL.subtract)
         cc = 256 * (j - 1) + 2 * o
         tt(r("NU", 2 * o, 2 * o + 2 * nt), ind(TW, ul), r("CC", cc, cc + 2 * nt), AL.add)
         if hook:
+            step()
             hook(kb)
-        key = r(kb, 0, 32 * A)
+        step()
+        key = r(kb, 0, 64)
         gid = (t, h, j, tb)
-        mm([(key, ID, r("RAMP", 0, 32 * A))], stop=False, grp=gid)
+        mm([(key, ID, r("RAMP"))], stop=False, grp=gid)
         st = 32 // rep
-        pieces = CFG["vp"].get(o // 32, [p + ("S",) for p in CFG["pieces"]])
-        for x, (b0, b1, eng) in enumerate(pieces):
+        for b0, b1, eng in gp:
             lo, hi = g0 + 32 * A * b0, g0 + 32 * A * b1
             k = pick(eng, r(n("G"), lo, hi), ind(XS, r("NU", 128 * h + lo // 16, 128 * h + hi // 16)), 0.5)
             if eng == "S":
                 ops[k]["after"] = last[0]
                 last[0] = k
-            for y in range(st):
-                tt(r(n("MX"), lo + y, hi, st), r(n("G"), lo + y, hi, st), r(rb, rep * A * b0, rep * A * b1), AL.max)
-            for z, src, end in (("ZA", "G", False), ("ZM", "MX", x == len(pieces) - 1)):
+        for x, (b0, b1) in enumerate(pieces):
+            lo, hi = g0 + 32 * A * b0, g0 + 32 * A * b1
+            for y0 in range(0, st, CFG["mg"]):
+                add("V", [("tt", (r(n("MX"), lo + y, hi, st), r(n("G"), lo + y, hi, st), r(rb, rep * A * b0, rep * A * b1), AL.max), {})
+                          for y in range(y0, y0 + CFG["mg"])], CFG["mg"] * vc(rep * A * (b1 - b0)),
+                    after=lastd["slot"] if (o // 32, j, x) == CFG["hold"] and y0 % 2 == 0 else lastd["out"] if (o // 32, j, x) == CFG["hold2"] else None)
+            for z, src, end in (("ZA", "G", False), ("ZX", "MX", x == len(pieces) - 1)):
                 mm([(key, sel(z, b), r(n(src), g0 + 32 * A * b, g0 + 32 * A * (b + 1))) for b in range(b0, b1)], start=False, stop=end, grp=gid)
-        row = lambda x: r(x, 2 * o, 2 * o + 32 * A)
-        ends = lambda x: r(x, 2 * o + 31, 2 * o + 32 * A, 32)
-        scan(row("S2"), key, r("ZERO", 0, 32 * A))
+        row = lambda x: r(x, 2 * o, 2 * o + 64)
+        ends = lambda x: r(x, 2 * o + 31, 2 * o + 64, 32)
+        step()
+        scan(row("S2"), key, r("ZERO", 0, 64))
         if j == NJ:
             scan(row("S3"), key, row("D3"))
-            tt(r("RV", o // 16, o // 16 + A), ends("S3"), ends("S2"), AL.subtract)
-        scan(row("S1"), key, r("D1", 0, 32 * A))
+            both = lambda x: r(x, 128 * h + 31, 128 * h + 128, 32)
+            if tb:
+                tt(r("RV", 4 * h, 4 * h + 4), both("S3"), both("S2"), AL.subtract)
+            if CFG["sn"] and t < RO - 1:
+                scan(row("S4"), key, row("D4"))
+                if tb:
+                    tt(r("OUT%d%d" % (t, h), 64, 68), both("S4"), both("S3"), AL.subtract)
+        scan(row("S1"), key, r("D1"))
         ou = r("OU", c0, c0 + A)
         tt(ou, ends("S1"), ends("S2"), AL.subtract)
         tt(r("SP", 128 * j + o, 128 * j + o + nt), ind(r(n("G"), g0, g0 + 32 * nt), ou), r("SH", o, o + nt), AL.add)
-        after_mid(h, tb, nt, j)
+        after_mid(t, h, tb, nt, j)
 
     def prepare(t):
         par = t % 2
         tt(r("SS"), r("XC"), r("SH"), AL.add)
         for h in range(2):
-            ts(slot(h, 0, 64, NJ), r("SS", 64 * h, 64 * h + 64), -1024.0, None, AL.add)
+            ts(slot(h, 0, 64, NJ), r("SS", 64 * h, 64 * h + 64), -1024.0, 0.5 if halved(t) else 1.0, AL.add, AL.mult)
             win = r("SB%d" % h, 1024 * par, 1024 * par + 2048)
-            tt(r("D15", 64 * h, 64 * h + 64), ind(win, r("O15", 4 * h, 4 * h + 4)), r("Z%d%d" % (t, h)), AL.subtract)
-        act(r("X", 8192, 8320), r("D15"), AF.Abs)
+            tt(r("D15", 64 * h, 64 * h + 64), ind(win, r("O15", 4 * h, 4 * h + 4)),
+               r("T", 64 * h, 64 * h + 64) if halved(t) else r("Z%d%d" % (t, h), 0, 64), AL.subtract)
+        if halved(t):
+            act(r("X", 8192, 8320), r("D15"), AF.Abs, scale=2.0, bias=r("CZ2"))
+        else:
+            act(r("X", 8192, 8320), r("D15"), AF.Abs)
         tt(r("NF", 0, 32), r("OU", 0, 32), r("BASE", 0, 32), AL.is_equal)
         tt(r("RK", 0, 32), r("NF", 0, 32), r("C0K", 0, 32), AL.add)
         tt(r("M1"), r("RK", 0, 16), r("RK", 16, 32), AL.min)
@@ -493,9 +606,19 @@ def build():
         tt(r("PQ", 0, 8), r("M3"), r("NK"), AL.min)
         tt(r("PQ", 8, 16), r("M3"), r("NP"), AL.min)
         ts(r("RI"), r("PQ"), 524288.0, None, AL.mult)
-        ts(r("RI"), r("RI"), 8191, None, AL.bitwise_and)
-        cp(r("RU"), r("RI"))
+        if CFG["bit"]:
+            ts(r("RU"), r("RI"), 8191, None, AL.bitwise_and)
+        else:
+            ts(r("RI"), r("RI"), 8191, None, AL.bitwise_and)
+            cp(r("RU"), r("RI"))
         pick(CFG["w"], r("W"), ind(r("X", 4096, 8320), r("RU")))
+        if CFG["sn"] and t < RO - 1:
+            mm16(r("QR10", 0, 16), "ZM", "W", 0, 256)
+            ts(r("RI"), r("QR10", 0, 16), 1.0 / 1024, None, AL.mult)
+            ts(r("RI"), r("RI"), 31, None, AL.bitwise_and)
+            tt(r("D4", 31, 256, 32), r("RI", 8, 16), r("D3", 31, 256, 32), AL.add)
+            tt(r("M3"), r("RI", 0, 8), r("RI", 8, 16), AL.subtract)
+            ts(r("D4", 0, 256, 32), r("M3"), -128.0, None, AL.add)
 
     def squares(t, kb):
         mm16(r(kb, 128, 168), "ZW1", "SP", 0, 640)
@@ -508,10 +631,10 @@ def build():
 
     def release(t, h):
         out = r("OUT%d%d" % (t, h))
-        cp(out, ind(r("W"), r("RV", 4 * h, 4 * h + 4)))
+        lastd["out"] = pick(CFG["out"], r(out[1], 0, 64), ind(r("W"), r("RV", 4 * h, 4 * h + 4)))
         land = landing(t, h)
         sid = add("G", [("send", (None, out, t, h), {})], 1200)
-        add("N", [("recv", (land,), {})], 0, lat=CFG["net"], sem="a%d%d" % (t, h), after=sid)
+        add("N", [("recv", (land,), {})], 0, lat=CFG["net"] + (CFG["pad"] if (t, h) == (RO - 1, 0) else 0), sem="a%d%d" % (t, h), after=sid)
         if t == RO - 1:
             dma("Y", "zo%d" % h, r("zo", 64 * h, 64 * h + 64), land, 16384)
 
@@ -522,73 +645,96 @@ def build():
         nx = 2048 * (1 - par)
         for q in range(2):
             dst = r(n("SB"), nx + 512 * q, nx + 512 * q + 512)
-            pick(CFG["ren"][2 * h + q], dst, ind(win, r("LRU", 64 * h + 32 * q, 64 * h + 32 * q + 32)))
+            c = (2.0 if halved(t) else 1.0) * (0.5 if t < RO - 1 and halved(t + 1) else 1.0)
+            k = pick(CFG["ren" if t < RO - 1 else "renl"][2 * h + q], dst, ind(win, r("LRU", 64 * h + 32 * q, 64 * h + 32 * q + 32)), c)
+            if h == 0:
+                lastd["renew"] = k
+            elif t < RO - 1 and q >= CFG["r1"]:
+                ops[k]["after"] = lastd["abs"]
             if t == RO - 1:
                 dma("Y", "so%d%d" % (h, q), r("so", 1024 * h + 512 * q, 1024 * h + 512 * q + 512), dst, 131072)
 
     def elected(t, a, b, bank):
         c = lambda x: r(x, a, b)
         tt(c("MU"), c("OU"), c("BASE"), AL.subtract)
-        pick(CFG["kg"], r("KG", 16 * a, 16 * b), ind(r("KW"), c("MU")))
+        k = pick(CFG["kg"][1 if a else 0], r("KG", 16 * a, 16 * b), ind(r("KW"), c("MU")))
+        if b == 40 and CFG["kga"]:
+            ops[k]["after"] = lastd["renew"]
         pk = r(bank, 128, 128 + b - a)
+        k = len(ops)
         mm16(pk, "Z15", "KG", 16 * a, 16 * b)
+        if b == 40 and t < RO - 1 and CFG["pka"]:
+            ops[k]["after"] = lastd["diff"]
         tt(c("DE"), c("DE"), c("NF"), AL.mult)
         tt(c("YI"), c("YI"), c("DE"), AL.add)
         tt(c("KU"), pk, c("UI"), AL.mult)
         tt(c("EI"), c("KU"), c("YI"), AL.add)
         ts(c("EI"), c("EI"), 4095, None, AL.bitwise_and)
-        cp(r("EU", a + 8, b + 8), c("EI"))
-        lo = 0 if a == 0 else a + 8
-        tt(r("EM", 16 * lo, 16 * b + 128), ind(r("IOTA"), r("EU", lo, b + 8)), r("MASK", 16 * lo, 16 * b + 128), AL.mult)
-        pm = r("QK00", 256, 384)
-        more = [(pm, SH1, r("MK", 0, 128)), (pm, ID, r("MK", 128, 256))] if a == 0 else []
-        mm(more + [(pm, ID, r("EM", 16 * d, 16 * d + 128)) for d in range(lo, b + 8, 8)], start=a == 0, stop=a > 0, grp=(t, "pm"))
+        ts(r("EH", a + 8, b + 8), c("EI"), -2048.0, None, AL.add)
+        lo, hi, qb = a + 8 if a else 0, b + 8, "QR10"
+        w = 16 * (hi - lo)
+        for q in range(4):
+            mms([(r(qb, x, w, 16), r("ZR", 128 * x, 128 * x + 128), r("EH", lo, hi)) for x in range(4 * q, 4 * q + 4)])
+        tt(r("EM", 16 * lo, 16 * hi), r(qb, 0, w), r("MASK", 16 * lo, 16 * hi), AL.mult)
         if a == 0:
             return
+        row = lambda x, d=0: r(x, 128 * d, 128 * d + 128)
+        mm([(PM, SH1, row("MK")), (PM, ID, row("MK", 1))] + [(PM, ID, row("EM", d)) for d in range(4)], stop=False, grp=(t, "pm"))
+        mm([(PM, ID, row("EM", d)) for d in (4, 5)], start=False, grp=(t, "pm"))
         if t < RO - 1:
-            cp(r("M"), pm)
+            act(r("M"), PM, AF.Copy)
         else:
-            act(r("MO"), pm, AF.Identity, bias=r("C2K"))
+            act(r("MO"), PM, AF.Identity, bias=r("C2K"))
             dma("Y", "mo", r("mo"), r("MO"), 65536)
 
     def count():
         tt(r("RK", 32, 40), r("NF", 32, 40), r("C0K", 32, 40), AL.add)
         tt(r("RM"), r("RK", 32, 40), r("PQ", 0, 8), AL.min)
         ts(r("RL"), r("RM"), NONE * RS, None, AL.is_lt)
-        pa = r("QK11", 480, 481)
+        pa = r("QK10", 480, 481)
         mm([(pa, r("ONES"), r("RL", k, k + 1)) for k in range(8)])
         cp(r("AI"), pa)
         ts(r("AI"), r("AI"), 63, None, AL.bitwise_and)
         cp(r("AF"), r("AI"))
 
+    def stepped(f):
+        def g_(*a):
+            step()
+            f(*a)
+        return g_
+
+    offsets, store, gap, names, prepare, squares, elected, release, renew, count = [stepped(f) for f in (offsets, store, gap, names, prepare, squares, elected, release, renew, count)]
     for t in range(RO):
         offsets()
         store(t, 0)
-        store(t, 1)
         gap(t, 0)
+        if t:
+            elected(t - 1, 24, 40, "QR11")
+            renew(t - 1, 1)
+        store(t, 1)
+        own_name(t, 0)
         gap(t, 1)
+        own_name(t, 1)
         for j in range(1, NJ + 1):
             for h, tb in STREAMS:
                 end = (h, tb) == STREAMS[-1]
-                hook = None
-                if (h, tb, j) == (1, 0, 1):
-                    hook = lambda kb, t=t: masks(t, kb if A == 2 else "QK11")
-                if end and j == 2:
-                    hook = lambda kb, t=t: names(t, kb)
-                if (h, tb, j) == (1, 0, NJ):
-                    hook = lambda kb, t=t: squares(t, kb)
-                corr(t, h, tb, j, hook)
+                corr(t, h, tb, j, (lambda kb, t=t: masks(t, "QR10")) if end and j == 1 else None)
+                if end and j == 1:
+                    names(t, "QR11")
                 if end and j == NJ - 1:
                     prepare(t)
+                    squares(t, "QR11")
+                    elected(t, 0, 24, "QR11")
                 if j == NJ and tb + 16 * A == 64:
                     release(t, h)
-                    renew(t, h)
-                if (h, tb, j) == (1, 0, NJ):
-                    elected(t, 0, 32, "QK00")
-        tt(r("NF", 32, 40), r("OU", 32, 40), r("BASE", 32, 40), AL.is_equal)
+        renew(t, 0)
+        if t == RO - 1:
+            renew(t, 1)
+        tt(r("NF", 32, 40), r("OU", 32, 40), r("BASE", 0, 8), AL.is_equal)
         if t < RO - 1:
             count()
-        elected(t, 32, 40, "QK01")
+        else:
+            elected(t, 24, 40, "QR11")
     return ops
 
 
@@ -653,33 +799,167 @@ def schedule(ops, deps):
         fin = [0.0] * n
         slots = {}
         for i in seq:
-            t = max([fin[p] + d for p, d in pre[i]] + [first[i]])
-            sl = slots.setdefault(ops[i]["eng"], [])
+            t, b = first[i], busy[i]
+            for p, d in pre[i]:
+                if fin[p] + d > t:
+                    t = fin[p] + d
+            sl = slots.setdefault(eng[i], [])
             k = len(sl)
             while k > 0 and sl[k - 1][1] > t:
                 k -= 1
-            while k < len(sl) and sl[k][0] < t + busy[i]:
-                t = max(t, sl[k][1])
+            while k < len(sl) and sl[k][0] < t + b:
+                if sl[k][1] > t:
+                    t = sl[k][1]
                 k += 1
-            sl.insert(k, (t, t + busy[i]))
-            fin[i] = t + busy[i]
+            sl.insert(k, (t, t + b))
+            fin[i] = t + b
         return fin
 
+    def both_ways(seq, passes):
+        best = None
+        for x in range(passes):
+            fin = place(seq, fw, zero)
+            end = max(fin[i] + tail[i] for i in range(n))
+            if best is None or end < best[0]:
+                best = (end, fin)
+            if x < passes - 1:
+                back = place(sorted(range(n), key=lambda i: (-fin[i], -i)), bw, tail)
+                seq = sorted(range(n), key=lambda i: (-back[i], i))
+        return best
+
+    eng = [o["eng"] for o in ops]
     prio = [0.0] * n
     for i in range(n - 1, -1, -1):
-        prio[i] = busy[i] + max([d * CFG["wl"] + prio[s] for s, d in bw[i]] + [ops[i]["lat"]])
+        prio[i] = busy[i] + max([d + prio[s] for s, d in bw[i]] + [ops[i]["lat"]])
     zero, tail = [0.0] * n, [o["lat"] for o in ops]
-    seq = sorted(range(n), key=lambda i: (-prio[i], i))
-    best = None
-    for _ in range(CFG["passes"]):
-        fin = place(seq, fw, zero)
-        end = max(fin[i] + tail[i] for i in range(n))
-        if best is None or end < best[0]:
-            best = (end, fin)
-        back = place(sorted(range(n), key=lambda i: (-fin[i], -i)), bw, tail)
-        seq = sorted(range(n), key=lambda i: (-back[i], i))
+    cases = []
+    for f, gc_, wake, fp in CFG["cases"]:
+        cases.append(([o["busy"] if o["eng"] in "GY" else (fp if o["eng"] == "P" else f) * (o["busy"] + o["ge"] * (gc_ - CFG["gather"])) for o in ops],
+                      [[(p, ops[p]["lat"] + wake if deps[i][p] else 0) for p in deps[i]] for i in range(n)]))
+
+    def score(plan_):
+        seq = sorted(range(n), key=lambda i: (plan_[1][i] - busy[i], i))
+        total = 0.0
+        for (bs, pre), w in weights:
+            fin, free = [0.0] * n, {"N": 0.0, "V": 0.0, "S": 0.0, "P": 0.0, "G": 0.0, "Y": 0.0}
+            for i in seq:
+                e = eng[i]
+                t = free[e]
+                for p, d in pre[i]:
+                    if fin[p] + d > t:
+                        t = fin[p] + d
+                fin[i] = free[e] = t + bs[i]
+                free["N"] = 0.0
+            total += w * math.log(max(fin[i] + tail[i] for i in ends))
+        return (total,) + plan_[1:]
+
+    ends = [i for i in range(n) if not succ[i]]
+    weights = [(cases[CFG["cases"].index(c)], CFG["cases"].count(c)) for c in sorted(set(CFG["cases"]))]
+
+    best = score(both_ways(sorted(range(n), key=lambda i: (-prio[i], i)), CFG["passes"]))
+    span = max(best[1])
+    rnd = np.random.RandomState(CFG["seed"])
+    for _ in range(CFG["iters"]):
+        lo, w = rnd.uniform(-4000, span), rnd.uniform(2000, 15000)
+        shake = rnd.uniform(-CFG["sig"], CFG["sig"], n).tolist()
+        if rnd.uniform() < CFG["byphase"]:
+            by = rnd.uniform(-CFG["sigp"], CFG["sigp"], ops[-1]["phase"] + 1) * (rnd.uniform(size=ops[-1]["phase"] + 1) < CFG["pp"])
+            shake = [float(by[o["phase"]]) for o in ops]
+        key = [0.0] * n
+        for i in range(n):
+            t = best[1][i] - busy[i]
+            if lo <= t < lo + w:
+                t += shake[i]
+            for p, d in fw[i]:
+                if key[p] > t:
+                    t = key[p]
+            key[i] = t
+        other = score(both_ways(sorted(range(n), key=lambda i: (key[i], i)), CFG["inner"]))
+        if other[0] <= best[0]:
+            best = other
     end, fin = best
-    return sorted(((i, fin[i] - busy[i]) for i in range(n)), key=lambda x: (x[1], x[0])), end
+    seq = sorted(range(n), key=lambda i: (fin[i] - busy[i], i))
+    views = []
+    for gc_, wake in CFG["views"]:
+        bs = [o["busy"] + o["ge"] * (gc_ - CFG["gather"]) for o in ops]
+        views.append((bs, [[(p, ops[p]["lat"] + wake if deps[i][p] else 0) for p in deps[i]] for i in range(n)],
+                      [[(s, ops[i]["lat"] + wake if deps[s][i] else 0) for s in succ[i]] for i in range(n)]))
+
+    def queue(order, bs, pre, first):
+        out, free = [0.0] * n, {}
+        for i in order:
+            t = max(first[i], free.get(eng[i], 0.0))
+            for p, d in pre[i]:
+                if out[p] + d > t:
+                    t = out[p] + d
+            out[i] = t + bs[i]
+            if eng[i] != "N":
+                free[eng[i]] = out[i]
+        return out
+
+    def fill(order, bs, pre, first, out):
+        slots = {}
+        for i in order:
+            t, b = first[i], bs[i]
+            for p, d in pre[i]:
+                if out[p] + d > t:
+                    t = out[p] + d
+            sl = slots.setdefault(eng[i], [])
+            k = len(sl)
+            while k > 0 and sl[k - 1][1] > t:
+                k -= 1
+            while k < len(sl) and sl[k][0] < t + b:
+                if sl[k][1] > t:
+                    t = sl[k][1]
+                k += 1
+            sl.insert(k, (t, t + b))
+            out[i] = t + b
+
+    def total(order):
+        s = 0.0
+        for (bs, pre), w in weights:
+            out = queue(order, bs, pre, zero)
+            s += w * math.log(max(out[i] + tail[i] for i in range(n)))
+        return s
+
+    cur, known = total(seq), {}
+    for _ in range(CFG["local"]):
+        v = rnd.randint(len(views))
+        bs, pre, post = views[v]
+        if v not in known:
+            known[v] = (queue(seq, bs, pre, zero), queue(seq[::-1], bs, post, tail))
+        ahead, behind = known[v]
+        w = rnd.randint(CFG["wmin"], CFG["wmax"])
+        a = min(max(0, rnd.randint(-w // 2, n - w // 2)), n - 1)
+        part = seq[a:a + w]
+        head, foot = {}, {}
+        for i in seq[max(0, a - 400):a]:
+            head[eng[i]] = ahead[i]
+        for i in seq[a + w + 400:a + w - 1:-1]:
+            foot[eng[i]] = behind[i]
+        head["N"] = foot["N"] = 0.0
+        first = {i: head.get(eng[i], 0.0) for i in part}
+        last_ = {i: max(tail[i], foot.get(eng[i], 0.0)) for i in part}
+        sig = rnd.uniform(0, CFG["sigl"])
+        key = {}
+        for i in part:
+            t = ahead[i] - bs[i] + rnd.uniform(-sig, sig)
+            for p, d in pre[i]:
+                if key.get(p, t) > t:
+                    t = key[p]
+            key[i] = t
+        rank = {i: k for k, i in enumerate(part)}
+        order = sorted(part, key=lambda i: (key[i], rank[i]))
+        f_, b_ = list(ahead), list(behind)
+        fill(order, bs, pre, first, f_)
+        for x in range(CFG["turns"]):
+            fill(sorted(part, key=lambda i: (-f_[i], -rank[i])), bs, post, last_, b_)
+            fill(sorted(part, key=lambda i: (-b_[i], rank[i])), bs, pre, first, f_)
+        other = seq[:a] + sorted(part, key=lambda i: (f_[i] - bs[i], rank[i])) + seq[a + w:]
+        s = total(other)
+        if s <= cur:
+            cur, seq, known = s, other, {}
+    return [(i, k) for k, i in enumerate(seq)], end
 
 
 def plan_waits(ops, deps, order):
@@ -759,6 +1039,8 @@ def rank_program(g, core, T, topo):
             return q.matmul(*a)
         if name == "iota":
             return q.iota(*a, **kw)
+        if name == "asel":
+            return q.affine_select(*a)
         return q.dma_start(*a)
 
     cnt = {"V": 0, "S": 0, "P": 0, "G": 0}

import math
import numpy as np
from concourse.mybir import dt, AluOpType, AxisListType, ActivationFunctionType

AL = AluOpType
AF = ActivationFunctionType
RO, NJ = 3, 5
CFG = {"gather": 1.4, "pe": 0.42, "ls": 240, "lx": 240, "net": 2600, "passes": 3, "mmsplit": 4, "wl": 1.0, "fe": 0.83, "mn": 53, "sfix": 0,
       "A": 2, "rep": 2, "pieces": [(0, 16)], "sh": "V", "cev": "V", "cod": "S", "st": 0, "ren": "SSSS", "renl": "SSSS", "w": "S", "kg": "SS", "xc": "S", "vp": {},
       "cases": [(1.0, 1.3, 180, 1.0), (1.2, 1.75, 200, 1.2), (1.2, 1.75, 200, 1.2), (1.2, 0.9, 260, 1.2), (1.1, 1.5, 320, 1.1), (1.1, 1.15, 200, 1.45)], "inner": 2, "iters": 700, "seed": 7, "sig": 300, "rsp": True,
       "pre": True, "ct": "SSSS", "sn": False, "bit": False, "fine": {(3, 5): (8, [(0, 8), (8, 12), (12, 16)])}, "one": False, "g6": False, "mg": 1, "r1": 1, "pka": False, "views": [(1.3, 220), (1.45, 240), (1.6, 220)], "local": 800, "wmin": 150, "wmax": 600, "sigl": 500, "turns": 1, "hold": None, "hold2": None, "kga": True, "pk": False, "md": True, "half": True, "out": "V", "hr": "V", "ce1": "V", "byphase": 0.3, "sigp": 1500, "pp": 0.3, "sb0": "S", "pad": 1500, "rrv": 4}
A = CFG["A"]
STREAMS = [(h, tb) for h in range(2) for tb in range(0, 64, 16 * A)]
T1 = 6144

POOL = {"PF": "float32", "PI": "int32", "PU": "uint16", "PH": "float16", "PB": "bfloat16"}
USED = {k: 0 for k in POOL}
LAY = {}
SCRATCH = {}


def own(name, where, shape, dtype):
    SCRATCH[name] = (where, shape, dtype)
    LAY[name] = (name, 0, shape[-1])


def alloc(name, pool, n):
    o = (USED[pool] + 15) // 16 * 16
    LAY[name] = (pool, o, n)
    USED[pool] = o + n


own("X", "sbuf", [128, 8320], "bfloat16")
own("TBL", "sbuf", [128, T1 + 4104], "float32")
own("ZR", "sbuf", [128, 2048], "bfloat16")
own("CC", "sbuf", [128, NJ * 256], "float32")
own("CT", "sbuf", [128, 1024], "float16")
own("RR", "sbuf", [128, 256], "float16")
own("NMI", "sbuf", [128, 128], "int32")
own("WTI", "sbuf", [128, 1], "int32")
own("KPI", "sbuf", [128, 2], "int32")
for _h in range(2):
    own("SB%d" % _h, "sbuf", [128, 3072], "bfloat16")
    own("G%d" % _h, "sbuf", [128, 2048], "bfloat16")
    own("MX%d" % _h, "sbuf", [128, 2048], "bfloat16")
    for _t in range(RO + 1):
        own("Z%d%d" % (_t, _h), "sbuf", [128, 68 if CFG["sn"] and 0 < _t < RO else 64], "bfloat16")
    for _t in range(RO):
        own("OUT%d%d" % (_t, _h), "sbuf", [128, 68 if CFG["sn"] and _t < RO - 1 else 64], "bfloat16")
    for _n in ("QK", "QR"):
        for _q in range(2):
            own("%s%d%d" % (_n, _h, _q), "psum", [128, 512], "float32")
own("MO", "sbuf", [128, 128], "float32")
own("CM", "sbuf", [128, 40, 16], "float16")
LAY["CM"] = ("CM", 0, 640)
for _n in ("S1", "S2", "S3", "S4"):
    alloc(_n, "PF", 264)
for _n, _w in (("QQ", 16), ("D4", 264), ("KM", 8), ("HO", 8), ("T", 128), ("C0F", 40), ("C0K", 40), ("C0S", 40), ("RK", 40), ("M1", 16), ("M3", 8),
               ("NP", 8), ("NK", 8), ("PQ", 16), ("RM", 8), ("NF", 40), ("KU", 40), ("YI", 40), ("DE", 40), ("NC", 8), ("D15", 128), ("SH", 128),
               ("XI", 144), ("XH", 144), ("BX", 128), ("DX", 16), ("DJ", 40), ("DA", 40), ("RA", 128), ("NN", 256), ("NQ", 256), ("G15", 1), ("G7", 1), ("B", 1), ("P1", 1), ("WF", 1),
               ("K15", 1), ("K1", 1), ("M2", 1), ("BA", 1), ("E0", 1), ("E13", 1), ("E2", 1), ("ES", 4), ("S16", 1), ("K2K", 1), ("LT", 16), ("INR", 16), ("TT", 16), ("TB", 32),
               ("I16", 128), ("KF", 2), ("KM16", 2), ("KW", 32), ("W1K", 1), ("NB", 16), ("K0J", 40), ("AF", 1), ("OF", 5), ("OF0", 5), ("C2K", 1), ("CSH", 1), ("B19", 1),
               ("C1K", 1), ("B16", 1), ("CKB", 1), ("KB", 1), ("CZH", 1), ("CZ2", 1), ("CK", 8), ("HB", 4), ("B15", 16), ("BASE", 40), ("D1", 64), ("D3", 256), ("ZERO", 128), ("DG", 64)):
    alloc(_n, "PF", _w)
for _n, _w in (("ZI", 8), ("RI", 16), ("UI", 40), ("SQ", 40), ("EI", 40), ("OI", 40),
               ("PP", 1), ("PT", 1), ("PT2", 1), ("PT3", 1), ("PT4", 1), ("PT5", 1), ("PT6", 1), ("K16", 2), ("BI", 16), ("NI", 256), ("AI", 1)):
    alloc(_n, "PI", _w)
for _n, _w in (("NU", 256), ("UL", 16), ("OU", 40), ("NL", 8), ("HU", 8), ("HV", 8), ("LRU", 128), ("O15", 8), ("RU", 16), ("RV", 8), ("C5", 8), ("MU", 40)):
    alloc(_n, "PU", _w)
for _n, _w in (("CG", 64), ("EH", 48), ("M", 128), ("CM1", 128), ("LRH", 128), ("EM", 768), ("MK", 256), ("SP", 768), ("SS", 128), ("KG", 640), ("KR", 32), ("CF", 156), ("R1", 256), ("R2", 256)):
    alloc(_n, "PH", _w)
for _n, _w in (("MASK", 768), ("XC", 128), ("W", 256), ("HR", 128), ("ZA", 144), ("ZM", 144), ("Z15", 144), ("ZW1", 144), ("ZW2", 144), ("IDW", 130), ("NID", 128), ("IDH", 128),
               ("NIH", 128), ("ZK", 144), ("ZX", 144), ("LG", 256), ("CN", 256), ("ONES", 128), ("BO", 128), ("TAB", 48), ("RAMP", 64), ("WM4", 1), ("RL", 8)):
    alloc(_n, "PB", _w)
for _k in POOL:
    SCRATCH[_k] = ("sbuf", [128, (USED[_k] + 15) // 16 * 16], POOL[_k])
for _n, _w in (("rec", 4096), ("st", 2048), ("nm", 128), ("arr", 128), ("wt", 1), ("kap", 2), ("so", 2048), ("mo", 128), ("zo", 128)):
    LAY[_n] = (_n, 0, _w)

DMAS = ["arr0", "arr1", "st0", "st1", "rec0", "rec1", "nm", "wt", "kap", "so00", "so01", "so10", "so11", "mo", "zo0", "zo1"]
SEMAPHORES = ["cV", "cS", "cP", "cG", "sent"] + ["d" + n for n in DMAS] + ["a%d%d" % (t, h) for t in range(RO) for h in range(2)]


def r(name, a=0, b=None, s=1):
    buf, o, n = LAY[name]
    if b is None:
        b = n
    cnt = (b - a + s - 1) // s
    mask = (((1 << (cnt * s)) - 1) // ((1 << s) - 1)) << (o + a)
    idx = (slice(None), slice(o + a, o + b) if s == 1 else slice(o + a, o + a + (cnt - 1) * s + 1, s))
    return ("@", buf, mask, idx, cnt)


def cmr(a, b, s=1):
    x = r("CM", a, b, s)
    return x[:3] + (((slice(None), slice(a // 16, b // 16), slice(None)) if s == 1 else (slice(None), slice(None), a)), x[4])


def cm4(j, q0, q1, a):
    mask = sum(r("CM", 128 * j + 32 * q + 16 * a, 128 * j + 32 * q + 16 * a + 16)[2] for q in range(q0, q1))
    return ("@", "CM", mask, (slice(None), slice(8 * j + 2 * q0 + a, 8 * j + 2 * q1, 2), slice(None)), 16 * (q1 - q0))


def ind(win, off):
    return ("#", win, off)


def is_acc(x):
    return isinstance(x, tuple) and len(x) > 0 and x[0] in ("@", "#")


def landing(t, h):
    return r("Z%d%d" % (t + 1, h))


def build():
    ops = []
    gc_ = CFG["gather"]
    lastd = {"phase": 0}

    def step():
        lastd["phase"] += 1

    def add(eng, calls, busy, lat=0, sem=None, grp=None, after=None):
        rd, wr = [], []
        for c in calls:
            for k, x in enumerate(c[1]):
                if not is_acc(x):
                    continue
                if x[0] == "#":
                    (wr if k == 0 else rd).append(x[1])
                    rd.append(x[2])
                else:
                    (wr if k == 0 else rd).append(x)
            for x in c[2].values():
                if is_acc(x):
                    rd.append(x)
        ge = sum(16 * x[2][4] for c in calls for x in c[1][1:2] if is_acc(x) and x[0] == "#")
        ops.append({"phase": lastd["phase"], "ge": ge, "eng": eng, "calls": calls, "busy": busy, "lat": lat, "sem": sem, "grp": grp, "rd": rd, "wr": wr, "after": after})
        return len(ops) - 1

    def short(x):
        return SCRATCH[x[1]][2] in ("bfloat16", "float16", "uint16")

    def vcost(out, ins, per):
        if out[0] == "#":
            return 50 + 3.2 * 16 * out[2][4]
        if ins[0] == "#":
            return 50 + gc_ * out[4]
        return vc(per * out[4])

    def vc(n):
        return max(CFG["mn"], n * CFG["fe"])

    def rate(out, a):
        return 0.5 if out[0] == "@" and a[0] == "@" and short(out) and short(a) else 1

    def tt(out, a, b, op):
        both = a[0] == "@" and a[1][0] != "Q" and b[1][0] != "Q"
        return add("V", [("tt", (out, a, b, op), {})], vcost(out, a, 2 if both else 1))

    def ts(out, a, s1, s2, op0, op1=None):
        args = (out, a, s1, s2, op0) if op1 is None else (out, a, s1, s2, op0, op1)
        return add("V", [("ts", args, {})], vcost(out, a, rate(out, a)))

    def cp(out, a):
        return add("V", [("cp", (out, a), {})], vcost(out, a, rate(out, a)))

    def red(out, a, op):
        return add("V", [("red", (out, a, AxisListType.X, op), {})], vc(a[4]))

    def scan(out, a, b):
        return add("V", [("scan", (out, a, b, 1.0e9, AL.min, AL.add), {})], vc(out[4]))

    def ms(out, v):
        return add("V", [("ms", (out, v), {})], vc(out[4] * (0.5 if short(out) else 1)))

    def act(out, a, f, **kw):
        return add("S", [("act", (out, a, f), kw)], 65 + gc_ * out[4] if a[0] == "#" else vc(out[4]) + CFG["sfix"])

    def lin(eng, out, a, scale, col):
        if eng == "S":
            return act(out, a, AF.Identity, scale=scale, bias=col)
        return ts(out, a, scale, col, AL.mult, AL.add)

    def pick(eng, out, a, scale=1.0):
        if eng == "S":
            return act(out, a, AF.Copy, scale=scale)
        return cp(out, a) if scale == 1.0 else ts(out, a, scale, None, AL.mult)

    def mm(lst, start=True, stop=True, grp=None):
        calls = [("mm", (o, l, x, start and k == 0, stop and k == len(lst) - 1), {}) for k, (o, l, x) in enumerate(lst)]
        if grp is None:
            grp = len(ops)
        w = CFG["mmsplit"]
        cuts = list(range(0, len(calls) - w // 2, w)) or [0]
        for a, b in zip(cuts, cuts[1:] + [len(calls)]):
            add("P", calls[a:b], sum(max(64, c[1][2][4]) for c in calls[a:b]) * CFG["pe"] + 5, lat=40, grp=grp)

    def mms(lst):
        add("P", [("mm", (o, l, x, True, True), {}) for o, l, x in lst], sum(max(64, x[4]) for o, l, x in lst) * CFG["pe"] + 5, lat=40)

    def sel(z, b):
        return r(z, 15 - b, 143 - b)

    def mm16(out, z, name, a, b):
        return mm([(out, sel(z, q), r(name, a + q, b, 16)) for q in range(16)])

    def dma(q, sem, out, src, nbytes):
        lastd[q] = add(q, [("dma", (out, src), {})], 60, lat=2000 + nbytes // 300, sem="d" + sem, after=lastd.get(q) if sem[:2] not in ("so", "mo", "zo") else None)

    def iota(out, pat, base, cm, flag=True):
        k = add("G", [("iota", (out, pat, base, cm), {"allow_small_or_imprecise_dtypes": True} if flag else {})], 130 + 1.66 * out[4], after=lastd.get("G"))
        lastd["G"] = k
        return k

    ID, SH1, NID, IDH = r("IDW", 1, 129), r("IDW", 2, 130), r("NID"), r("IDH")
    XS = r("X", 0, 8192)
    HX = r("XI", 0, 16)
    OFC = 524288.0 + 2048.0

    dma("Y", "kap", r("KPI"), r("kap"), 4000)
    dma("S", "wt", r("WTI"), ("@", "wt", 1, (slice(None),), 1), 4000)
    dma("Y", "arr0", r("Z00"), r("arr", 0, 64), 30000)
    dma("S", "st0", r("SB0", 0, 1024), r("st", 0, 1024), 300000)
    dma("Y", "arr1", r("Z01"), r("arr", 64, 128), 60000)
    dma("S", "nm", r("NMI"), r("nm"), 400000)
    dma("Y", "st1", r("SB1", 0, 1024), r("st", 1024, 2048), 700000)
    dma("S", "rec0", r("X", 0, 4096), r("rec"), 2000000)
    dma("Y", "rec1", r("X", 4096, 8192), r("rec"), 2700000)
    iota(r("PP"), [[1, 1]], 0, 1, False)
    iota(r("NN"), [[-1, 256]], 255, 0)
    iota(r("XI"), [[1, 144]], 0, 0)
    iota(r("BX"), [[16, 8], [0, 16]], 15, 0)
    iota(r("NB"), [[-1, 16]], 16391, 0)
    iota(r("XH"), [[1, 72], [0, 2]], 0, 0)
    iota(r("B19"), [[0, 1]], 524288, 0)
    iota(r("AF"), [[0, 1]], 0, 0)
    iota(r("C1K"), [[0, 1]], 1024, 0)
    iota(r("DJ"), [[1, 5], [0, 8]], 1, 0)
    iota(r("DG"), [[1, 16], [256, 4]], 0, 0) if CFG["g6"] else iota(r("DG"), [[0, 64]], -1, 0)
    iota(r("ZERO"), [[0, 128]], 0, 0)
    iota(r("DA"), [[0, 40 // A], [32, A]], 0, 0)
    iota(r("D1"), [[0, 64]], -1, 0)
    iota(r("RAMP", 0, 32), [[0, 32]], 0, 0)
    iota(r("RAMP", 32, 64), [[0, 32]], -8388608, 0)
    iota(r("CN"), [[0, 256]], -1024, 0)
    iota(r("SB0", 1024, 2048), [[0, 1024]], 0, 0)
    iota(r("SB1", 1024, 2048), [[0, 1024]], 0, 0)
    iota(r("TBL", 4097, T1), [[0, T1 - 4097]], 0, 0)
    iota(r("I16"), [[0, 2], [16, 64]], 0, 0)
    iota(r("C2K"), [[0, 1]], 2048, 0)
    iota(r("D3"), [[0, 256]], 0, 0)
    iota(r("D3", 0, 256, 32), [[0, 8]], -128, 0)
    if CFG["sn"]:
        iota(r("D4"), [[0, 256]], 0, 0)
    iota(r("ONES"), [[0, 128]], 1, 0)
    iota(r("ZR"), [[0, 2048]], 1, 0)
    lastd["G"] = add("G", [("asel", (r("ZR"), r("ZR"), [[-1, 16], [-16, 8], [0, 16]], AL.is_equal, 0.0, 0, 1), {})], 170 + 1.66 * 2048, after=lastd["G"])
    ts(r("PT"), r("PP"), 112, None, AL.bitwise_and)
    ts(r("G15"), r("PT"), 15.0, None, AL.add)
    ts(r("G7"), r("PT"), 0.5, 7.0, AL.mult, AL.add)
    ts(r("CF", 71, 128, 8), r("XI", 0, 8), 0.0, 2048.0, AL.mult, AL.add)
    ts(r("PT2"), r("PP"), 15, None, AL.bitwise_and)
    cp(r("B"), r("PT2"))
    act(r("BA"), r("B"), AF.Copy, scale=32.0 * A)
    ts(r("P1"), r("PP"), 1.0, None, AL.add)
    ts(r("K15"), r("PT2"), 15.0, None, AL.is_equal)
    ts(r("K1"), r("PT2"), 1.0, None, AL.is_ge)
    act(r("S16"), r("K1"), AF.Copy, scale=16.0)
    act(r("K2K"), r("K1"), AF.Copy, scale=2048.0)
    ts(r("PT3"), r("PP"), 1, None, AL.bitwise_and)
    ts(r("M2"), r("PT3"), -float(T1), 2.0 ** 35 - 2048.0, AL.mult, AL.add)
    cp(r("WF"), r("WTI"))
    ts(r("WM4"), r("WTI"), -4.0, None, AL.mult)
    ts(r("IDW"), r("XI", 0, 130), r("P1"), None, AL.is_equal)
    act(r("NID"), ID, AF.Copy, scale=-1.0)
    act(r("IDH"), ID, AF.Copy, scale=0.5)
    ts(r("ZM"), r("XI"), r("G15"), 1024.0, AL.is_equal, AL.mult)
    act(r("ZA"), r("ZM"), AF.Copy, scale=-2.0)
    act(r("ZX"), r("ZM"), AF.Copy, scale=4.0)
    ts(r("Z15"), r("XI"), r("G15"), r("K15"), AL.is_equal, AL.mult)
    ts(r("ZW1"), r("XI"), r("G15"), r("WF"), AL.is_equal, AL.mult)
    ts(r("ZW2"), r("XH"), r("G7"), r("WF"), AL.is_equal, AL.mult)
    ts(r("BO"), r("BX"), r("G15"), None, AL.is_equal)
    act(r("CSH"), r("C1K"), AF.Copy, scale=511.75 / 1024)
    act(r("CZH"), r("C1K"), AF.Copy, scale=1023.75 / 1024)
    act(r("CZ2"), r("C1K"), AF.Copy, scale=2047.5 / 1024)
    act(r("NIH"), ID, AF.Copy, scale=-0.5)
    lin("S", r("CK"), r("XI", 0, 8), 16.0, r("B"))
    act(r("HB"), r("CK", 0, 4), AF.Copy, scale=16.0)
    lin("S", r("BASE"), r("DA"), 1.0, r("BA"))
    lin("S", r("D1", 31, 64, 32), r("BASE", 0, A), 1.0, r("XI", 31, 32))
    lin("S", r("D3", 31, 256, 32), r("CK"), 1.0, r("XI", 128, 129))
    if CFG["g6"]:
        act(r("B16"), r("B"), AF.Copy, scale=16.0)
        lin("S", r("CG"), r("DG"), 1.0, r("B16"))
    else:
        lin("S", r("DG", 15, 64, 16), r("HB"), 1.0, r("XI", 15, 16))
    ts(r("TAB", 0, 16), HX, 1.0, r("B"), AL.add, AL.is_equal)
    ts(r("TAB", 32, 48), HX, 5.0, r("B"), AL.add, AL.is_lt)
    ts(r("LT"), HX, r("B"), None, AL.is_gt)
    tt(r("INR"), r("LT"), r("TAB", 32, 48), AL.add)
    lin("S", r("INR"), r("INR"), -1.0, r("XI", 1, 2))
    lin("S", r("TT"), HX, -1.0, r("C1K"))
    tt(r("TT"), r("TT"), r("INR"), AL.mult)
    lin("S", r("LT"), r("LT"), 1.0, r("B"))
    tt(r("TB", 0, 16), r("TT"), r("LT"), AL.add)
    lin("S", r("INR"), r("INR"), -2048.0, r("C1K"))
    tt(r("TB", 16, 32), r("TB", 0, 16), r("INR"), AL.add)
    cp(r("KF"), r("KPI"))
    for q in range(2):
        ts(r("KR", 16 * q, 16 * q + 16), HX, r("B"), r("KF", q, q + 1), AL.is_equal, AL.mult)
    mms([(r("QK11", 0, 1), r("BO"), r("WM4"))])
    ts(r("BI"), r("NB"), r("QK11", 0, 1), None, AL.add)
    ts(r("W1K"), r("QK11", 0, 1), 256.0, None, AL.mult)
    mms([(r("QK10", 0, 32), r("BO"), r("KR"))])
    cp(r("KW"), r("QK10", 0, 32))
    ts(r("K0J"), r("DJ"), r("KW", 0, 1), None, AL.mult)
    ms(r("KW", 0, 1), 0.0)

    ts(r("BI"), r("BI"), 15, None, AL.bitwise_and)
    ts(r("K16"), r("KPI"), 15, None, AL.bitwise_and)
    ts(r("KM16", 0, 1), r("K16", 0, 1), 256.0, r("K1"), AL.mult, AL.mult)
    ts(r("KM16", 1, 2), r("K16", 1, 2), 256.0, None, AL.mult)
    ts(r("KF", 0, 1), r("KF", 0, 1), r("K1"), None, AL.mult)
    for q in range(2):
        ts(r("CF", 64 * q, 64 * q + 64, 4), r("BI"), r("S16") if q == 0 else 16.0, r("KF", q, q + 1), AL.mult, AL.add)
        ts(r("CF", 64 * q + 1, 64 * q + 64, 4), r("BI"), r("KM16", q, q + 1), None, AL.mult)
    lin("S", r("CF", 2, 64, 4), HX, 0.0, r("K1"))
    lin("S", r("CF", 66, 128, 4), HX, 0.0, r("XI", 1, 2))
    lin("S", r("CF", 7, 64, 8), r("XI", 0, 8), 0.0, r("K2K"))
    act(r("CF", 3, 128, 8), HX, AF.Copy, scale=0.0)
    act(r("CF", 128, 156), r("XI", 0, 28), AF.Copy, scale=0.0)
    ts(r("PT4"), r("PP"), 31, None, AL.bitwise_and)
    ts(r("PT5"), r("PP"), 29, None, AL.bitwise_and)
    ts(r("E0"), r("PT4"), 0.0, None, AL.is_equal)
    ts(r("E2"), r("PT4"), 2.0, 1.0 / 32, AL.is_equal, AL.mult)
    ts(r("E13"), r("PT5"), 1.0, None, AL.is_equal)
    act(r("NQ"), r("NN"), AF.Square)
    ts(r("NI"), r("NQ"), r("E2"), -0.484375, AL.mult, AL.add)
    act(r("R1"), r("NN"), AF.Identity, scale=r("E0"), bias=r("E13"))
    tt(r("RR"), r("R1"), r("NI"), AL.add)

    def part(x, s):
        return x[:3] + ((slice(32 * s, 32 * s + 32), x[3][1]), x[4])

    for q in range(2):
        for k in range(2):
            bank = "QK%d%d" % (q, k)
            mms([(r(bank, 128 * i, 128 * i + 128), r("CF", 16 * q + 8 * k + 4 * i, 16 * q + 8 * k + 4 * i + 128), ID) for i in range(2)])
            o, src = r("CT", 512 * q + 256 * k, 512 * q + 256 * k + 256), r(bank, 0, 256)
            act(o, src, AF.Copy) if CFG["ct"][2 * q + k] == "S" else cp(o, src)
    for x in range(16):
        bank, tmp = ("QK00", "QK01", "QK10", "QK11")[x % 4], r("G%d" % (x % 2), 512 * (x // 2 % 4), 512 * (x // 2 % 4) + 512)
        s, i = x // 4, 2 * x % 8
        blocks = [(r(bank, 256 * k, 256 * k + 256), part(r("CT", 128 * (i + k), 128 * (i + k) + 128), s), part(r("RR"), s)) for k in range(2)]
        mms(blocks)
        act(tmp, r(bank), AF.Identity, bias=r("B19"))
        o = T1 * (x // 8) + 1 + 512 * (x % 8)
        if CFG["st"] and x % CFG["st"] == CFG["st"] - 1:
            add("P", [("mm", (r(bank), NID, tmp, True, False), {})] + [("mm", b + (False, k == 1), {}) for k, b in enumerate(blocks)], 1024 * CFG["pe"], lat=40)
            act(r("TBL", o, o + 512), r(bank), AF.Copy)
        else:
            tt(r("TBL", o, o + 512), r(bank), tmp, AL.subtract)
    cp(r("TBL", 0, T1 + 1, T1), r("TBL", 4096, T1 + 4097, T1))
    TW = r("TBL", 0, T1 + 4097)

    NONE = 15 * 16384 + 8192
    RS = 1.0 / 524288
    ts(r("M"), r("NMI"), -2048.0, None, AL.add)
    PM = r("QK11", 320, 448)
    mms([(PM, ID, r("M"))])
    act(r("NC"), r("CK"), AF.Copy, scale=32.0)
    for h in range(2):
        lin("S", r("B15", 4 * h, 4 * h + 4), r("HB"), 1.0, r("XI", 15, 16))
    lin("S", r("B15", 8, 16), r("B15", 0, 8), 1.0, r("C1K"))
    ts(r("NK"), r("CK"), float(NONE + 4096), RS, AL.add, AL.mult)
    if CFG["pk"]:
        act(r("CKB"), r("C1K"), AF.Copy, scale=(32 * 16384 + 2048) * RS / 1024)
        act(r("KB"), r("B19"), AF.Copy, scale=-1.0)
        lin("S", r("KB"), r("B"), 16384.0, r("KB"))
        act(r("ZK"), r("ZM"), AF.Copy, scale=r("KB"))

    def offsets():
        ts(r("OI"), r("K0J"), r("AF"), None, AL.add)
        ts(r("OI"), r("OI"), 4095, None, AL.bitwise_and)
        ts(r("OF0"), r("OI", 0, 40, 8), r("K1"), OFC, AL.mult, AL.add)
        ts(r("OF"), r("OI", 0, 40, 8), OFC, None, AL.add)
        for j in range(NJ):
            lin(CFG["cod"], r("CC", 256 * j + 1, 256 * j + 256, 2), r("ZERO"), 1.0, r("OF", j, j + 1))

    def store(t, h):
        z = "Z%d%d" % (t, h)
        four = lambda x: r(x, 4 * h, 4 * h + 4)
        if t == 0 or not CFG["sn"]:
            ps = r("QR%d0" % h, 0, 4)
            mm16(ps, "ZM", z, 0, 64)
            ts(four("ZI"), ps, 1.0 / 1024, None, AL.mult)
            ts(four("ZI"), four("ZI"), 31, None, AL.bitwise_and)
            tt(four("NL"), four("ZI"), four("NC"), AL.add)
        else:
            tt(four("NL"), r(z, 64, 68), four("NC"), AL.add)
        cp(ind(r("X", 0, 4096), four("NL")), r(z, 0, 64))
        cp(ind(r("X", 4096, 8192), four("NL")), r(z, 0, 64))

    def slot(h, tb, nt, d):
        return r("SB%d" % h, 1024 + 16 * tb + d, 1024 + 16 * (tb + nt), 16)

    def halved(t):
        return CFG["half"] and t > 0

    def after_mid(t, h, tb, nt, d):
        o = 64 * h + tb
        sp = r("SP", 128 * d + o, 128 * d + o + nt)
        if tb + nt == 64:
            c = 0.5 if halved(t) else 1.0
            lastd["slot"] = ts(slot(h, 0, 64, d), r("SP", 128 * d + 64 * h, 128 * d + 64 * h + 64), -1024.0, c, AL.add, AL.mult)
            if d < NJ:
                lin(CFG["sh"] if d else CFG["sb0"], r("SH", 64 * h, 64 * h + 64), r("SP", 128 * d + 64 * h, 128 * d + 64 * h + 64), 0.5, r("CSH"))

    def lanes(bank, j, t0, t1):
        w = t1 - t0
        if j:
            return [(r(bank[0], bank[1] + a, bank[1] + w, 2), sel("ZM", 0), cm4(j, t0 // 32, t1 // 32, a)) for a in range(2)]
        return [(r(bank[0], bank[1] + tb + a, bank[1] + tb + 16 * A, A), sel("ZM", 0), r("CM1", t0 + tb + 16 * a, t0 + tb + 16 * a + 16))
                for tb in range(0, w, 16 * A) for a in range(A)]

    def even(bank, j, t0, t1):
        lin(CFG["cev"] if j else CFG["ce1"], r("CC", 256 * j + 2 * t0, 256 * j + 2 * t1, 2), r(bank[0], bank[1], bank[1] + t1 - t0), 1.0 / 1024, r("OF0", j, j + 1))

    def gap(t, h):
        n = lambda x: x + str(h)
        four = lambda x: r(x, 4 * h, 4 * h + 4)
        half = lambda x, o=0: r(x, o + 64 * h, o + 64 * h + 64)
        z = r("Z%d%d" % (t, h), 0, 64)
        so = 2048 * (t % 2)
        if halved(t):
            lin("S", half("T"), z, 0.5, r("CZH"))
        for q in (1, 0):
            bank = n("QR") + str(q)
            rows = [(r(bank, 64 * k, 64 * k + 64), ID, r(n("SB"), so + 8 * q + k, so + 1024, 16)) for k in range(8)]
            less = [(r(bank, 64 * k, 64 * k + 64), r("NIH") if halved(t) else NID, z) for k in range(8)]
            if CFG["pre"]:
                mm(less + rows if h == 0 else rows + less)
            else:
                for k2 in (0, 4):
                    add("P", [("mm", x[k] + (x is rows, x is less), {}) for k in range(k2, k2 + 4) for x in (rows, less)], 8 * 64 * CFG["pe"] + 5, lat=40)
            if q == 0:
                ops[-1]["after"] = lastd["diff"]
            lastd["diff"] = len(ops) - 1
            k = act(r(n("MX"), 512 * q, 512 * q + 512), r(bank), AF.Abs, scale=2.0 if halved(t) else 1.0)
            if q == 0:
                ops[k]["after"] = lastd["abs"]
            lastd["abs"] = k
        kb = n("QR") + "1"
        o = 128 * h
        if CFG["g6"]:
            mm([(r(kb, 0, 64), ID, r("CG"))] + [(r(kb, 0, 64), sel("ZX", q), r(n("MX"), q, 1024, 16)) for q in range(16)])
            for a in range(4):
                red(r("KM", 4 * h + a, 4 * h + a + 1), r(kb, a, 64, 4), AL.min)
            ts(four("HO"), four("KM"), 1.5 * 2.0 ** 35, 1.5 * 2.0 ** 35, AL.add, AL.subtract)
            tt(four("HV"), four("KM"), four("HO"), AL.subtract)
        else:
            mm16(r(kb, 0, 64), "ZM", n("MX"), 0, 1024)
        for a in range(0 if CFG["g6"] else 4):
            scan(r("S1", o + 16 * a, o + 16 * a + 16), r(kb, a, 64, 4), r("DG", 16 * a, 16 * a + 16))
            if not CFG["bit"]:
                red(r("KM", 4 * h + a, 4 * h + a + 1), r(kb, a, 64, 4), AL.min)
        if not CFG["g6"]:
            tt(four("HV"), r("S1", o + 15, o + 64, 16), four("KM"), AL.subtract)
        if halved(t):
            tt(half("SP"), ind(r(n("SB"), so, so + 1024), four("HV")), half("T"), AL.add)
        else:
            tt(half("T"), ind(r(n("SB"), so, so + 1024), four("HV")), z, AL.add)
            ts(half("SP"), half("T"), 0.5, 1023.75, AL.mult, AL.add)
        after_mid(t, h, 0, 64, 0)

    def own_name(t, h):
        n = lambda x: x + str(h)
        four = lambda x: r(x, 4 * h, 4 * h + 4)
        half = lambda x, o=0: r(x, o + 64 * h, o + 64 * h + 64)
        tt(four("HU"), four("HV"), r("HB"), AL.subtract)
        tt(half("CM1"), ind(r("TAB", 0, 16), four("HU")), half("M"), AL.mult)
        bank = (n("QK") + "1", 0)
        mms(lanes(bank, 0, 64 * h, 64 * h + 64))
        even(bank, 0, 64 * h, 64 * h + 64)

    def masks(t, kb):
        hu = r("HU")
        pick(CFG["hr"], r("HR"), ind(HX, hu))
        for d in (2, 3, 4, 5, 0, 1):
            ts(r("MASK", 128 * d, 128 * d + 128), r("HR"), float(d), r("B"), AL.add, AL.is_equal)
        for j in range(1, NJ):
            tt(cmr(128 * j, 128 * j + 128), PM, r("MASK", 128 * j + 128, 128 * j + 256), AL.mult)
            mms(lanes((kb, 128 * j - 128), j, 0, 128))
        ts(r("LG", 0, 128), r("HR"), r("B"), r("K1"), AL.is_ge, AL.mult)
        ts(r("LG", 128, 256), r("HR"), 5.0, r("B"), AL.add, AL.is_lt)
        for q in range(2):
            tt(r("MK", 128 * q, 128 * q + 128), PM, r("LG", 128 * q, 128 * q + 128), AL.mult)
        for j in range(1, NJ):
            even((kb, 128 * j - 128), j, 0, 128)
        par = t % 2
        tt(r("LRU"), ind(r("TB", 16 * par, 16 * par + 16), hu), r("I16"), AL.add)
        ts(r("EH", 0, 8), r("NL"), -2048.0, None, AL.add)

    def names(t, cb):
        cp(cmr(0, 128), r("CM1"))
        mm([(r(cb, 320, 360), sel("ZM", q), cmr(q, 640, 16)) for q in range(16)])
        ts(r("M1", 0, 8), r("HU"), -1.0, 1024.0 - 2048.0 * (t % 2), AL.mult, AL.add)
        ts(r("M1", 8, 16), r("HU"), 10.0, None, AL.is_ge)
        tt(r("M3"), r("M1", 0, 8), r("M1", 8, 16), AL.mult)
        tt(r("O15"), r("M3"), r("B15", 8 * (t % 2), 8 * (t % 2) + 8), AL.add)
        if CFG["pk"]:
            mm([(r(cb, 368, 408), sel("ZM", q), cmr(q, 640, 16)) for q in range(16)] + [(r(cb, 368, 408), sel("ZK", q), r("MASK", 128 + q, 768, 16)) for q in range(16)])
            act(r("C0K"), r(cb, 368, 408), AF.Identity, scale=RS / 1024, bias=r("CKB"))
        else:
            for j in range(NJ):
                ts(r("C0S", 8 * j, 8 * j + 8), r("HU"), j + 1.125, 16384.0 * RS, AL.add, AL.mult)
            act(r("C0K"), r(cb, 320, 360), AF.Copy, scale=RS / 1024)
            tt(r("C0K"), r("C0K"), r("C0S"), AL.add)
        act(r("C0F"), r(cb, 320, 360), AF.Identity, scale=1.0 / 1024, bias=r("C2K"))
        cp(r("C5"), r("C0F", 32, 40))
        tt(r("NP"), r("NK"), r("C0K", 32, 40), AL.min)
        pick(CFG["xc"], r("XC"), ind(XS, r("C5")), 0.5)

    last = [None]

    def corr(t, h, tb, j, hook):
        n = lambda x: x + str(h)
        kb, rb = "QK%d%d" % (h, tb // 32), "QR0%d" % (tb // 32 if A == 2 else h)
        nt, bn, rep = 16 * A, 8 // A, CFG["rep"]
        o = 64 * h + tb
        gp, pieces = CFG["vp"].get(o // 32, [p + ("S",) for p in CFG["pieces"]]), CFG.get("mp") or CFG["pieces"]
        if (o // 32, j) in CFG["fine"]:
            rep, pieces = CFG["fine"][(o // 32, j)][:2]
            gp = [p + ("S",) for p in pieces] if len(CFG["fine"][(o // 32, j)]) == 2 else CFG["fine"][(o // 32, j)][2]
        sv, u0, g0, c0 = 128 * (j - 1) + o, o // 8, 32 * tb, 8 * (j - 1) + o // 16
        step()
        pu = r(kb, 448, 448 + 2 * A)
        mm([(pu, r("ZW2", 14 - 2 * i, 142 - 2 * i), r("SP", sv + 16 * (i % A) + i // A, sv + 16 * (i % A) + 16, bn)) for i in range(8)])
        mm([(r(rb, 0, rep * nt), IDH, r("CN", 0, rep * nt))]
           + [(r(rb, rep * a + i, rep * nt, rep * A), IDH, r("SP", sv + 16 * a, sv + 16 * a + 16)) for a in range(A) for i in range(rep)])
        qq, ul = r("QQ", u0, u0 + 2 * A), r("UL", u0, u0 + 2 * A)
        ts(qq, pu, 2.0 ** 35, r("M2"), AL.add, AL.subtract)
        tt(ul, qq, pu, AL.subtract)
        cc = 256 * (j - 1) + 2 * o
        tt(r("NU", 2 * o, 2 * o + 2 * nt), ind(TW, ul), r("CC", cc, cc + 2 * nt), AL.add)
        if hook:
            step()
            hook(kb)
        step()
        key = r(kb, 0, 64)
        gid = (t, h, j, tb)
        mm([(key, ID, r("RAMP"))], stop=False, grp=gid)
        st = 32 // rep
        for b0, b1, eng in gp:
            lo, hi = g0 + 32 * A * b0, g0 + 32 * A * b1
            k = pick(eng, r(n("G"), lo, hi), ind(XS, r("NU", 128 * h + lo // 16, 128 * h + hi // 16)), 0.5)
            if eng == "S":
                ops[k]["after"] = last[0]
                last[0] = k
        for x, (b0, b1) in enumerate(pieces):
            lo, hi = g0 + 32 * A * b0, g0 + 32 * A * b1
            for y0 in range(0, st, CFG["mg"]):
                add("V", [("tt", (r(n("MX"), lo + y, hi, st), r(n("G"), lo + y, hi, st), r(rb, rep * A * b0, rep * A * b1), AL.max), {})
                          for y in range(y0, y0 + CFG["mg"])], CFG["mg"] * vc(rep * A * (b1 - b0)),
                    after=lastd["slot"] if (o // 32, j, x) == CFG["hold"] and y0 % 2 == 0 else lastd["out"] if (o // 32, j, x) == CFG["hold2"] else None)
            for z, src, end in (("ZA", "G", False), ("ZX", "MX", x == len(pieces) - 1)):
                mm([(key, sel(z, b), r(n(src), g0 + 32 * A * b, g0 + 32 * A * (b + 1))) for b in range(b0, b1)], start=False, stop=end, grp=gid)
        row = lambda x: r(x, 2 * o, 2 * o + 64)
        ends = lambda x: r(x, 2 * o + 31, 2 * o + 64, 32)
        step()
        scan(row("S2"), key, r("ZERO", 0, 64))
        if j == NJ:
            scan(row("S3"), key, row("D3"))
            both = lambda x: r(x, 128 * h + 31, 128 * h + 128, 32)
            if tb:
                tt(r("RV", 4 * h, 4 * h + 4), both("S3"), both("S2"), AL.subtract)
            if CFG["sn"] and t < RO - 1:
                scan(row("S4"), key, row("D4"))
                if tb:
                    tt(r("OUT%d%d" % (t, h), 64, 68), both("S4"), both("S3"), AL.subtract)
        scan(row("S1"), key, r("D1"))
        ou = r("OU", c0, c0 + A)
        tt(ou, ends("S1"), ends("S2"), AL.subtract)
        tt(r("SP", 128 * j + o, 128 * j + o + nt), ind(r(n("G"), g0, g0 + 32 * nt), ou), r("SH", o, o + nt), AL.add)
        after_mid(t, h, tb, nt, j)

    def prepare(t):
        par = t % 2
        tt(r("SS"), r("XC"), r("SH"), AL.add)
        for h in range(2):
            ts(slot(h, 0, 64, NJ), r("SS", 64 * h, 64 * h + 64), -1024.0, 0.5 if halved(t) else 1.0, AL.add, AL.mult)
            win = r("SB%d" % h, 1024 * par, 1024 * par + 2048)
            tt(r("D15", 64 * h, 64 * h + 64), ind(win, r("O15", 4 * h, 4 * h + 4)),
               r("T", 64 * h, 64 * h + 64) if halved(t) else r("Z%d%d" % (t, h), 0, 64), AL.subtract)
        if halved(t):
            act(r("X", 8192, 8320), r("D15"), AF.Abs, scale=2.0, bias=r("CZ2"))
        else:
            act(r("X", 8192, 8320), r("D15"), AF.Abs)
        tt(r("NF", 0, 32), r("OU", 0, 32), r("BASE", 0, 32), AL.is_equal)
        tt(r("RK", 0, 32), r("NF", 0, 32), r("C0K", 0, 32), AL.add)
        tt(r("M1"), r("RK", 0, 16), r("RK", 16, 32), AL.min)
        tt(r("M3"), r("M1", 0, 8), r("M1", 8, 16), AL.min)
        tt(r("PQ", 0, 8), r("M3"), r("NK"), AL.min)
        tt(r("PQ", 8, 16), r("M3"), r("NP"), AL.min)
        ts(r("RI"), r("PQ"), 524288.0, None, AL.mult)
        if CFG["bit"]:
            ts(r("RU"), r("RI"), 8191, None, AL.bitwise_and)
        else:
            ts(r("RI"), r("RI"), 8191, None, AL.bitwise_and)
            cp(r("RU"), r("RI"))
        pick(CFG["w"], r("W"), ind(r("X", 4096, 8320), r("RU")))
        if CFG["sn"] and t < RO - 1:
            mm16(r("QR10", 0, 16), "ZM", "W", 0, 256)
            ts(r("RI"), r("QR10", 0, 16), 1.0 / 1024, None, AL.mult)
            ts(r("RI"), r("RI"), 31, None, AL.bitwise_and)
            tt(r("D4", 31, 256, 32), r("RI", 8, 16), r("D3", 31, 256, 32), AL.add)
            tt(r("M3"), r("RI", 0, 8), r("RI", 8, 16), AL.subtract)
            ts(r("D4", 0, 256, 32), r("M3"), -128.0, None, AL.add)

    def squares(t, kb):
        mm16(r(kb, 128, 168), "ZW1", "SP", 0, 640)
        ts(r("UI"), r(kb, 128, 168), r("W1K"), None, AL.add)
        ts(r("UI"), r("UI"), 4095, None, AL.bitwise_and)
        tt(r("SQ"), r("UI"), r("UI"), AL.mult)
        ts(r("SQ"), r("SQ"), 5, None, AL.arith_shift_right)
        tt(r("YI"), r("SQ"), r("OI"), AL.add)
        tt(r("DE"), r("C0F"), r("YI"), AL.subtract)

    def release(t, h):
        out = r("OUT%d%d" % (t, h))
        lastd["out"] = pick(CFG["out"], r(out[1], 0, 64), ind(r("W"), r("RV", 4 * h, 4 * h + 4)))
        land = landing(t, h)
        sid = add("G", [("send", (None, out, t, h), {})], 1200)
        add("N", [("recv", (land,), {})], 0, lat=CFG["net"] + (CFG["pad"] if (t, h) == (RO - 1, 0) else 0), sem="a%d%d" % (t, h), after=sid)
        if t == RO - 1:
            dma("Y", "zo%d" % h, r("zo", 64 * h, 64 * h + 64), land, 16384)

    def renew(t, h):
        n = lambda x: x + str(h)
        par = t % 2
        win = r(n("SB"), 1024 * par, 1024 * par + 2048)
        nx = 2048 * (1 - par)
        for q in range(2):
            dst = r(n("SB"), nx + 512 * q, nx + 512 * q + 512)
            c = (2.0 if halved(t) else 1.0) * (0.5 if t < RO - 1 and halved(t + 1) else 1.0)
            k = pick(CFG["ren" if t < RO - 1 else "renl"][2 * h + q], dst, ind(win, r("LRU", 64 * h + 32 * q, 64 * h + 32 * q + 32)), c)
            if h == 0:
                lastd["renew"] = k
            elif t < RO - 1 and q >= CFG["r1"]:
                ops[k]["after"] = lastd["abs"]
            if t == RO - 1:
                dma("Y", "so%d%d" % (h, q), r("so", 1024 * h + 512 * q, 1024 * h + 512 * q + 512), dst, 131072)

    def elected(t, a, b, bank):
        c = lambda x: r(x, a, b)
        tt(c("MU"), c("OU"), c("BASE"), AL.subtract)
        k = pick(CFG["kg"][1 if a else 0], r("KG", 16 * a, 16 * b), ind(r("KW"), c("MU")))
        if b == 40 and CFG["kga"]:
            ops[k]["after"] = lastd["renew"]
        pk = r(bank, 128, 128 + b - a)
        k = len(ops)
        mm16(pk, "Z15", "KG", 16 * a, 16 * b)
        if b == 40 and t < RO - 1 and CFG["pka"]:
            ops[k]["after"] = lastd["diff"]
        tt(c("DE"), c("DE"), c("NF"), AL.mult)
        tt(c("YI"), c("YI"), c("DE"), AL.add)
        tt(c("KU"), pk, c("UI"), AL.mult)
        tt(c("EI"), c("KU"), c("YI"), AL.add)
        ts(c("EI"), c("EI"), 4095, None, AL.bitwise_and)
        ts(r("EH", a + 8, b + 8), c("EI"), -2048.0, None, AL.add)
        lo, hi, qb = a + 8 if a else 0, b + 8, "QR10"
        w = 16 * (hi - lo)
        for q in range(4):
            mms([(r(qb, x, w, 16), r("ZR", 128 * x, 128 * x + 128), r("EH", lo, hi)) for x in range(4 * q, 4 * q + 4)])
        tt(r("EM", 16 * lo, 16 * hi), r(qb, 0, w), r("MASK", 16 * lo, 16 * hi), AL.mult)
        if a == 0:
            return
        row = lambda x, d=0: r(x, 128 * d, 128 * d + 128)
        mm([(PM, SH1, row("MK")), (PM, ID, row("MK", 1))] + [(PM, ID, row("EM", d)) for d in range(4)], stop=False, grp=(t, "pm"))
        mm([(PM, ID, row("EM", d)) for d in (4, 5)], start=False, grp=(t, "pm"))
        if t < RO - 1:
            act(r("M"), PM, AF.Copy)
        else:
            act(r("MO"), PM, AF.Identity, bias=r("C2K"))
            dma("Y", "mo", r("mo"), r("MO"), 65536)

    def count():
        tt(r("RK", 32, 40), r("NF", 32, 40), r("C0K", 32, 40), AL.add)
        tt(r("RM"), r("RK", 32, 40), r("PQ", 0, 8), AL.min)
        ts(r("RL"), r("RM"), NONE * RS, None, AL.is_lt)
        pa = r("QK10", 480, 481)
        mm([(pa, r("ONES"), r("RL", k, k + 1)) for k in range(8)])
        cp(r("AI"), pa)
        ts(r("AI"), r("AI"), 63, None, AL.bitwise_and)
        cp(r("AF"), r("AI"))

    def stepped(f):
        def g_(*a):
            step()
            f(*a)
        return g_

    offsets, store, gap, names, prepare, squares, elected, release, renew, count = [stepped(f) for f in (offsets, store, gap, names, prepare, squares, elected, release, renew, count)]
    for t in range(RO):
        offsets()
        store(t, 0)
        gap(t, 0)
        if t:
            elected(t - 1, 24, 40, "QR11")
            renew(t - 1, 1)
        store(t, 1)
        own_name(t, 0)
        gap(t, 1)
        own_name(t, 1)
        for j in range(1, NJ + 1):
            for h, tb in STREAMS:
                end = (h, tb) == STREAMS[-1]
                corr(t, h, tb, j, (lambda kb, t=t: masks(t, "QR10")) if end and j == 1 else None)
                if end and j == 1:
                    names(t, "QR11")
                if end and j == NJ - 1:
                    prepare(t)
                    squares(t, "QR11")
                    elected(t, 0, 24, "QR11")
                if j == NJ and tb + 16 * A == 64:
                    release(t, h)
        renew(t, 0)
        if t == RO - 1:
            renew(t, 1)
        tt(r("NF", 32, 40), r("OU", 32, 40), r("BASE", 0, 8), AL.is_equal)
        if t < RO - 1:
            count()
        else:
            elected(t, 24, 40, "QR11")
    return ops


def depend(ops):
    live = {}
    bank = {}
    deps = []
    for i, o in enumerate(ops):
        d = {}
        for x in o["rd"]:
            for e in live.get(x[1], []):
                if e[2] and e[1] & x[2]:
                    d[e[0]] = True
        for x in o["wr"]:
            for e in live.get(x[1], []):
                if e[1] & x[2]:
                    d[e[0]] = not (o["grp"] is not None and ops[e[0]]["grp"] == o["grp"])
        for x in o["wr"]:
            keep = []
            for e in live.get(x[1], []):
                m = e[1] & ~x[2]
                if m:
                    keep.append([e[0], m, e[2]])
            live[x[1]] = keep
        for x in o["wr"]:
            live[x[1]].append([i, x[2], True])
        for x in o["rd"]:
            live.setdefault(x[1], []).append([i, x[2], False])
        for b in set(x[1] for x in o["rd"] + o["wr"] if x[1][0] == "Q"):
            st = bank.setdefault(b, {"eng": None, "cur": [], "prev": []})
            if st["eng"] != o["eng"]:
                st["prev"], st["cur"], st["eng"] = st["cur"], [], o["eng"]
            for p in st["prev"]:
                d[p] = True
            if o["eng"] == "P" and st["cur"]:
                d.setdefault(st["cur"][-1], False)
            st["cur"].append(i)
        if o["after"] is not None:
            d.setdefault(o["after"], False)
        d.pop(i, None)
        deps.append(d)
    return deps


def schedule(ops, deps):
    n = len(ops)
    succ = [[] for _ in range(n)]
    for i in range(n):
        for p in deps[i]:
            succ[p].append(i)

    def gap_(p, i):
        if not deps[i][p]:
            return 0
        return ops[p]["lat"] + (CFG["ls"] if ops[p]["eng"] == ops[i]["eng"] else CFG["lx"])

    fw = [[(p, gap_(p, i)) for p in deps[i]] for i in range(n)]
    bw = [[(s, gap_(i, s)) for s in succ[i]] for i in range(n)]
    busy = [o["busy"] for o in ops]

    def place(seq, pre, first):
        fin = [0.0] * n
        slots = {}
        for i in seq:
            t, b = first[i], busy[i]
            for p, d in pre[i]:
                if fin[p] + d > t:
                    t = fin[p] + d
            sl = slots.setdefault(eng[i], [])
            k = len(sl)
            while k > 0 and sl[k - 1][1] > t:
                k -= 1
            while k < len(sl) and sl[k][0] < t + b:
                if sl[k][1] > t:
                    t = sl[k][1]
                k += 1
            sl.insert(k, (t, t + b))
            fin[i] = t + b
        return fin

    def both_ways(seq, passes):
        best = None
        for x in range(passes):
            fin = place(seq, fw, zero)
            end = max(fin[i] + tail[i] for i in range(n))
            if best is None or end < best[0]:
                best = (end, fin)
            if x < passes - 1:
                back = place(sorted(range(n), key=lambda i: (-fin[i], -i)), bw, tail)
                seq = sorted(range(n), key=lambda i: (-back[i], i))
        return best

    eng = [o["eng"] for o in ops]
    prio = [0.0] * n
    for i in range(n - 1, -1, -1):
        prio[i] = busy[i] + max([d + prio[s] for s, d in bw[i]] + [ops[i]["lat"]])
    zero, tail = [0.0] * n, [o["lat"] for o in ops]
    cases = []
    for f, gc_, wake, fp in CFG["cases"]:
        cases.append(([o["busy"] if o["eng"] in "GY" else (fp if o["eng"] == "P" else f) * (o["busy"] + o["ge"] * (gc_ - CFG["gather"])) for o in ops],
                      [[(p, ops[p]["lat"] + wake if deps[i][p] else 0) for p in deps[i]] for i in range(n)]))

    def score(plan_):
        seq = sorted(range(n), key=lambda i: (plan_[1][i] - busy[i], i))
        total = 0.0
        for (bs, pre), w in weights:
            fin, free = [0.0] * n, {"N": 0.0, "V": 0.0, "S": 0.0, "P": 0.0, "G": 0.0, "Y": 0.0}
            for i in seq:
                e = eng[i]
                t = free[e]
                for p, d in pre[i]:
                    if fin[p] + d > t:
                        t = fin[p] + d
                fin[i] = free[e] = t + bs[i]
                free["N"] = 0.0
            total += w * math.log(max(fin[i] + tail[i] for i in ends))
        return (total,) + plan_[1:]

    ends = [i for i in range(n) if not succ[i]]
    weights = [(cases[CFG["cases"].index(c)], CFG["cases"].count(c)) for c in sorted(set(CFG["cases"]))]

    best = score(both_ways(sorted(range(n), key=lambda i: (-prio[i], i)), CFG["passes"]))
    span = max(best[1])
    rnd = np.random.RandomState(CFG["seed"])
    for _ in range(CFG["iters"]):
        lo, w = rnd.uniform(-4000, span), rnd.uniform(2000, 15000)
        shake = rnd.uniform(-CFG["sig"], CFG["sig"], n).tolist()
        if rnd.uniform() < CFG["byphase"]:
            by = rnd.uniform(-CFG["sigp"], CFG["sigp"], ops[-1]["phase"] + 1) * (rnd.uniform(size=ops[-1]["phase"] + 1) < CFG["pp"])
            shake = [float(by[o["phase"]]) for o in ops]
        key = [0.0] * n
        for i in range(n):
            t = best[1][i] - busy[i]
            if lo <= t < lo + w:
                t += shake[i]
            for p, d in fw[i]:
                if key[p] > t:
                    t = key[p]
            key[i] = t
        other = score(both_ways(sorted(range(n), key=lambda i: (key[i], i)), CFG["inner"]))
        if other[0] <= best[0]:
            best = other
    end, fin = best
    seq = sorted(range(n), key=lambda i: (fin[i] - busy[i], i))
    views = []
    for gc_, wake in CFG["views"]:
        bs = [o["busy"] + o["ge"] * (gc_ - CFG["gather"]) for o in ops]
        views.append((bs, [[(p, ops[p]["lat"] + wake if deps[i][p] else 0) for p in deps[i]] for i in range(n)],
                      [[(s, ops[i]["lat"] + wake if deps[s][i] else 0) for s in succ[i]] for i in range(n)]))

    def queue(order, bs, pre, first):
        out, free = [0.0] * n, {}
        for i in order:
            t = max(first[i], free.get(eng[i], 0.0))
            for p, d in pre[i]:
                if out[p] + d > t:
                    t = out[p] + d
            out[i] = t + bs[i]
            if eng[i] != "N":
                free[eng[i]] = out[i]
        return out

    def fill(order, bs, pre, first, out):
        slots = {}
        for i in order:
            t, b = first[i], bs[i]
            for p, d in pre[i]:
                if out[p] + d > t:
                    t = out[p] + d
            sl = slots.setdefault(eng[i], [])
            k = len(sl)
            while k > 0 and sl[k - 1][1] > t:
                k -= 1
            while k < len(sl) and sl[k][0] < t + b:
                if sl[k][1] > t:
                    t = sl[k][1]
                k += 1
            sl.insert(k, (t, t + b))
            out[i] = t + b

    def total(order):
        s = 0.0
        for (bs, pre), w in weights:
            out = queue(order, bs, pre, zero)
            s += w * math.log(max(out[i] + tail[i] for i in range(n)))
        return s

    cur, known = total(seq), {}
    for _ in range(CFG["local"]):
        v = rnd.randint(len(views))
        bs, pre, post = views[v]
        if v not in known:
            known[v] = (queue(seq, bs, pre, zero), queue(seq[::-1], bs, post, tail))
        ahead, behind = known[v]
        w = rnd.randint(CFG["wmin"], CFG["wmax"])
        a = min(max(0, rnd.randint(-w // 2, n - w // 2)), n - 1)
        part = seq[a:a + w]
        head, foot = {}, {}
        for i in seq[max(0, a - 400):a]:
            head[eng[i]] = ahead[i]
        for i in seq[a + w + 400:a + w - 1:-1]:
            foot[eng[i]] = behind[i]
        head["N"] = foot["N"] = 0.0
        first = {i: head.get(eng[i], 0.0) for i in part}
        last_ = {i: max(tail[i], foot.get(eng[i], 0.0)) for i in part}
        sig = rnd.uniform(0, CFG["sigl"])
        key = {}
        for i in part:
            t = ahead[i] - bs[i] + rnd.uniform(-sig, sig)
            for p, d in pre[i]:
                if key.get(p, t) > t:
                    t = key[p]
            key[i] = t
        rank = {i: k for k, i in enumerate(part)}
        order = sorted(part, key=lambda i: (key[i], rank[i]))
        f_, b_ = list(ahead), list(behind)
        fill(order, bs, pre, first, f_)
        for x in range(CFG["turns"]):
            fill(sorted(part, key=lambda i: (-f_[i], -rank[i])), bs, post, last_, b_)
            fill(sorted(part, key=lambda i: (-b_[i], rank[i])), bs, pre, first, f_)
        other = seq[:a] + sorted(part, key=lambda i: (f_[i] - bs[i], rank[i])) + seq[a + w:]
        s = total(other)
        if s <= cur:
            cur, seq, known = s, other, {}
    return [(i, k) for k, i in enumerate(seq)], end


def plan_waits(ops, deps, order):
    pos, key = {}, {}
    for k, (i, s) in enumerate(order):
        pos[i] = k
        key[i] = ops[i]["sem"] if ops[i]["sem"] else ops[i]["eng"]
    known, clock, waits, signal = {}, {}, {}, set()
    for i, s in order:
        e = ops[i]["eng"]
        kn = known.setdefault(e, {}) if e != "N" else {}
        w = []
        if e != "N":
            for p in sorted((p for p in deps[i] if deps[i][p]), key=lambda p: -pos[p]):
                if kn.get(key[p], -1) >= pos[p]:
                    continue
                w.append(p)
                signal.add(p)
                for k2, v in clock[p].items():
                    if kn.get(k2, -1) < v:
                        kn[k2] = v
        waits[i] = w
        c = dict(kn)
        c[key[i]] = pos[i]
        clock[i] = c
    return waits, signal


PLAN = {}


def plan():
    if not PLAN:
        ops = build()
        deps = depend(ops)
        order, end = schedule(ops, deps)
        waits, signal = plan_waits(ops, deps, order)
        PLAN.update({"ops": ops, "order": order, "waits": waits, "signal": signal, "end": end})
    return PLAN


def rank_program(g, core, T, topo):
    rank = T.rank_of(core)
    if rank is None:
        return
    p = plan()
    ops, waits, signal = p["ops"], p["waits"], p["signal"]
    cores = list(T.cores)
    nr = len(cores)
    queue = {"V": g.vector, "S": g.scalar, "P": g.tensor, "G": g, "Y": g.sync}

    def res(x):
        if not is_acc(x):
            return x
        if x[0] == "#":
            return res(x[1]).indirect(res(x[2]))
        return T[x[1]][x[3]]

    def call(q, name, a, kw):
        a = [res(x) for x in a]
        kw = {k: res(v) for k, v in kw.items()}
        if name == "tt":
            return q.tensor_tensor(*a)
        if name == "ts":
            return q.tensor_scalar(*a)
        if name == "cp":
            return q.tensor_copy(*a)
        if name == "red":
            return q.tensor_reduce(*a)
        if name == "scan":
            return q.tensor_tensor_scan(*a)
        if name == "ms":
            return q.memset(*a)
        if name == "act":
            return q.activation(*a, **kw)
        if name == "mm":
            return q.matmul(*a)
        if name == "iota":
            return q.iota(*a, **kw)
        if name == "asel":
            return q.affine_select(*a)
        return q.dma_start(*a)

    cnt = {"V": 0, "S": 0, "P": 0, "G": 0}
    val = {}
    sent = 0
    outs = []
    for i, s in p["order"]:
        o = ops[i]
        e = o["eng"]
        if e == "N":
            t = int(o["sem"][1])
            src = cores[(rank - 1 - t % 3) % nr]
            val[i] = (o["sem"], len(topo.engines(src, core)))
            continue
        q = queue[e]
        for w in waits[i]:
            q.wait_ge(T.sem[val[w][0]], val[w][1])
        name = o["calls"][0][0]
        if name == "send":
            _, src, t, h = o["calls"][0][1]
            dst = cores[(rank + 1 + t % 3) % nr]
            rid, pid, _ = topo.addr(dst)
            g.remote_dma(res(landing(t, h)), res(src), T.sem["a%d%d" % (t, h)], T.sem["sent"], pid, rid, topo.mask(core, dst))
            sent += len(topo.engines(core, dst))
            continue
        ins = None
        for c in o["calls"]:
            ins = call(q, c[0], c[1], c[2])
        if name == "dma":
            ins.then_inc(T.sem[o["sem"]], 16)
            val[i] = (o["sem"], 16)
            if i not in signal:
                outs.append(o["sem"])
        elif i in signal:
            cnt[e] += 1
            ins.then_inc(T.sem["c" + e], 1)
            val[i] = ("c" + e, cnt[e])
    g.wait_ge(T.sem["sent"], sent)
    for sname in outs:
        g.sync.wait_ge(T.sem[sname], 16)
